import numpy as np
import ml_dtypes


def mxq(x, axis, fmt="e4m3"):
    dtype, down = {"e4m3": (ml_dtypes.float8_e4m3fn, 7), "e5m2": (ml_dtypes.float8_e5m2, 14)}[fmt]
    v = np.moveaxis(np.asarray(x, np.float32).astype(ml_dtypes.bfloat16).astype(np.float64), axis, -1)
    blocks = v.reshape(v.shape[:-1] + (-1, 32))
    amax = np.abs(blocks).max(-1, keepdims=True)
    byte = np.maximum(np.where(amax > 0, np.frexp(amax)[1] - 1 + 127, 0) - down, 1)
    scale = np.exp2(byte - 127.0)
    codes = (blocks / scale).astype(np.float32).astype(dtype).astype(np.float64)
    return np.moveaxis((codes * scale).reshape(v.shape), -1, axis)


WIDE = False


def mx_kscale(k):
    if not WIDE:
        return np.ones(k)
    levels = np.array([30, -30])
    if k % 512:
        return np.exp2(np.random.permutation(np.resize(levels, k // 32))).repeat(32)
    a = np.empty((k // 512, 16))
    for p in range(k // 512):
        a[p, :8] = np.random.permutation(np.resize(levels, 8))
        for g in range(8):
            far = levels[np.abs(levels - a[p, g]) >= 10]
            a[p, g + 8] = far[np.random.randint(len(far))]
    return np.exp2(a.ravel()).repeat(32)


def f64(x):
    return np.asarray(x).astype(np.float64)


def striped(idx):
    return np.tile(idx.reshape(-1, 16).T, (8, 1)).astype(np.uint16)


def unstriped(offs):
    return offs[:16].T.reshape(-1).astype(np.int64)


E2M1 = np.array([0.0, 0.5, 1.0, 1.5, 2.0, 3.0, 4.0, 6.0, -0.0, -0.5, -1.0, -1.5, -2.0, -3.0, -4.0, -6.0])


def pack_weight(w, fmt):
    k, n = w.shape
    w = f64(np.asarray(w, np.float32).astype(ml_dtypes.bfloat16)).reshape(k // 32, 32, n)
    amax = np.abs(w).max(1)
    if fmt == "e4m3":
        byte = np.frexp(amax)[1] - 1 + 127 - 7
    else:
        mant, ex = np.frexp(amax / 6.0)
        byte = np.where(mant > 0.5, ex, ex - 1) + 127
    byte = np.clip(np.where(amax > 0, byte, 1), 1, 254)
    scaled = (w * np.exp2(127.0 - byte)[:, None, :]).reshape(k, n).astype(np.float32)
    by_word = np.ascontiguousarray(scaled.reshape(k // 512, 128, 4, n).transpose(0, 1, 3, 2))
    if fmt == "e4m3":
        words = by_word.astype(ml_dtypes.float8_e4m3fn).view(np.uint8)
    else:
        c = by_word.astype(ml_dtypes.float4_e2m1fn).view(np.uint8) & 0xF
        words = (c[..., 0::2] | (c[..., 1::2] << 4)).reshape(k // 512, 128, 2 * n)
    return np.ascontiguousarray(words), np.ascontiguousarray(byte.astype(np.uint8).reshape(k // 512, 16, n))


def unpack_weight(words, scales, fmt):
    g, _, n = scales.shape
    words = np.ascontiguousarray(words).reshape(g, 128, n, -1)
    if fmt == "e4m3":
        vals = words.view(ml_dtypes.float8_e4m3fn).astype(np.float64)
    else:
        nib = np.empty((g, 128, n, 4), np.uint8)
        nib[..., 0::2] = words & 0xF
        nib[..., 1::2] = words >> 4
        vals = E2M1[nib]
    vals = vals * np.repeat(np.exp2(scales.astype(np.float64) - 127.0), 8, axis=1)[..., None]
    return vals.transpose(0, 1, 3, 2).reshape(g * 512, n)


def d_relu(v):
    return (v > 0).astype(np.float64)


K, T, E, C, H, N = 128, 1024, 4, 512, 512, 512


def by_expert(wq, xq):
    return np.concatenate([wq[e].T @ xq[:, e * C:(e + 1) * C] for e in range(E)], axis=1)


def setup_inputs():
    n = np.random.standard_normal
    s = mx_kscale(N)[:, None]
    u = mx_kscale(H)
    first = np.random.permutation(np.repeat(np.arange(E), T // E))
    second = (first + 1 + np.random.permutation(np.repeat(np.arange(E - 1), -(-T // (E - 1)))[:T])) % E
    while np.bincount(second, minlength=E).max() != T // E:
        load = np.bincount(second, minlength=E); hi, lo = int(load.argmax()), int(load.argmin())
        t = np.flatnonzero((second == hi) & (first != lo))[0]; second[t] = lo
    slot_token = np.empty(E * C, np.int64); pos = np.empty((2, T), np.int64); fill = np.zeros(E, np.int64)
    place = np.stack([np.random.permutation(C) for _ in range(E)])
    for r, deal in enumerate((first, second)):
        for t in np.random.permutation(T):
            e = deal[t]; j = e * C + place[e, fill[e]]; fill[e] += 1; slot_token[j] = t; pos[r, t] = j
    g = np.random.uniform(0.2, 0.8, T)
    w_slot = np.empty(E * C); w_slot[pos[0]] = g; w_slot[pos[1]] = 1.0 - g
    w2 = [pack_weight(m, "e2m1") for m in n((E, N, H)) / np.sqrt(N) / s[None] * u[None, None, :]]
    w1 = [pack_weight(m, "e2m1") for m in n((E, H, K)) / np.sqrt(H) / u[None, :, None]]
    return {
        "dyT": (n((N, T)) * s).astype(np.float32),
        "a": n((H, E * C)).astype(np.float32),
        "w2_words": np.stack([m[0] for m in w2]),
        "w2_scales": np.stack([m[1] for m in w2]),
        "w1_words": np.stack([m[0] for m in w1]),
        "w1_scales": np.stack([m[1] for m in w1]),
        "gate": np.tile(w_slot, (N, 1)).astype(np.float32),
        "offs": striped(slot_token),
        "pos1": striped(pos[0]),
        "pos2": striped(pos[1]),
    }


def reference(dyT, a, w2_words, w2_scales, w1_words, w1_scales, gate, offs, pos1, pos2):
    idx = unstriped(offs)
    w2 = np.stack([unpack_weight(w2_words[e], w2_scales[e], "e2m1") for e in range(E)])
    w1 = np.stack([unpack_weight(w1_words[e], w1_scales[e], "e2m1") for e in range(E)])
    gq = mxq(f64(gate) * f64(dyT)[:, idx], 0, "e5m2")
    dh = by_expert(w2, gq)
    da = dh * d_relu(f64(a))
    dx = by_expert(w1, mxq(da, 0, "e5m2"))
    return dx[:, unstriped(pos1)] + dx[:, unstriped(pos2)]

@@ -1,0 +1,249 @@
+from contextlib import ExitStack
+
+import concourse.mybir as mybir
+
+N, H, K = 512, 512, 128
+T, E, C = 1024, 4, 512
+S = E * C
+P = 128
+PACK = 4
+
+FLOPS = 2 * S * (N * H + H * K)
+BYTES = 4 * N * T + 4 * H * S + E * (N * H + H * K) // 2 + E * (N * H + H * K) // 32 + 4 * S + 2 * P * (S + 2 * T) // 16 + 4 * K * T
+
+F32 = mybir.dt.float32
+BF16 = mybir.dt.bfloat16
+I32 = mybir.dt.int32
+U32 = mybir.dt.uint32
+U16 = mybir.dt.uint16
+U8 = mybir.dt.uint8
+E5M2X4 = mybir.dt.float8_e5m2_x4
+E2M1X4 = mybir.dt.float4_e2m1fn_x4
+MULT = mybir.AluOpType.mult
+IS_GT = mybir.AluOpType.is_gt
+
+
+def tile_moe_bdx_mlp_relu_kernel(
+    tc, dyT, a, w2_words, w2_scales, w1_words, w1_scales, gate, offs, pos1, pos2, out
+):
+    nc = tc.nc
+    with ExitStack() as ctx:
+        lists = ctx.enter_context(tc.tile_pool(name="lists", bufs=1))
+        held = ctx.enter_context(tc.tile_pool(name="held", bufs=1))
+        work = ctx.enter_context(tc.tile_pool(name="work", bufs=4))
+        dh_psum = ctx.enter_context(tc.psum_pool(name="dh_psum", bufs=6))
+        dx_psum = ctx.enter_context(tc.psum_pool(name="dx_psum", bufs=2))
+
+        offs_sb = lists.tile([P, S // 16], U16, name="offs_sb")
+        pos1_sb = lists.tile([P, T // 16], U16, name="pos1_sb")
+        pos2_sb = lists.tile([P, T // 16], U16, name="pos2_sb")
+
+        w2_raw = [held.tile([P, 2 * 2 * H], U8, name=f"w2_raw{h}", align_bytes=64) for h in range(2)]
+        w2_sb = [held.tile([P, 2 * 2 * H], U8, name=f"w2_sb{h}", align_bytes=64) for h in range(2)]
+        s2_raw = held.tile([P, H], U8, name="s2_raw", align_bytes=64)
+        s2_sb = [held.tile([P, H], U8, name=f"s2_sb{e}", align_bytes=64) for e in range(E)]
+        w1_sb = held.tile([P, E * 2 * K], U8, name="w1_sb", align_bytes=64)
+        s1_sb = held.tile([P, E * K], U8, name="s1_sb", align_bytes=64)
+        dy_sb = [held.tile([P, T], F32, name=f"dy_sb{t}") for t in range(PACK)]
+        gate_sb = [held.tile([P, C], F32, name=f"gate_sb{e}") for e in range(E)]
+        a_sb = [held.tile([P, PACK, C], F32, name=f"a_sb{e}") for e in range(E)]
+        dx_sb = held.tile([P, S], F32, name="dx_sb")
+
+        nc.gpsimd.memset(s2_raw[:].bitcast(I32), 0)
+        nc.gpsimd.memset(s1_sb[:].bitcast(I32), 0)
+        for e in range(1, E):
+            nc.gpsimd.memset(s2_sb[e][:].bitcast(I32), 0)
+
+        w2_i32 = w2_words.bitcast(I32)
+        w1_i32 = w1_words.bitcast(I32)
+        s2_i32 = w2_scales.bitcast(I32)
+        s1_i32 = w1_scales.bitcast(I32)
+        dy_planes = dyT.rearrange("(p t) c -> p t c", t=PACK)
+        a_planes = a.rearrange("(p t) c -> p t c", t=PACK)
+
+        def load_w2(h):
+            nc.sync.dma_start(
+                out=w2_raw[h][:].bitcast(I32).rearrange("p (e w) -> p e w", e=2),
+                in_=w2_i32[2 * h : 2 * h + 2, 0].rearrange("e p w -> p e w"),
+            )
+
+        def load_dy(t):
+            nc.sync.dma_start(out=dy_sb[t][:], in_=dy_planes[:, t, :])
+
+        def load_gate(e):
+            nc.sync.dma_start(out=gate_sb[e][:], in_=gate[0:P, e * C : (e + 1) * C])
+
+        def load_a(e):
+            nc.sync.dma_start(out=a_sb[e][:], in_=a_planes[:, :, e * C : (e + 1) * C])
+
+        load_w2(0)
+        nc.sync.dma_start(offs_sb[:], offs)
+        load_dy(0)
+        load_gate(0)
+        load_dy(1)
+        load_dy(2)
+        load_dy(3)
+        load_gate(1)
+        for q in range(4):
+            nc.sync.dma_start(
+                out=s2_raw[32 * q : 32 * q + 16, :].bitcast(I32), in_=s2_i32[:, 0, 4 * q : 4 * q + 4, :]
+            )
+        load_a(0)
+        load_gate(2)
+        load_w2(1)
+        nc.sync.dma_start(
+            out=w1_sb[:].bitcast(I32).rearrange("p (e w) -> p e w", e=E), in_=w1_i32[:, 0].rearrange("e p w -> p e w")
+        )
+        for q in range(4):
+            nc.sync.dma_start(
+                out=s1_sb[32 * q : 32 * q + 4, :].bitcast(I32).rearrange("p (e w) -> p e w", e=E),
+                in_=s1_i32[:, 0, 4 * q : 4 * q + 4, :].rearrange("e f w -> f e w"),
+            )
+        load_gate(3)
+        load_a(1)
+        load_a(2)
+        load_a(3)
+        nc.sync.dma_start(pos1_sb[:], pos1)
+        nc.sync.dma_start(pos2_sb[:], pos2)
+
+        def permute_w2(h):
+            nc.vector.tensor_copy(
+                out=w2_sb[h][:].bitcast(U16).rearrange("p (e t m) -> p e t m", e=2, t=PACK),
+                in_=w2_raw[h][:].bitcast(U16).rearrange("p (e m t) -> p e t m", e=2, t=PACK),
+            )
+
+        def permute_s2():
+            nc.vector.tensor_copy(
+                out=s2_sb[0][:].rearrange("p (t m) -> p t m", t=PACK),
+                in_=s2_raw[:].rearrange("p (m t) -> p t m", t=PACK),
+            )
+            for e in range(1, E):
+                nc.sync.dma_start(out=s2_sb[e][0:112, :].bitcast(I32), in_=s2_sb[0][4 * e : 4 * e + 112, :].bitcast(I32))
+
+        def gather(e):
+            g4 = work.tile([P, PACK, C], F32, name="g4")
+            for t in range(PACK):
+                nc.vector.tensor_tensor(
+                    g4[:, t, :],
+                    dy_sb[t][:].indirect(offs_sb[:, e * (C // 16) : (e + 1) * (C // 16)]),
+                    gate_sb[e][:],
+                    MULT,
+                )
+            return g4
+
+        def interleave(src, name, lines):
+            flat = work.tile([P, C * PACK], BF16, name=name, align_bytes=64)
+            nc.scalar.copy(
+                flat[:].rearrange("p (c i t) -> p c t i", i=lines, t=PACK),
+                src[:].rearrange("p t (c i) -> p c t i", i=lines),
+            )
+            return flat
+
+        def quantise(flat, name):
+            codes = work.tile([P, C], U32, name=name + "_codes", align_bytes=64)
+            scales = work.tile([P, C], U8, name=name + "_scales", align_bytes=64)
+            nc.vector.quantize_mx(out=codes[:].bitcast(E5M2X4), scales=scales[:], in_=flat[:])
+            return codes, scales
+
+        def product2(e, g):
+            banks = []
+            for t in range(PACK):
+                dh = dh_psum.tile([P, C], F32, name="dh")
+                at = (e % 2) * H + t * P
+                nc.tensor.matmul_mx(
+                    out=dh[:],
+                    lhsT=w2_sb[e // 2][:, 2 * at : 2 * (at + P)].bitcast(E2M1X4),
+                    lhsT_scale=s2_sb[e][:, t * P : (t + 1) * P],
+                    rhs=g[0][:].bitcast(E5M2X4),
+                    rhs_scale=g[1][:],
+                    start=True,
+                    stop=True,
+                )
+                banks.append(dh)
+            return banks
+
+        def mask(e, banks):
+            da = work.tile([P, PACK, C], BF16, name="da")
+            for t in range(PACK):
+                nc.vector.scalar_tensor_tensor(
+                    out=da[:, t, :], in0=a_sb[e][:, t, :], scalar=0.0, in1=banks[t][:], op0=IS_GT, op1=MULT
+                )
+            return da
+
+        def product1(e, d):
+            dx = dx_psum.tile([P, C], F32, name="dx")
+            nc.tensor.matmul_mx(
+                out=dx[:],
+                lhsT=w1_sb[:, 2 * e * K : 2 * (e + 1) * K].bitcast(E2M1X4),
+                lhsT_scale=s1_sb[:, e * K : (e + 1) * K],
+                rhs=d[0][:].bitcast(E5M2X4),
+                rhs_scale=d[1][:],
+                start=True,
+                stop=True,
+            )
+            nc.scalar.copy(dx_sb[:, e * C : (e + 1) * C], dx[:])
+
+        permute_w2(0)
+        g4_0 = gather(0)
+        gi_0 = interleave(g4_0, "gi", 4)
+        g4_1 = gather(1)
+        gi_1 = interleave(g4_1, "gi", 4)
+        permute_s2()
+        dh_0 = product2(0, quantise(gi_0, "g"))
+        g4_2 = gather(2)
+        gi_2 = interleave(g4_2, "gi", 4)
+        permute_w2(1)
+        dm_0 = mask(0, dh_0)
+        di_0 = interleave(dm_0, "di", 4)
+        dh_1 = product2(1, quantise(gi_1, "g"))
+        g4_3 = gather(3)
+        gi_3 = interleave(g4_3, "gi", 4)
+        dm_1 = mask(1, dh_1)
+        di_1 = interleave(dm_1, "di", 4)
+        dh_2 = product2(2, quantise(gi_2, "g"))
+        product1(0, quantise(di_0, "d"))
+        dh_3 = product2(3, quantise(gi_3, "g"))
+        dm_2 = mask(2, dh_2)
+        di_2 = interleave(dm_2, "di", 4)
+        da_3 = work.tile([P, PACK, C], BF16, name="da")
+        di_3 = work.tile([P, C * PACK], BF16, name="di", align_bytes=64)
+        d_3 = (
+            work.tile([P, C], U32, name="d_codes", align_bytes=64),
+            work.tile([P, C], U8, name="d_scales", align_bytes=64),
+        )
+        parts = 2
+        wide = C // parts
+        for j in range(parts):
+            part = slice(j * wide, (j + 1) * wide)
+            for t in range(PACK):
+                nc.vector.scalar_tensor_tensor(
+                    out=da_3[:, t, part], in0=a_sb[3][:, t, part], scalar=0.0, in1=dh_3[t][:, part], op0=IS_GT, op1=MULT
+                )
+            nc.scalar.copy(
+                di_3[:, PACK * j * wide : PACK * (j + 1) * wide].rearrange("p (c i t) -> p c t i", i=4, t=PACK),
+                da_3[:, :, part].rearrange("p t (c i) -> p c t i", i=4),
+            )
+        product1(1, quantise(di_1, "d"))
+        product1(2, quantise(di_2, "d"))
+        for j in range(parts):
+            part = slice(j * wide, (j + 1) * wide)
+            nc.vector.quantize_mx(
+                out=d_3[0][:, part].bitcast(E5M2X4),
+                scales=d_3[1][:, part],
+                in_=di_3[:, PACK * j * wide : PACK * (j + 1) * wide],
+            )
+        product1(3, d_3)
+
+        half = T // 2
+        first = held.tile([P, T], F32, name="first")
+        nc.vector.tensor_copy(first[:], dx_sb[:].indirect(pos1_sb[:]))
+        second = [work.tile([P, half], F32, name="second") for h in range(2)]
+        for h in range(2):
+            nc.vector.tensor_copy(
+                second[h][:], dx_sb[:].indirect(pos2_sb[:, h * half // 16 : (h + 1) * half // 16])
+            )
+        for h in range(2):
+            total = work.tile([P, half], F32, name="total")
+            adder = nc.gpsimd if h == 0 else nc.vector
+            adder.tensor_tensor(total[:], first[:, h * half : (h + 1) * half], second[h][:], mybir.AluOpType.add)
+            nc.sync.dma_start(out=out[:, h * half : (h + 1) * half], in_=total[:])

@@ -1,6 +1,7 @@
 from contextlib import ExitStack
 
 import concourse.mybir as mybir
+from concourse.masks import make_identity
 
 N, H, K = 512, 512, 128
 T, E, C = 1024, 4, 512
@@ -20,7 +21,10 @@ U8 = mybir.dt.uint8
 E5M2X4 = mybir.dt.float8_e5m2_x4
 E2M1X4 = mybir.dt.float4_e2m1fn_x4
 MULT = mybir.AluOpType.mult
+ADD = mybir.AluOpType.add
+MAX = mybir.AluOpType.max
 IS_GT = mybir.AluOpType.is_gt
+SIGN = mybir.ActivationFunctionType.Sign
 
 
 def tile_moe_bdx_mlp_relu_kernel(
@@ -31,28 +35,38 @@ def tile_moe_bdx_mlp_relu_kernel(
         lists = ctx.enter_context(tc.tile_pool(name="lists", bufs=1))
         held = ctx.enter_context(tc.tile_pool(name="held", bufs=1))
         work = ctx.enter_context(tc.tile_pool(name="work", bufs=4))
-        dh_psum = ctx.enter_context(tc.psum_pool(name="dh_psum", bufs=6))
-        dx_psum = ctx.enter_context(tc.psum_pool(name="dx_psum", bufs=2))
+        dh_psum = ctx.enter_context(tc.psum_pool(name="dh_psum", bufs=4))
+        turn_psum = ctx.enter_context(tc.psum_pool(name="turn_psum", bufs=3))
+        dx_psum = ctx.enter_context(tc.psum_pool(name="dx_psum", bufs=1))
 
         offs_sb = lists.tile([P, S // 16], U16, name="offs_sb")
         pos1_sb = lists.tile([P, T // 16], U16, name="pos1_sb")
         pos2_sb = lists.tile([P, T // 16], U16, name="pos2_sb")
 
-        w2_raw = [held.tile([P, 2 * 2 * H], U8, name=f"w2_raw{h}", align_bytes=64) for h in range(2)]
+        half = C // 2
         w2_sb = [held.tile([P, 2 * 2 * H], U8, name=f"w2_sb{h}", align_bytes=64) for h in range(2)]
-        s2_raw = held.tile([P, H], U8, name="s2_raw", align_bytes=64)
-        s2_sb = [held.tile([P, H], U8, name=f"s2_sb{e}", align_bytes=64) for e in range(E)]
+        s2_sb = held.tile([P, E * H], U8, name="s2_sb", align_bytes=64)
         w1_sb = held.tile([P, E * 2 * K], U8, name="w1_sb", align_bytes=64)
         s1_sb = held.tile([P, E * K], U8, name="s1_sb", align_bytes=64)
         dy_sb = [held.tile([P, T], F32, name=f"dy_sb{t}") for t in range(PACK)]
         gate_sb = [held.tile([P, C], F32, name=f"gate_sb{e}") for e in range(E)]
         a_sb = [held.tile([P, PACK, C], F32, name=f"a_sb{e}") for e in range(E)]
+        g_01 = held.tile([P, (PACK + 2) * C], F32, name="g_01")
+        g_0 = g_01[:, 0 : PACK * C]
+        g_1 = g_01[:, 2 * C :]
+        g_2 = held.tile([P, PACK * C], F32, name="g_2", align_bytes=64)
+        g_3a = held.tile([P, PACK * half], F32, name="g_3a", align_bytes=64)
+        g_3b = held.tile([P, PACK * half], F32, name="g_3b", align_bytes=64)
+        sign_0 = g_2[:, 0 : 2 * C].bitcast(BF16)
+        gi_1 = g_2[:, 2 * C : 4 * C].bitcast(BF16)
+        sign_1 = g_3a[:].bitcast(BF16)
+        gi_2 = g_3b[:].bitcast(BF16)
         dx_sb = held.tile([P, S], F32, name="dx_sb")
+        ident = held.tile([P, P], F32, name="ident")
 
-        nc.gpsimd.memset(s2_raw[:].bitcast(I32), 0)
+        nc.gpsimd.memset(s2_sb[:].bitcast(I32), 0)
         nc.gpsimd.memset(s1_sb[:].bitcast(I32), 0)
-        for e in range(1, E):
-            nc.gpsimd.memset(s2_sb[e][:].bitcast(I32), 0)
+        make_identity(nc, ident[:])
 
         w2_i32 = w2_words.bitcast(I32)
         w1_i32 = w1_words.bitcast(I32)
@@ -63,9 +77,16 @@ def tile_moe_bdx_mlp_relu_kernel(
 
         def load_w2(h):
             nc.sync.dma_start(
-                out=w2_raw[h][:].bitcast(I32).rearrange("p (e w) -> p e w", e=2),
+                out=w2_sb[h][:].bitcast(I32).rearrange("p (e w) -> p e w", e=2),
                 in_=w2_i32[2 * h : 2 * h + 2, 0].rearrange("e p w -> p e w"),
             )
+
+        def load_scales(dst, src):
+            for q in range(4):
+                nc.sync.dma_start(
+                    out=dst[32 * q : 32 * q + 4, :].bitcast(I32).rearrange("p (e w) -> p e w", e=E),
+                    in_=src[:, 0, 4 * q : 4 * q + 4, :].rearrange("e f w -> f e w"),
+                )
 
         def load_dy(t):
             nc.sync.dma_start(out=dy_sb[t][:], in_=dy_planes[:, t, :])
@@ -76,99 +97,99 @@ def tile_moe_bdx_mlp_relu_kernel(
         def load_a(e):
             nc.sync.dma_start(out=a_sb[e][:], in_=a_planes[:, :, e * C : (e + 1) * C])
 
-        load_w2(0)
-        nc.sync.dma_start(offs_sb[:], offs)
         load_dy(0)
+        nc.sync.dma_start(offs_sb[:], offs)
         load_gate(0)
         load_dy(1)
         load_dy(2)
         load_dy(3)
         load_gate(1)
-        for q in range(4):
-            nc.sync.dma_start(
-                out=s2_raw[32 * q : 32 * q + 16, :].bitcast(I32), in_=s2_i32[:, 0, 4 * q : 4 * q + 4, :]
-            )
         load_a(0)
+        load_w2(0)
+        load_scales(s2_sb, s2_i32)
         load_gate(2)
+        load_a(1)
         load_w2(1)
         nc.sync.dma_start(
             out=w1_sb[:].bitcast(I32).rearrange("p (e w) -> p e w", e=E), in_=w1_i32[:, 0].rearrange("e p w -> p e w")
         )
-        for q in range(4):
-            nc.sync.dma_start(
-                out=s1_sb[32 * q : 32 * q + 4, :].bitcast(I32).rearrange("p (e w) -> p e w", e=E),
-                in_=s1_i32[:, 0, 4 * q : 4 * q + 4, :].rearrange("e f w -> f e w"),
-            )
+        load_scales(s1_sb, s1_i32)
         load_gate(3)
-        load_a(1)
         load_a(2)
         load_a(3)
         nc.sync.dma_start(pos1_sb[:], pos1)
         nc.sync.dma_start(pos2_sb[:], pos2)
 
-        def permute_w2(h):
-            nc.vector.tensor_copy(
-                out=w2_sb[h][:].bitcast(U16).rearrange("p (e t m) -> p e t m", e=2, t=PACK),
-                in_=w2_raw[h][:].bitcast(U16).rearrange("p (e m t) -> p e t m", e=2, t=PACK),
-            )
-
-        def permute_s2():
-            nc.vector.tensor_copy(
-                out=s2_sb[0][:].rearrange("p (t m) -> p t m", t=PACK),
-                in_=s2_raw[:].rearrange("p (m t) -> p t m", t=PACK),
-            )
-            for e in range(1, E):
-                nc.sync.dma_start(out=s2_sb[e][0:112, :].bitcast(I32), in_=s2_sb[0][4 * e : 4 * e + 112, :].bitcast(I32))
-
-        def gather(e):
-            g4 = work.tile([P, PACK, C], F32, name="g4")
-            for t in range(PACK):
+        def gather(dst, e, first, wide, planes=range(PACK)):
+            at = (e * C + first) // 16
+            for t in planes:
                 nc.vector.tensor_tensor(
-                    g4[:, t, :],
-                    dy_sb[t][:].indirect(offs_sb[:, e * (C // 16) : (e + 1) * (C // 16)]),
-                    gate_sb[e][:],
+                    dst[:, t * wide : (t + 1) * wide],
+                    dy_sb[t][:].indirect(offs_sb[:, at : at + wide // 16]),
+                    gate_sb[e][:, first : first + wide],
                     MULT,
                 )
-            return g4
 
-        def interleave(src, name, lines):
-            flat = work.tile([P, C * PACK], BF16, name=name, align_bytes=64)
-            nc.scalar.copy(
-                flat[:].rearrange("p (c i t) -> p c t i", i=lines, t=PACK),
-                src[:].rearrange("p t (c i) -> p c t i", i=lines),
-            )
-            return flat
+        def side_by_side(flat):
+            return flat.rearrange("p (c i t) -> p c t i", i=4, t=PACK)
 
-        def quantise(flat, name):
+        def by_planes(planes):
+            return planes.rearrange("p t (c i) -> p c t i", i=4)
+
+        def interleave(flat, src):
+            nc.scalar.copy(side_by_side(flat), by_planes(src.rearrange("p (t c) -> p t c", t=PACK)))
+
+        def flat_tile(wide, name):
+            return work.tile([P, wide * PACK], BF16, name=name, align_bytes=64)[:]
+
+        def operand(name):
             codes = work.tile([P, C], U32, name=name + "_codes", align_bytes=64)
             scales = work.tile([P, C], U8, name=name + "_scales", align_bytes=64)
-            nc.vector.quantize_mx(out=codes[:].bitcast(E5M2X4), scales=scales[:], in_=flat[:])
             return codes, scales
 
-        def product2(e, g):
-            banks = []
-            for t in range(PACK):
-                dh = dh_psum.tile([P, C], F32, name="dh")
-                at = (e % 2) * H + t * P
+        def quantise(dst, flat, first, wide):
+            nc.vector.quantize_mx(
+                out=dst[0][:, first : first + wide].bitcast(E5M2X4), scales=dst[1][:, first : first + wide], in_=flat
+            )
+
+        def sign_of(sign, e):
+            nc.scalar.activation(side_by_side(sign), by_planes(a_sb[e][:]), SIGN)
+
+        def clip(keep, sign):
+            nc.vector.tensor_scalar(keep, sign, 0.0, None, op0=MAX)
+
+        def keep_by_vector(keep, e):
+            nc.vector.tensor_scalar(side_by_side(keep), by_planes(a_sb[e][:]), 0.0, None, op0=IS_GT)
+
+        def product2(e, g, h):
+            turned = turn_psum.tile([P, 2 * half], F32, name="turned")
+            for b in range(2):
+                at = h * half + b * P
+                dh = dh_psum.tile([P, H], F32, name="dh")
                 nc.tensor.matmul_mx(
                     out=dh[:],
-                    lhsT=w2_sb[e // 2][:, 2 * at : 2 * (at + P)].bitcast(E2M1X4),
-                    lhsT_scale=s2_sb[e][:, t * P : (t + 1) * P],
-                    rhs=g[0][:].bitcast(E5M2X4),
-                    rhs_scale=g[1][:],
+                    lhsT=g[0][:, at : at + P].bitcast(E5M2X4),
+                    lhsT_scale=g[1][:, at : at + P],
+                    rhs=w2_sb[e // 2][:, (e % 2) * 2 * H : (e % 2 + 1) * 2 * H].bitcast(E2M1X4),
+                    rhs_scale=s2_sb[:, e * H : (e + 1) * H],
                     start=True,
                     stop=True,
                 )
-                banks.append(dh)
-            return banks
-
-        def mask(e, banks):
-            da = work.tile([P, PACK, C], BF16, name="da")
-            for t in range(PACK):
-                nc.vector.scalar_tensor_tensor(
-                    out=da[:, t, :], in0=a_sb[e][:, t, :], scalar=0.0, in1=banks[t][:], op0=IS_GT, op1=MULT
+                rounded = work.tile([P, H], BF16, name="rounded")
+                nc.scalar.copy(
+                    rounded[:].rearrange("s (u p d) -> s u p d", u=2, d=2),
+                    dh[:].rearrange("s (p u d) -> s u p d", u=2, d=2),
                 )
-            return da
+                pairs = rounded[:].bitcast(F32)
+                for u in range(2):
+                    nc.tensor.transpose(
+                        turned[:, 2 * b * P + u : 2 * (b + 1) * P : 2], pairs[:, u * P : (u + 1) * P], ident[:]
+                    )
+            return turned
+
+        def masked(da, turned, keep, h):
+            cols = slice(h * half * PACK, (h + 1) * half * PACK)
+            nc.vector.tensor_tensor(da[:, cols], turned[:].bitcast(BF16), keep[:, cols], MULT)
 
         def product1(e, d):
             dx = dx_psum.tile([P, C], F32, name="dx")
@@ -183,67 +204,70 @@ def tile_moe_bdx_mlp_relu_kernel(
             )
             nc.scalar.copy(dx_sb[:, e * C : (e + 1) * C], dx[:])
 
-        permute_w2(0)
-        g4_0 = gather(0)
-        gi_0 = interleave(g4_0, "gi", 4)
-        g4_1 = gather(1)
-        gi_1 = interleave(g4_1, "gi", 4)
-        permute_s2()
-        dh_0 = product2(0, quantise(gi_0, "g"))
-        g4_2 = gather(2)
-        gi_2 = interleave(g4_2, "gi", 4)
-        permute_w2(1)
-        dm_0 = mask(0, dh_0)
-        di_0 = interleave(dm_0, "di", 4)
-        dh_1 = product2(1, quantise(gi_1, "g"))
-        g4_3 = gather(3)
-        gi_3 = interleave(g4_3, "gi", 4)
-        dm_1 = mask(1, dh_1)
-        di_1 = interleave(dm_1, "di", 4)
-        dh_2 = product2(2, quantise(gi_2, "g"))
-        product1(0, quantise(di_0, "d"))
-        dh_3 = product2(3, quantise(gi_3, "g"))
-        dm_2 = mask(2, dh_2)
-        di_2 = interleave(dm_2, "di", 4)
-        da_3 = work.tile([P, PACK, C], BF16, name="da")
-        di_3 = work.tile([P, C * PACK], BF16, name="di", align_bytes=64)
-        d_3 = (
-            work.tile([P, C], U32, name="d_codes", align_bytes=64),
-            work.tile([P, C], U8, name="d_scales", align_bytes=64),
-        )
-        parts = 2
-        wide = C // parts
-        for j in range(parts):
-            part = slice(j * wide, (j + 1) * wide)
-            for t in range(PACK):
-                nc.vector.scalar_tensor_tensor(
-                    out=da_3[:, t, part], in0=a_sb[3][:, t, part], scalar=0.0, in1=dh_3[t][:, part], op0=IS_GT, op1=MULT
-                )
-            nc.scalar.copy(
-                di_3[:, PACK * j * wide : PACK * (j + 1) * wide].rearrange("p (c i t) -> p c t i", i=4, t=PACK),
-                da_3[:, :, part].rearrange("p t (c i) -> p c t i", i=4),
-            )
-        product1(1, quantise(di_1, "d"))
-        product1(2, quantise(di_2, "d"))
-        for j in range(parts):
-            part = slice(j * wide, (j + 1) * wide)
-            nc.vector.quantize_mx(
-                out=d_3[0][:, part].bitcast(E5M2X4),
-                scales=d_3[1][:, part],
-                in_=di_3[:, PACK * j * wide : PACK * (j + 1) * wide],
-            )
-        product1(3, d_3)
+        g = [operand("g") for e in range(E)]
+        d = [operand("d") for e in range(E)]
+        da = [flat_tile(C, "da") for e in range(E)]
+        gi_0 = flat_tile(C, "gi")
+        keep = [flat_tile(C, "keep") for e in range(E)]
+        sign_2 = flat_tile(C, "sign")
+        gi_3a = flat_tile(half, "gi")
+        gi_3b = flat_tile(half, "gi")
 
-        half = T // 2
+        gather(g_0, 0, 0, C)
+        interleave(gi_0, g_0)
+        gather(g_1, 1, 0, C, (2, 3))
+        quantise(g[0], gi_0, 0, C)
+        sign_of(sign_0, 0)
+        turned = [product2(0, g[0], h) for h in range(2)]
+        gather(g_1, 1, 0, C, (0, 1))
+        interleave(gi_1, g_1)
+        clip(keep[0], sign_0)
+
+        for h in range(2):
+            masked(da[0], turned[h], keep[0], h)
+        gather(g_2, 2, 0, C, (0, 1))
+        quantise(g[1], gi_1, 0, C)
+        sign_of(sign_1, 1)
+        turned = [product2(1, g[1], h) for h in range(2)]
+        quantise(d[0], da[0], 0, C)
+        product1(0, d[0])
+        gather(g_2, 2, 0, C, (2, 3))
+        interleave(gi_2, g_2[:])
+        clip(keep[1], sign_1)
+
+        for h in range(2):
+            masked(da[1], turned[h], keep[1], h)
+        gather(g_3a, 3, 0, half)
+        quantise(g[2], gi_2, 0, C)
+        sign_of(sign_2, 2)
+        interleave(gi_3a, g_3a[:])
+        turned = [product2(2, g[2], h) for h in range(2)]
+        quantise(d[1], da[1], 0, C)
+        gather(g_3b, 3, half, half)
+        interleave(gi_3b, g_3b[:])
+        quantise(g[3], gi_3a, 0, half)
+        turned_3a = product2(3, g[3], 0)
+        product1(1, d[1])
+        clip(keep[2], sign_2)
+        masked(da[2], turned[0], keep[2], 0)
+        quantise(g[3], gi_3b, half, half)
+        masked(da[2], turned[1], keep[2], 1)
+        turned_3b = product2(3, g[3], 1)
+        keep_by_vector(keep[3], 3)
+        quantise(d[2], da[2], 0, C)
+        masked(da[3], turned_3a, keep[3], 0)
+        product1(2, d[2])
+        quantise(d[3], da[3][:, 0 : half * PACK], 0, half)
+        masked(da[3], turned_3b, keep[3], 1)
+        quantise(d[3], da[3][:, half * PACK :], half, half)
+        product1(3, d[3])
+
         first = held.tile([P, T], F32, name="first")
         nc.vector.tensor_copy(first[:], dx_sb[:].indirect(pos1_sb[:]))
-        second = [work.tile([P, half], F32, name="second") for h in range(2)]
         for h in range(2):
-            nc.vector.tensor_copy(
-                second[h][:], dx_sb[:].indirect(pos2_sb[:, h * half // 16 : (h + 1) * half // 16])
+            cols = slice(h * T // 2, (h + 1) * T // 2)
+            total = work.tile([P, T // 2], F32, name="total")
+            nc.vector.tensor_tensor(
+                total[:], dx_sb[:].indirect(pos2_sb[:, h * T // 32 : (h + 1) * T // 32]), first[:, cols], ADD
             )
-        for h in range(2):
-            total = work.tile([P, half], F32, name="total")
-            adder = nc.gpsimd if h == 0 else nc.vector
-            adder.tensor_tensor(total[:], first[:, h * half : (h + 1) * half], second[h][:], mybir.AluOpType.add)
-            nc.sync.dma_start(out=out[:, h * half : (h + 1) * half], in_=total[:])
+            nc.sync.dma_start(out=out[:, cols], in_=total[:])

@@ -57,9 +57,9 @@ def tile_moe_bdx_mlp_relu_kernel(
         g_2 = held.tile([P, PACK * C], F32, name="g_2", align_bytes=64)
         g_3a = held.tile([P, PACK * half], F32, name="g_3a", align_bytes=64)
         g_3b = held.tile([P, PACK * half], F32, name="g_3b", align_bytes=64)
-        sign_0 = g_2[:, 0 : 2 * C].bitcast(BF16)
+        keep_0 = g_2[:, 0 : 2 * C].bitcast(BF16)
         gi_1 = g_2[:, 2 * C : 4 * C].bitcast(BF16)
-        sign_1 = g_3a[:].bitcast(BF16)
+        keep_1 = g_3a[:].bitcast(BF16)
         gi_2 = g_3b[:].bitcast(BF16)
         dx_sb = held.tile([P, S], F32, name="dx_sb")
         ident = held.tile([P, P], F32, name="ident")
@@ -104,18 +104,18 @@ def tile_moe_bdx_mlp_relu_kernel(
         load_dy(2)
         load_dy(3)
         load_gate(1)
-        load_a(0)
+        load_a(1)
         load_w2(0)
         load_scales(s2_sb, s2_i32)
+        load_a(0)
         load_gate(2)
-        load_a(1)
+        load_a(2)
         load_w2(1)
         nc.sync.dma_start(
             out=w1_sb[:].bitcast(I32).rearrange("p (e w) -> p e w", e=E), in_=w1_i32[:, 0].rearrange("e p w -> p e w")
         )
         load_scales(s1_sb, s1_i32)
         load_gate(3)
-        load_a(2)
         load_a(3)
         nc.sync.dma_start(pos1_sb[:], pos1)
         nc.sync.dma_start(pos2_sb[:], pos2)
@@ -208,7 +208,8 @@ def tile_moe_bdx_mlp_relu_kernel(
         d = [operand("d") for e in range(E)]
         da = [flat_tile(C, "da") for e in range(E)]
         gi_0 = flat_tile(C, "gi")
-        keep = [flat_tile(C, "keep") for e in range(E)]
+        keep = [keep_0, keep_1, flat_tile(C, "keep"), flat_tile(C, "keep")]
+        sign_1 = flat_tile(C, "sign")
         sign_2 = flat_tile(C, "sign")
         gi_3a = flat_tile(half, "gi")
         gi_3b = flat_tile(half, "gi")
@@ -217,41 +218,40 @@ def tile_moe_bdx_mlp_relu_kernel(
         interleave(gi_0, g_0)
         gather(g_1, 1, 0, C, (2, 3))
         quantise(g[0], gi_0, 0, C)
-        sign_of(sign_0, 0)
+        sign_of(sign_1, 1)
         turned = [product2(0, g[0], h) for h in range(2)]
         gather(g_1, 1, 0, C, (0, 1))
         interleave(gi_1, g_1)
-        clip(keep[0], sign_0)
+        keep_by_vector(keep[0], 0)
+        clip(keep[1], sign_1)
 
         for h in range(2):
             masked(da[0], turned[h], keep[0], h)
         gather(g_2, 2, 0, C, (0, 1))
         quantise(g[1], gi_1, 0, C)
-        sign_of(sign_1, 1)
+        sign_of(sign_2, 2)
         turned = [product2(1, g[1], h) for h in range(2)]
         quantise(d[0], da[0], 0, C)
         product1(0, d[0])
         gather(g_2, 2, 0, C, (2, 3))
         interleave(gi_2, g_2[:])
-        clip(keep[1], sign_1)
+        clip(keep[2], sign_2)
 
         for h in range(2):
             masked(da[1], turned[h], keep[1], h)
         gather(g_3a, 3, 0, half)
         quantise(g[2], gi_2, 0, C)
-        sign_of(sign_2, 2)
         interleave(gi_3a, g_3a[:])
         turned = [product2(2, g[2], h) for h in range(2)]
         quantise(d[1], da[1], 0, C)
         gather(g_3b, 3, half, half)
         interleave(gi_3b, g_3b[:])
         quantise(g[3], gi_3a, 0, half)
-        turned_3a = product2(3, g[3], 0)
         product1(1, d[1])
-        clip(keep[2], sign_2)
+        turned_3a = product2(3, g[3], 0)
         masked(da[2], turned[0], keep[2], 0)
-        quantise(g[3], gi_3b, half, half)
         masked(da[2], turned[1], keep[2], 1)
+        quantise(g[3], gi_3b, half, half)
         turned_3b = product2(3, g[3], 1)
         keep_by_vector(keep[3], 3)
         quantise(d[2], da[2], 0, C)
@@ -264,10 +264,11 @@ def tile_moe_bdx_mlp_relu_kernel(
 
         first = held.tile([P, T], F32, name="first")
         nc.vector.tensor_copy(first[:], dx_sb[:].indirect(pos1_sb[:]))
-        for h in range(2):
-            cols = slice(h * T // 2, (h + 1) * T // 2)
-            total = work.tile([P, T // 2], F32, name="total")
+        at = 0
+        for wide in (T // 2, 3 * T // 8, T // 8):
+            total = work.tile([P, wide], F32, name="total")
             nc.vector.tensor_tensor(
-                total[:], dx_sb[:].indirect(pos2_sb[:, h * T // 32 : (h + 1) * T // 32]), first[:, cols], ADD
+                total[:], dx_sb[:].indirect(pos2_sb[:, at // 16 : (at + wide) // 16]), first[:, at : at + wide], ADD
             )
-            nc.sync.dma_start(out=out[:, cols], in_=total[:])
+            nc.sync.dma_start(out=out[:, at : at + wide], in_=total[:])
+            at = at + wide

@@ -36,8 +36,7 @@ def tile_moe_bdx_mlp_relu_kernel(
         held = ctx.enter_context(tc.tile_pool(name="held", bufs=1))
         work = ctx.enter_context(tc.tile_pool(name="work", bufs=4))
         dh_psum = ctx.enter_context(tc.psum_pool(name="dh_psum", bufs=4))
-        turn_psum = ctx.enter_context(tc.psum_pool(name="turn_psum", bufs=3))
-        dx_psum = ctx.enter_context(tc.psum_pool(name="dx_psum", bufs=1))
+        turn_psum = ctx.enter_context(tc.psum_pool(name="turn_psum", bufs=4))
 
         offs_sb = lists.tile([P, S // 16], U16, name="offs_sb")
         pos1_sb = lists.tile([P, T // 16], U16, name="pos1_sb")
@@ -51,16 +50,12 @@ def tile_moe_bdx_mlp_relu_kernel(
         dy_sb = [held.tile([P, T], F32, name=f"dy_sb{t}") for t in range(PACK)]
         gate_sb = [held.tile([P, C], F32, name=f"gate_sb{e}") for e in range(E)]
         a_sb = [held.tile([P, PACK, C], F32, name=f"a_sb{e}") for e in range(E)]
-        g_01 = held.tile([P, (PACK + 2) * C], F32, name="g_01")
-        g_0 = g_01[:, 0 : PACK * C]
-        g_1 = g_01[:, 2 * C :]
-        g_2 = held.tile([P, PACK * C], F32, name="g_2", align_bytes=64)
-        g_3a = held.tile([P, PACK * half], F32, name="g_3a", align_bytes=64)
-        g_3b = held.tile([P, PACK * half], F32, name="g_3b", align_bytes=64)
-        keep_0 = g_2[:, 0 : 2 * C].bitcast(BF16)
-        gi_1 = g_2[:, 2 * C : 4 * C].bitcast(BF16)
-        keep_1 = g_3a[:].bitcast(BF16)
-        gi_2 = g_3b[:].bitcast(BF16)
+        room = held.tile([P, 9 * C], F32, name="room", align_bytes=64)
+        gi_0 = room[:, 0 : 2 * C].bitcast(BF16)
+        g4 = [room[:, at * C : (at + PACK) * C] for at in (2, 5, 1, 5)]
+        gi_1 = held.tile([P, PACK * C], BF16, name="gi_1", align_bytes=64)
+        gi_2 = held.tile([P, PACK * C], BF16, name="gi_2", tag="gi_2", align_bytes=64)
+        keep = [gi_1[:]] + [room[:, at * C : (at + 2) * C].bitcast(BF16) for at in (1, 3, 5)]
         dx_sb = held.tile([P, S], F32, name="dx_sb")
         ident = held.tile([P, P], F32, name="ident")
 
@@ -107,15 +102,15 @@ def tile_moe_bdx_mlp_relu_kernel(
         load_a(1)
         load_w2(0)
         load_scales(s2_sb, s2_i32)
-        load_a(0)
         load_gate(2)
         load_a(2)
+        load_gate(3)
+        load_a(0)
         load_w2(1)
         nc.sync.dma_start(
             out=w1_sb[:].bitcast(I32).rearrange("p (e w) -> p e w", e=E), in_=w1_i32[:, 0].rearrange("e p w -> p e w")
         )
         load_scales(s1_sb, s1_i32)
-        load_gate(3)
         load_a(3)
         nc.sync.dma_start(pos1_sb[:], pos1)
         nc.sync.dma_start(pos2_sb[:], pos2)
@@ -183,16 +178,21 @@ def tile_moe_bdx_mlp_relu_kernel(
                 pairs = rounded[:].bitcast(F32)
                 for u in range(2):
                     nc.tensor.transpose(
-                        turned[:, 2 * b * P + u : 2 * (b + 1) * P : 2], pairs[:, u * P : (u + 1) * P], ident[:]
+                        turned[:, u * half + b * P : u * half + (b + 1) * P], pairs[:, u * P : (u + 1) * P], ident[:]
                     )
             return turned
 
         def masked(da, turned, keep, h):
             cols = slice(h * half * PACK, (h + 1) * half * PACK)
-            nc.vector.tensor_tensor(da[:, cols], turned[:].bitcast(BF16), keep[:, cols], MULT)
+            nc.vector.tensor_tensor(
+                da[:, cols].rearrange("p (c u d) -> p c u d", u=2, d=2),
+                turned[:].bitcast(BF16).rearrange("p (u c d) -> p c u d", u=2, d=2),
+                keep[:, cols].rearrange("p (c u d) -> p c u d", u=2, d=2),
+                MULT,
+            )
 
         def product1(e, d):
-            dx = dx_psum.tile([P, C], F32, name="dx")
+            dx = dh_psum.tile([P, C], F32, name="dh")
             nc.tensor.matmul_mx(
                 out=dx[:],
                 lhsT=w1_sb[:, 2 * e * K : 2 * (e + 1) * K].bitcast(E2M1X4),
@@ -207,58 +207,49 @@ def tile_moe_bdx_mlp_relu_kernel(
         g = [operand("g") for e in range(E)]
         d = [operand("d") for e in range(E)]
         da = [flat_tile(C, "da") for e in range(E)]
-        gi_0 = flat_tile(C, "gi")
-        keep = [keep_0, keep_1, flat_tile(C, "keep"), flat_tile(C, "keep")]
         sign_1 = flat_tile(C, "sign")
         sign_2 = flat_tile(C, "sign")
-        gi_3a = flat_tile(half, "gi")
-        gi_3b = flat_tile(half, "gi")
+        gi_3 = flat_tile(C, "gi")
 
-        gather(g_0, 0, 0, C)
-        interleave(gi_0, g_0)
-        gather(g_1, 1, 0, C, (2, 3))
+        gather(g4[0], 0, 0, C)
+        interleave(gi_0, g4[0])
+        gather(g4[1], 1, 0, C, (1, 2, 3))
         quantise(g[0], gi_0, 0, C)
         sign_of(sign_1, 1)
-        turned = [product2(0, g[0], h) for h in range(2)]
-        gather(g_1, 1, 0, C, (0, 1))
-        interleave(gi_1, g_1)
-        keep_by_vector(keep[0], 0)
-        clip(keep[1], sign_1)
-
-        for h in range(2):
-            masked(da[0], turned[h], keep[0], h)
-        gather(g_2, 2, 0, C, (0, 1))
-        quantise(g[1], gi_1, 0, C)
+        turned_0 = [product2(0, g[0], h) for h in range(2)]
+        gather(g4[1], 1, 0, C, (0,))
+        interleave(gi_1[:], g4[1])
+        gather(g4[2], 2, 0, C, (1, 2, 3, 0))
+        quantise(g[1], gi_1[:], 0, C)
         sign_of(sign_2, 2)
-        turned = [product2(1, g[1], h) for h in range(2)]
+        turned_1 = [product2(1, g[1], h) for h in range(2)]
+        interleave(gi_2[:], g4[2])
+        gather(g4[3], 3, 0, C)
+        interleave(gi_3, g4[3])
+        keep_by_vector(keep[0], 0)
+        for h in range(2):
+            masked(da[0], turned_0[h], keep[0], h)
+        quantise(g[2], gi_2[:], 0, C)
+        turned_2 = [product2(2, g[2], h) for h in range(2)]
+        clip(keep[1], sign_1)
+        clip(keep[2], sign_2)
+        for h in range(2):
+            masked(da[1], turned_1[h], keep[1], h)
+        quantise(g[3], gi_3, 0, C)
+        turned_3 = [product2(3, g[3], h) for h in range(2)]
+        d[0] = (held.tile([P, C], U32, name="d_codes_0", tag="gi_2", align_bytes=64), d[0][1])
         quantise(d[0], da[0], 0, C)
         product1(0, d[0])
-        gather(g_2, 2, 0, C, (2, 3))
-        interleave(gi_2, g_2[:])
-        clip(keep[2], sign_2)
-
-        for h in range(2):
-            masked(da[1], turned[h], keep[1], h)
-        gather(g_3a, 3, 0, half)
-        quantise(g[2], gi_2, 0, C)
-        interleave(gi_3a, g_3a[:])
-        turned = [product2(2, g[2], h) for h in range(2)]
         quantise(d[1], da[1], 0, C)
-        gather(g_3b, 3, half, half)
-        interleave(gi_3b, g_3b[:])
-        quantise(g[3], gi_3a, 0, half)
         product1(1, d[1])
-        turned_3a = product2(3, g[3], 0)
-        masked(da[2], turned[0], keep[2], 0)
-        masked(da[2], turned[1], keep[2], 1)
-        quantise(g[3], gi_3b, half, half)
-        turned_3b = product2(3, g[3], 1)
         keep_by_vector(keep[3], 3)
+        for h in range(2):
+            masked(da[2], turned_2[h], keep[2], h)
+        masked(da[3], turned_3[0], keep[3], 0)
         quantise(d[2], da[2], 0, C)
-        masked(da[3], turned_3a, keep[3], 0)
         product1(2, d[2])
+        masked(da[3], turned_3[1], keep[3], 1)
         quantise(d[3], da[3][:, 0 : half * PACK], 0, half)
-        masked(da[3], turned_3b, keep[3], 1)
         quantise(d[3], da[3][:, half * PACK :], half, half)
         product1(3, d[3])
 

@@ -55,7 +55,8 @@ def tile_moe_bdx_mlp_relu_kernel(
         g4 = [room[:, at * C : (at + PACK) * C] for at in (2, 5, 1, 5)]
         gi_1 = held.tile([P, PACK * C], BF16, name="gi_1", align_bytes=64)
         gi_2 = held.tile([P, PACK * C], BF16, name="gi_2", tag="gi_2", align_bytes=64)
-        keep = [gi_1[:]] + [room[:, at * C : (at + 2) * C].bitcast(BF16) for at in (1, 3, 5)]
+        keep_1 = held.tile([P, PACK * C], BF16, name="keep_1")
+        keep = [gi_1[:], keep_1[:]] + [room[:, at * C : (at + 2) * C].bitcast(BF16) for at in (4, 6)]
         dx_sb = held.tile([P, S], F32, name="dx_sb")
         ident = held.tile([P, P], F32, name="ident")
 
@@ -115,11 +116,11 @@ def tile_moe_bdx_mlp_relu_kernel(
         nc.sync.dma_start(pos1_sb[:], pos1)
         nc.sync.dma_start(pos2_sb[:], pos2)
 
-        def gather(dst, e, first, wide, planes=range(PACK)):
+        def gather(e, planes, first=0, wide=C):
             at = (e * C + first) // 16
             for t in planes:
                 nc.vector.tensor_tensor(
-                    dst[:, t * wide : (t + 1) * wide],
+                    g4[e][:, t * C + first : t * C + first + wide],
                     dy_sb[t][:].indirect(offs_sb[:, at : at + wide // 16]),
                     gate_sb[e][:, first : first + wide],
                     MULT,
@@ -128,11 +129,15 @@ def tile_moe_bdx_mlp_relu_kernel(
         def side_by_side(flat):
             return flat.rearrange("p (c i t) -> p c t i", i=4, t=PACK)
 
+        def in_pairs(flat):
+            return flat.rearrange("p (u c d) -> p u c d", u=2, d=2)
+
         def by_planes(planes):
             return planes.rearrange("p t (c i) -> p c t i", i=4)
 
-        def interleave(flat, src):
-            nc.scalar.copy(side_by_side(flat), by_planes(src.rearrange("p (t c) -> p t c", t=PACK)))
+        def interleave(flat, e, first=0, wide=C):
+            planes = g4[e].rearrange("p (t c) -> p t c", t=PACK)[:, :, first : first + wide]
+            nc.scalar.copy(side_by_side(flat[:, PACK * first : PACK * (first + wide)]), by_planes(planes))
 
         def flat_tile(wide, name):
             return work.tile([P, wide * PACK], BF16, name=name, align_bytes=64)[:]
@@ -148,13 +153,15 @@ def tile_moe_bdx_mlp_relu_kernel(
             )
 
         def sign_of(sign, e):
-            nc.scalar.activation(side_by_side(sign), by_planes(a_sb[e][:]), SIGN)
+            nc.scalar.activation(in_pairs(sign), a_sb[e][:].rearrange("p (u d) c -> p u c d", u=2), SIGN)
 
         def clip(keep, sign):
             nc.vector.tensor_scalar(keep, sign, 0.0, None, op0=MAX)
 
         def keep_by_vector(keep, e):
-            nc.vector.tensor_scalar(side_by_side(keep), by_planes(a_sb[e][:]), 0.0, None, op0=IS_GT)
+            nc.vector.tensor_scalar(
+                in_pairs(keep), a_sb[e][:].rearrange("p (u d) c -> p u c d", u=2), 0.0, None, op0=IS_GT
+            )
 
         def product2(e, g, h):
             turned = turn_psum.tile([P, 2 * half], F32, name="turned")
@@ -187,7 +194,7 @@ def tile_moe_bdx_mlp_relu_kernel(
             nc.vector.tensor_tensor(
                 da[:, cols].rearrange("p (c u d) -> p c u d", u=2, d=2),
                 turned[:].bitcast(BF16).rearrange("p (u c d) -> p c u d", u=2, d=2),
-                keep[:, cols].rearrange("p (c u d) -> p c u d", u=2, d=2),
+                in_pairs(keep)[:, :, h * half : (h + 1) * half, :].rearrange("p u c d -> p c u d"),
                 MULT,
             )
 
@@ -206,33 +213,37 @@ def tile_moe_bdx_mlp_relu_kernel(
 
         g = [operand("g") for e in range(E)]
         d = [operand("d") for e in range(E)]
-        da = [flat_tile(C, "da") for e in range(E)]
+        da = [gi_0, room[:, 2 * C : 4 * C].bitcast(BF16), flat_tile(C, "da"), flat_tile(C, "da")]
         sign_1 = flat_tile(C, "sign")
         sign_2 = flat_tile(C, "sign")
         gi_3 = flat_tile(C, "gi")
 
-        gather(g4[0], 0, 0, C)
-        interleave(gi_0, g4[0])
-        gather(g4[1], 1, 0, C, (1, 2, 3))
-        quantise(g[0], gi_0, 0, C)
+        gather(0, (0, 1, 2))
+        for h in range(2):
+            gather(0, (3,), h * half, half)
+            interleave(gi_0, 0, h * half, half)
+        gather(1, (1, 2))
+        quantise(g[0], gi_0[:, 0 : PACK * half], 0, half)
+        gather(1, (3,))
+        quantise(g[0], gi_0[:, PACK * half :], half, half)
         sign_of(sign_1, 1)
         turned_0 = [product2(0, g[0], h) for h in range(2)]
-        gather(g4[1], 1, 0, C, (0,))
-        interleave(gi_1[:], g4[1])
-        gather(g4[2], 2, 0, C, (1, 2, 3, 0))
+        gather(1, (0,))
+        interleave(gi_1[:], 1)
+        gather(2, (1, 2, 3, 0))
+        clip(keep[1], sign_1)
         quantise(g[1], gi_1[:], 0, C)
         sign_of(sign_2, 2)
         turned_1 = [product2(1, g[1], h) for h in range(2)]
-        interleave(gi_2[:], g4[2])
-        gather(g4[3], 3, 0, C)
-        interleave(gi_3, g4[3])
+        interleave(gi_2[:], 2)
+        gather(3, (0, 1, 2))
         keep_by_vector(keep[0], 0)
-        for h in range(2):
-            masked(da[0], turned_0[h], keep[0], h)
+        gather(3, (3,))
+        interleave(gi_3, 3)
+        masked(da[0], turned_0[0], keep[0], 0)
         quantise(g[2], gi_2[:], 0, C)
         turned_2 = [product2(2, g[2], h) for h in range(2)]
-        clip(keep[1], sign_1)
-        clip(keep[2], sign_2)
+        masked(da[0], turned_0[1], keep[0], 1)
         for h in range(2):
             masked(da[1], turned_1[h], keep[1], h)
         quantise(g[3], gi_3, 0, C)
@@ -240,11 +251,12 @@ def tile_moe_bdx_mlp_relu_kernel(
         d[0] = (held.tile([P, C], U32, name="d_codes_0", tag="gi_2", align_bytes=64), d[0][1])
         quantise(d[0], da[0], 0, C)
         product1(0, d[0])
-        quantise(d[1], da[1], 0, C)
-        product1(1, d[1])
+        clip(keep[2], sign_2)
         keep_by_vector(keep[3], 3)
         for h in range(2):
             masked(da[2], turned_2[h], keep[2], h)
+        quantise(d[1], da[1], 0, C)
+        product1(1, d[1])
         masked(da[3], turned_3[0], keep[3], 0)
         quantise(d[2], da[2], 0, C)
         product1(2, d[2])
@@ -254,7 +266,10 @@ def tile_moe_bdx_mlp_relu_kernel(
         product1(3, d[3])
 
         first = held.tile([P, T], F32, name="first")
-        nc.vector.tensor_copy(first[:], dx_sb[:].indirect(pos1_sb[:]))
+        for h in range(2):
+            nc.vector.tensor_copy(
+                first[:, h * T // 2 : (h + 1) * T // 2], dx_sb[:].indirect(pos1_sb[:, h * T // 32 : (h + 1) * T // 32])
+            )
         at = 0
         for wide in (T // 2, 3 * T // 8, T // 8):
             total = work.tile([P, wide], F32, name="total")

@@ -43,20 +43,20 @@ def tile_moe_bdx_mlp_relu_kernel(
         pos2_sb = lists.tile([P, T // 16], U16, name="pos2_sb")
 
         half = C // 2
-        w2_sb = [held.tile([P, 2 * 2 * H], U8, name=f"w2_sb{h}", align_bytes=64) for h in range(2)]
+        w2_sb = held.tile([P, E * 2 * H], U8, name="w2_sb", align_bytes=64)
         s2_sb = held.tile([P, E * H], U8, name="s2_sb", align_bytes=64)
         w1_sb = held.tile([P, E * 2 * K], U8, name="w1_sb", align_bytes=64)
         s1_sb = held.tile([P, E * K], U8, name="s1_sb", align_bytes=64)
         dy_sb = [held.tile([P, T], F32, name=f"dy_sb{t}") for t in range(PACK)]
         gate_sb = [held.tile([P, C], F32, name=f"gate_sb{e}") for e in range(E)]
         a_sb = [held.tile([P, PACK, C], F32, name=f"a_sb{e}") for e in range(E)]
-        room = held.tile([P, 9 * C], F32, name="room", align_bytes=64)
-        gi_0 = room[:, 0 : 2 * C].bitcast(BF16)
-        g4 = [room[:, at * C : (at + PACK) * C] for at in (2, 5, 1, 5)]
-        gi_1 = held.tile([P, PACK * C], BF16, name="gi_1", align_bytes=64)
+        room = held.tile([P, 10 * C], F32, name="room", align_bytes=64)
+        g4 = [room[:, at * C : (at + PACK) * C] for at in (4, 2, 5, 1)]
+        gi_0 = room[:, 8 * C : 10 * C].bitcast(BF16)
+        gi_1 = room[:, 0 : 2 * C].bitcast(BF16)
         gi_2 = held.tile([P, PACK * C], BF16, name="gi_2", tag="gi_2", align_bytes=64)
-        keep_1 = held.tile([P, PACK * C], BF16, name="keep_1")
-        keep = [gi_1[:], keep_1[:]] + [room[:, at * C : (at + 2) * C].bitcast(BF16) for at in (4, 6)]
+        keep_0, keep_3 = [room[:, at * C : (at + 2) * C].bitcast(BF16) for at in (7, 3)]
+        keep = [keep_0] + [held.tile([P, PACK * C], BF16, name=f"keep_{e}")[:] for e in (1, 2)] + [keep_3]
         dx_sb = held.tile([P, S], F32, name="dx_sb")
         ident = held.tile([P, P], F32, name="ident")
 
@@ -71,17 +71,15 @@ def tile_moe_bdx_mlp_relu_kernel(
         dy_planes = dyT.rearrange("(p t) c -> p t c", t=PACK)
         a_planes = a.rearrange("(p t) c -> p t c", t=PACK)
 
-        def load_w2(h):
-            nc.sync.dma_start(
-                out=w2_sb[h][:].bitcast(I32).rearrange("p (e w) -> p e w", e=2),
-                in_=w2_i32[2 * h : 2 * h + 2, 0].rearrange("e p w -> p e w"),
-            )
+        def load_words(dst, src, first, last):
+            rows = dst[:].bitcast(I32).rearrange("p (e w) -> p e w", e=E)
+            nc.sync.dma_start(out=rows[:, first:last, :], in_=src[first:last, 0].rearrange("e p w -> p e w"))
 
-        def load_scales(dst, src):
+        def load_scales(dst, src, first, last):
             for q in range(4):
+                rows = dst[32 * q : 32 * q + 4, :].bitcast(I32).rearrange("p (e w) -> p e w", e=E)
                 nc.sync.dma_start(
-                    out=dst[32 * q : 32 * q + 4, :].bitcast(I32).rearrange("p (e w) -> p e w", e=E),
-                    in_=src[:, 0, 4 * q : 4 * q + 4, :].rearrange("e f w -> f e w"),
+                    out=rows[:, first:last, :], in_=src[first:last, 0, 4 * q : 4 * q + 4, :].rearrange("e f w -> f e w")
                 )
 
         def load_dy(t):
@@ -101,17 +99,15 @@ def tile_moe_bdx_mlp_relu_kernel(
         load_dy(3)
         load_gate(1)
         load_a(1)
-        load_w2(0)
-        load_scales(s2_sb, s2_i32)
+        load_words(w2_sb, w2_i32, 0, 2)
+        load_scales(s2_sb, s2_i32, 0, E)
         load_gate(2)
         load_a(2)
         load_gate(3)
         load_a(0)
-        load_w2(1)
-        nc.sync.dma_start(
-            out=w1_sb[:].bitcast(I32).rearrange("p (e w) -> p e w", e=E), in_=w1_i32[:, 0].rearrange("e p w -> p e w")
-        )
-        load_scales(s1_sb, s1_i32)
+        load_words(w2_sb, w2_i32, 2, E)
+        load_words(w1_sb, w1_i32, 0, E)
+        load_scales(s1_sb, s1_i32, 0, E)
         load_a(3)
         nc.sync.dma_start(pos1_sb[:], pos1)
         nc.sync.dma_start(pos2_sb[:], pos2)
@@ -129,9 +125,6 @@ def tile_moe_bdx_mlp_relu_kernel(
         def side_by_side(flat):
             return flat.rearrange("p (c i t) -> p c t i", i=4, t=PACK)
 
-        def in_pairs(flat):
-            return flat.rearrange("p (u c d) -> p u c d", u=2, d=2)
-
         def by_planes(planes):
             return planes.rearrange("p t (c i) -> p c t i", i=4)
 
@@ -145,7 +138,7 @@ def tile_moe_bdx_mlp_relu_kernel(
         def operand(name):
             codes = work.tile([P, C], U32, name=name + "_codes", align_bytes=64)
             scales = work.tile([P, C], U8, name=name + "_scales", align_bytes=64)
-            return codes, scales
+            return codes[:], scales[:]
 
         def quantise(dst, flat, first, wide):
             nc.vector.quantize_mx(
@@ -153,15 +146,13 @@ def tile_moe_bdx_mlp_relu_kernel(
             )
 
         def sign_of(sign, e):
-            nc.scalar.activation(in_pairs(sign), a_sb[e][:].rearrange("p (u d) c -> p u c d", u=2), SIGN)
+            nc.scalar.activation(side_by_side(sign), by_planes(a_sb[e][:]), SIGN)
 
         def clip(keep, sign):
             nc.vector.tensor_scalar(keep, sign, 0.0, None, op0=MAX)
 
         def keep_by_vector(keep, e):
-            nc.vector.tensor_scalar(
-                in_pairs(keep), a_sb[e][:].rearrange("p (u d) c -> p u c d", u=2), 0.0, None, op0=IS_GT
-            )
+            nc.vector.tensor_scalar(side_by_side(keep), by_planes(a_sb[e][:]), 0.0, None, op0=IS_GT)
 
         def product2(e, g, h):
             turned = turn_psum.tile([P, 2 * half], F32, name="turned")
@@ -172,7 +163,7 @@ def tile_moe_bdx_mlp_relu_kernel(
                     out=dh[:],
                     lhsT=g[0][:, at : at + P].bitcast(E5M2X4),
                     lhsT_scale=g[1][:, at : at + P],
-                    rhs=w2_sb[e // 2][:, (e % 2) * 2 * H : (e % 2 + 1) * 2 * H].bitcast(E2M1X4),
+                    rhs=w2_sb[:, e * 2 * H : (e + 1) * 2 * H].bitcast(E2M1X4),
                     rhs_scale=s2_sb[:, e * H : (e + 1) * H],
                     start=True,
                     stop=True,
@@ -194,26 +185,28 @@ def tile_moe_bdx_mlp_relu_kernel(
             nc.vector.tensor_tensor(
                 da[:, cols].rearrange("p (c u d) -> p c u d", u=2, d=2),
                 turned[:].bitcast(BF16).rearrange("p (u c d) -> p c u d", u=2, d=2),
-                in_pairs(keep)[:, :, h * half : (h + 1) * half, :].rearrange("p u c d -> p c u d"),
+                keep[:, cols].rearrange("p (c u d) -> p c u d", u=2, d=2),
                 MULT,
             )
 
-        def product1(e, d):
+        def product1(e, d, first=0, wide=C, to=0):
             dx = dh_psum.tile([P, C], F32, name="dh")
             nc.tensor.matmul_mx(
                 out=dx[:],
                 lhsT=w1_sb[:, 2 * e * K : 2 * (e + 1) * K].bitcast(E2M1X4),
                 lhsT_scale=s1_sb[:, e * K : (e + 1) * K],
-                rhs=d[0][:].bitcast(E5M2X4),
-                rhs_scale=d[1][:],
+                rhs=d[0].bitcast(E5M2X4),
+                rhs_scale=d[1],
                 start=True,
                 stop=True,
             )
-            nc.scalar.copy(dx_sb[:, e * C : (e + 1) * C], dx[:])
+            nc.scalar.copy(dx_sb[:, e * C + to : e * C + to + wide], dx[:, first : first + wide])
 
         g = [operand("g") for e in range(E)]
-        d = [operand("d") for e in range(E)]
-        da = [gi_0, room[:, 2 * C : 4 * C].bitcast(BF16), flat_tile(C, "da"), flat_tile(C, "da")]
+        d_codes = held.tile([P, 2 * C], U32, name="d_codes_23", align_bytes=64)
+        d_scales = held.tile([P, 2 * C], U8, name="d_scales_23", align_bytes=64)
+        d = [operand("d"), operand("d")] + [(d_codes[:, j * C : (j + 1) * C], d_scales[:, j * C : (j + 1) * C]) for j in range(2)]
+        da = [flat_tile(C, "da"), room[:, 5 * C : 7 * C].bitcast(BF16), flat_tile(C, "da"), flat_tile(C, "da")]
         sign_1 = flat_tile(C, "sign")
         sign_2 = flat_tile(C, "sign")
         gi_3 = flat_tile(C, "gi")
@@ -222,37 +215,35 @@ def tile_moe_bdx_mlp_relu_kernel(
         for h in range(2):
             gather(0, (3,), h * half, half)
             interleave(gi_0, 0, h * half, half)
-        gather(1, (1, 2))
-        quantise(g[0], gi_0[:, 0 : PACK * half], 0, half)
-        gather(1, (3,))
-        quantise(g[0], gi_0[:, PACK * half :], half, half)
+        gather(1, (0, 1))
+        quantise(g[0], gi_0, 0, C)
         sign_of(sign_1, 1)
         turned_0 = [product2(0, g[0], h) for h in range(2)]
-        gather(1, (0,))
-        interleave(gi_1[:], 1)
-        gather(2, (1, 2, 3, 0))
+        gather(1, (2, 3))
+        interleave(gi_1, 1)
+        gather(2, (1, 2, 3))
         clip(keep[1], sign_1)
-        quantise(g[1], gi_1[:], 0, C)
+        quantise(g[1], gi_1, 0, C)
         sign_of(sign_2, 2)
         turned_1 = [product2(1, g[1], h) for h in range(2)]
+        gather(2, (0,))
         interleave(gi_2[:], 2)
-        gather(3, (0, 1, 2))
-        keep_by_vector(keep[0], 0)
-        gather(3, (3,))
+        gather(3, (1, 2, 3, 0))
         interleave(gi_3, 3)
-        masked(da[0], turned_0[0], keep[0], 0)
+        clip(keep[2], sign_2)
         quantise(g[2], gi_2[:], 0, C)
         turned_2 = [product2(2, g[2], h) for h in range(2)]
-        masked(da[0], turned_0[1], keep[0], 1)
-        for h in range(2):
-            masked(da[1], turned_1[h], keep[1], h)
+        masked(da[1], turned_1[0], keep[1], 0)
+        keep_by_vector(keep[0], 0)
+        masked(da[1], turned_1[1], keep[1], 1)
+        masked(da[0], turned_0[0], keep[0], 0)
         quantise(g[3], gi_3, 0, C)
         turned_3 = [product2(3, g[3], h) for h in range(2)]
-        d[0] = (held.tile([P, C], U32, name="d_codes_0", tag="gi_2", align_bytes=64), d[0][1])
+        masked(da[0], turned_0[1], keep[0], 1)
+        d[0] = (held.tile([P, C], U32, name="d_codes_0", tag="gi_2", align_bytes=64)[:], d[0][1])
+        keep_by_vector(keep[3], 3)
         quantise(d[0], da[0], 0, C)
         product1(0, d[0])
-        clip(keep[2], sign_2)
-        keep_by_vector(keep[3], 3)
         for h in range(2):
             masked(da[2], turned_2[h], keep[2], h)
         quantise(d[1], da[1], 0, C)
@@ -262,8 +253,9 @@ def tile_moe_bdx_mlp_relu_kernel(
         product1(2, d[2])
         masked(da[3], turned_3[1], keep[3], 1)
         quantise(d[3], da[3][:, 0 : half * PACK], 0, half)
+        product1(3, (d_codes[:, half : half + C], d_scales[:, half : half + C]), half, half, 0)
         quantise(d[3], da[3][:, half * PACK :], half, half)
-        product1(3, d[3])
+        product1(3, d[3], half, half, half)
 
         first = held.tile([P, T], F32, name="first")
         for h in range(2):

@@ -43,13 +43,16 @@ def tile_moe_bdx_mlp_relu_kernel(
         pos2_sb = lists.tile([P, T // 16], U16, name="pos2_sb")
 
         half = C // 2
-        w2_sb = held.tile([P, E * 2 * H], U8, name="w2_sb", align_bytes=64)
-        s2_sb = held.tile([P, E * H], U8, name="s2_sb", align_bytes=64)
+        w2_sb = [held.tile([P, n * 2 * H], U8, name=f"w2_sb{j}", align_bytes=64) for j, n in enumerate((1, 1, 2))]
+        s2_sb = [held.tile([P, n * H], U8, name=f"s2_sb{j}", align_bytes=64) for j, n in enumerate((1, 3))]
+        w2_of = [w2_sb[0][:], w2_sb[1][:], w2_sb[2][:, 0 : 2 * H], w2_sb[2][:, 2 * H :]]
+        s2_of = [s2_sb[0][:]] + [s2_sb[1][:, j * H : (j + 1) * H] for j in range(3)]
         w1_sb = held.tile([P, E * 2 * K], U8, name="w1_sb", align_bytes=64)
         s1_sb = held.tile([P, E * K], U8, name="s1_sb", align_bytes=64)
         dy_sb = [held.tile([P, T], F32, name=f"dy_sb{t}") for t in range(PACK)]
         gate_sb = [held.tile([P, C], F32, name=f"gate_sb{e}") for e in range(E)]
-        a_sb = [held.tile([P, PACK, C], F32, name=f"a_sb{e}") for e in range(E)]
+        a_sb = {e: held.tile([P, PACK, C], F32, name=f"a_sb{e}") for e in (0, 2, 3)}
+        a_1 = [held.tile([P, 2, C], F32, name=f"a_1{u}") for u in range(2)]
         room = held.tile([P, 10 * C], F32, name="room", align_bytes=64)
         g4 = [room[:, at * C : (at + PACK) * C] for at in (4, 2, 5, 1)]
         gi_0 = room[:, 8 * C : 10 * C].bitcast(BF16)
@@ -60,7 +63,8 @@ def tile_moe_bdx_mlp_relu_kernel(
         dx_sb = held.tile([P, S], F32, name="dx_sb")
         ident = held.tile([P, P], F32, name="ident")
 
-        nc.gpsimd.memset(s2_sb[:].bitcast(I32), 0)
+        for plane in s2_sb:
+            nc.gpsimd.memset(plane[:].bitcast(I32), 0)
         nc.gpsimd.memset(s1_sb[:].bitcast(I32), 0)
         make_identity(nc, ident[:])
 
@@ -72,14 +76,14 @@ def tile_moe_bdx_mlp_relu_kernel(
         a_planes = a.rearrange("(p t) c -> p t c", t=PACK)
 
         def load_words(dst, src, first, last):
-            rows = dst[:].bitcast(I32).rearrange("p (e w) -> p e w", e=E)
-            nc.sync.dma_start(out=rows[:, first:last, :], in_=src[first:last, 0].rearrange("e p w -> p e w"))
+            rows = dst[:].bitcast(I32).rearrange("p (e w) -> p e w", e=last - first)
+            nc.sync.dma_start(out=rows, in_=src[first:last, 0].rearrange("e p w -> p e w"))
 
-        def load_scales(dst, src, first, last):
+        def load_scales(dst, src, first, last, queue=nc.sync):
             for q in range(4):
-                rows = dst[32 * q : 32 * q + 4, :].bitcast(I32).rearrange("p (e w) -> p e w", e=E)
-                nc.sync.dma_start(
-                    out=rows[:, first:last, :], in_=src[first:last, 0, 4 * q : 4 * q + 4, :].rearrange("e f w -> f e w")
+                rows = dst[32 * q : 32 * q + 4, :].bitcast(I32).rearrange("p (e w) -> p e w", e=last - first)
+                queue.dma_start(
+                    out=rows, in_=src[first:last, 0, 4 * q : 4 * q + 4, :].rearrange("e f w -> f e w")
                 )
 
         def load_dy(t):
@@ -94,18 +98,21 @@ def tile_moe_bdx_mlp_relu_kernel(
         load_dy(0)
         nc.sync.dma_start(offs_sb[:], offs)
         load_gate(0)
+        load_scales(s2_sb[0], s2_i32, 0, 1, nc.scalar)
         load_dy(1)
         load_dy(2)
         load_dy(3)
         load_gate(1)
-        load_a(1)
-        load_words(w2_sb, w2_i32, 0, 2)
-        load_scales(s2_sb, s2_i32, 0, E)
+        for u in range(2):
+            nc.sync.dma_start(out=a_1[u][:], in_=a_planes[:, 2 * u : 2 * u + 2, C : 2 * C])
+        load_words(w2_sb[0], w2_i32, 0, 1)
         load_gate(2)
         load_a(2)
+        load_words(w2_sb[1], w2_i32, 1, 2)
+        load_scales(s2_sb[1], s2_i32, 1, E)
         load_gate(3)
         load_a(0)
-        load_words(w2_sb, w2_i32, 2, E)
+        load_words(w2_sb[2], w2_i32, 2, E)
         load_words(w1_sb, w1_i32, 0, E)
         load_scales(s1_sb, s1_i32, 0, E)
         load_a(3)
@@ -124,6 +131,9 @@ def tile_moe_bdx_mlp_relu_kernel(
 
         def side_by_side(flat):
             return flat.rearrange("p (c i t) -> p c t i", i=4, t=PACK)
+
+        def in_pairs(flat):
+            return flat.rearrange("p (u c d) -> p u c d", u=2, d=2)
 
         def by_planes(planes):
             return planes.rearrange("p t (c i) -> p c t i", i=4)
@@ -146,13 +156,15 @@ def tile_moe_bdx_mlp_relu_kernel(
             )
 
         def sign_of(sign, e):
-            nc.scalar.activation(side_by_side(sign), by_planes(a_sb[e][:]), SIGN)
+            nc.scalar.activation(in_pairs(sign), a_sb[e][:].rearrange("p (u d) c -> p u c d", u=2), SIGN)
 
         def clip(keep, sign):
             nc.vector.tensor_scalar(keep, sign, 0.0, None, op0=MAX)
 
         def keep_by_vector(keep, e):
-            nc.vector.tensor_scalar(side_by_side(keep), by_planes(a_sb[e][:]), 0.0, None, op0=IS_GT)
+            nc.vector.tensor_scalar(
+                in_pairs(keep), a_sb[e][:].rearrange("p (u d) c -> p u c d", u=2), 0.0, None, op0=IS_GT
+            )
 
         def product2(e, g, h):
             turned = turn_psum.tile([P, 2 * half], F32, name="turned")
@@ -163,8 +175,8 @@ def tile_moe_bdx_mlp_relu_kernel(
                     out=dh[:],
                     lhsT=g[0][:, at : at + P].bitcast(E5M2X4),
                     lhsT_scale=g[1][:, at : at + P],
-                    rhs=w2_sb[:, e * 2 * H : (e + 1) * 2 * H].bitcast(E2M1X4),
-                    rhs_scale=s2_sb[:, e * H : (e + 1) * H],
+                    rhs=w2_of[e].bitcast(E2M1X4),
+                    rhs_scale=s2_of[e],
                     start=True,
                     stop=True,
                 )
@@ -185,7 +197,7 @@ def tile_moe_bdx_mlp_relu_kernel(
             nc.vector.tensor_tensor(
                 da[:, cols].rearrange("p (c u d) -> p c u d", u=2, d=2),
                 turned[:].bitcast(BF16).rearrange("p (u c d) -> p c u d", u=2, d=2),
-                keep[:, cols].rearrange("p (c u d) -> p c u d", u=2, d=2),
+                in_pairs(keep)[:, :, h * half : (h + 1) * half, :].rearrange("p u c d -> p c u d"),
                 MULT,
             )
 
@@ -217,7 +229,8 @@ def tile_moe_bdx_mlp_relu_kernel(
             interleave(gi_0, 0, h * half, half)
         gather(1, (0, 1))
         quantise(g[0], gi_0, 0, C)
-        sign_of(sign_1, 1)
+        for u in range(2):
+            nc.scalar.activation(in_pairs(sign_1)[:, u], a_1[u][:].rearrange("p d c -> p c d"), SIGN)
         turned_0 = [product2(0, g[0], h) for h in range(2)]
         gather(1, (2, 3))
         interleave(gi_1, 1)

@@ -23,6 +23,7 @@ E2M1X4 = mybir.dt.float4_e2m1fn_x4
 MULT = mybir.AluOpType.mult
 ADD = mybir.AluOpType.add
 MAX = mybir.AluOpType.max
+MIN = mybir.AluOpType.min
 IS_GT = mybir.AluOpType.is_gt
 SIGN = mybir.ActivationFunctionType.Sign
 
@@ -34,8 +35,9 @@ def tile_moe_bdx_mlp_relu_kernel(
     with ExitStack() as ctx:
         lists = ctx.enter_context(tc.tile_pool(name="lists", bufs=1))
         held = ctx.enter_context(tc.tile_pool(name="held", bufs=1))
+        over = ctx.enter_context(tc.tile_pool(name="over", bufs=1))
         work = ctx.enter_context(tc.tile_pool(name="work", bufs=4))
-        dh_psum = ctx.enter_context(tc.psum_pool(name="dh_psum", bufs=4))
+        dh_psum = ctx.enter_context(tc.psum_pool(name="dh_psum", bufs=1))
         turn_psum = ctx.enter_context(tc.psum_pool(name="turn_psum", bufs=4))
 
         offs_sb = lists.tile([P, S // 16], U16, name="offs_sb")
@@ -50,16 +52,19 @@ def tile_moe_bdx_mlp_relu_kernel(
         w1_sb = held.tile([P, E * 2 * K], U8, name="w1_sb", align_bytes=64)
         s1_sb = held.tile([P, E * K], U8, name="s1_sb", align_bytes=64)
         dy_sb = [held.tile([P, T], F32, name=f"dy_sb{t}") for t in range(PACK)]
-        gate_sb = [held.tile([P, C], F32, name=f"gate_sb{e}") for e in range(E)]
-        a_sb = {e: held.tile([P, PACK, C], F32, name=f"a_sb{e}") for e in (0, 2, 3)}
-        a_1 = [held.tile([P, 2, C], F32, name=f"a_1{u}") for u in range(2)]
+        a_sb = {e: held.tile([P, PACK, C], F32, name=f"a_sb{e}")[:] for e in (0, 1)}
+        a_sb[2] = over.tile([P, PACK, C], F32, name="a_sb2", offset=0, align_bytes=64)[:]
+        a_3 = [held.tile([P, 2, C], F32, name=f"a_3{u}") for u in range(2)]
+        early = held.tile([P, half], F32, name="early")
         room = held.tile([P, 10 * C], F32, name="room", align_bytes=64)
         g4 = [room[:, at * C : (at + PACK) * C] for at in (4, 2, 5, 1)]
+        gate_sb = [held.tile([P, C], F32, name=f"gate_sb{e}")[:] for e in (0, 1, 3)]
+        gate_sb.insert(2, room[:, C : 2 * C])
         gi_0 = room[:, 8 * C : 10 * C].bitcast(BF16)
-        gi_1 = room[:, 0 : 2 * C].bitcast(BF16)
-        gi_2 = held.tile([P, PACK * C], BF16, name="gi_2", tag="gi_2", align_bytes=64)
-        keep_0, keep_3 = [room[:, at * C : (at + 2) * C].bitcast(BF16) for at in (7, 3)]
-        keep = [keep_0] + [held.tile([P, PACK * C], BF16, name=f"keep_{e}")[:] for e in (1, 2)] + [keep_3]
+        gi_1 = held.tile([P, PACK * C], BF16, name="gi_1", align_bytes=64)[:]
+        gi_3 = held.tile([P, PACK * C], BF16, name="gi_3", align_bytes=64)[:]
+        keep_0 = held.tile([P, PACK * C], BF16, name="keep_0")
+        keep = [keep_0[:], room[:, 7 * C : 9 * C].bitcast(BF16), room[:, 5 * C : 7 * C].bitcast(BF16), gi_1]
         dx_sb = held.tile([P, S], F32, name="dx_sb")
         ident = held.tile([P, P], F32, name="ident")
 
@@ -90,10 +95,10 @@ def tile_moe_bdx_mlp_relu_kernel(
             nc.sync.dma_start(out=dy_sb[t][:], in_=dy_planes[:, t, :])
 
         def load_gate(e):
-            nc.sync.dma_start(out=gate_sb[e][:], in_=gate[0:P, e * C : (e + 1) * C])
+            nc.sync.dma_start(out=gate_sb[e], in_=gate[0:P, e * C : (e + 1) * C])
 
         def load_a(e):
-            nc.sync.dma_start(out=a_sb[e][:], in_=a_planes[:, :, e * C : (e + 1) * C])
+            nc.sync.dma_start(out=a_sb[e], in_=a_planes[:, :, e * C : (e + 1) * C])
 
         load_dy(0)
         nc.sync.dma_start(offs_sb[:], offs)
@@ -104,18 +109,18 @@ def tile_moe_bdx_mlp_relu_kernel(
         load_dy(3)
         load_gate(1)
         for u in range(2):
-            nc.sync.dma_start(out=a_1[u][:], in_=a_planes[:, 2 * u : 2 * u + 2, C : 2 * C])
+            nc.sync.dma_start(out=a_3[u][:], in_=a_planes[:, 2 * u : 2 * u + 2, 3 * C :])
         load_words(w2_sb[0], w2_i32, 0, 1)
         load_gate(2)
+        load_a(0)
         load_a(2)
         load_words(w2_sb[1], w2_i32, 1, 2)
         load_scales(s2_sb[1], s2_i32, 1, E)
         load_gate(3)
-        load_a(0)
+        load_a(1)
         load_words(w2_sb[2], w2_i32, 2, E)
         load_words(w1_sb, w1_i32, 0, E)
         load_scales(s1_sb, s1_i32, 0, E)
-        load_a(3)
         nc.sync.dma_start(pos1_sb[:], pos1)
         nc.sync.dma_start(pos2_sb[:], pos2)
 
@@ -156,21 +161,21 @@ def tile_moe_bdx_mlp_relu_kernel(
             )
 
         def sign_of(sign, e):
-            nc.scalar.activation(in_pairs(sign), a_sb[e][:].rearrange("p (u d) c -> p u c d", u=2), SIGN)
+            nc.scalar.activation(in_pairs(sign), a_sb[e].rearrange("p (u d) c -> p u c d", u=2), SIGN)
 
         def clip(keep, sign):
             nc.vector.tensor_scalar(keep, sign, 0.0, None, op0=MAX)
 
         def keep_by_vector(keep, e):
             nc.vector.tensor_scalar(
-                in_pairs(keep), a_sb[e][:].rearrange("p (u d) c -> p u c d", u=2), 0.0, None, op0=IS_GT
+                in_pairs(keep), a_sb[e].rearrange("p (u d) c -> p u c d", u=2), 0.0, None, op0=IS_GT
             )
 
-        def product2(e, g, h):
+        def product2(e, g, h, space=None):
             turned = turn_psum.tile([P, 2 * half], F32, name="turned")
             for b in range(2):
                 at = h * half + b * P
-                dh = dh_psum.tile([P, H], F32, name="dh")
+                dh = dh_psum.tile([P, H], F32, name="dh", tag=f"bank{2 * h + b}")
                 nc.tensor.matmul_mx(
                     out=dh[:],
                     lhsT=g[0][:, at : at + P].bitcast(E5M2X4),
@@ -180,12 +185,15 @@ def tile_moe_bdx_mlp_relu_kernel(
                     start=True,
                     stop=True,
                 )
-                rounded = work.tile([P, H], BF16, name="rounded")
+                if space is None:
+                    rounded = work.tile([P, H], BF16, name="rounded")[:]
+                else:
+                    rounded = space[:, b * H : (b + 1) * H]
                 nc.scalar.copy(
-                    rounded[:].rearrange("s (u p d) -> s u p d", u=2, d=2),
+                    rounded.rearrange("s (u p d) -> s u p d", u=2, d=2),
                     dh[:].rearrange("s (p u d) -> s u p d", u=2, d=2),
                 )
-                pairs = rounded[:].bitcast(F32)
+                pairs = rounded.bitcast(F32)
                 for u in range(2):
                     nc.tensor.transpose(
                         turned[:, u * half + b * P : u * half + (b + 1) * P], pairs[:, u * P : (u + 1) * P], ident[:]
@@ -201,8 +209,8 @@ def tile_moe_bdx_mlp_relu_kernel(
                 MULT,
             )
 
-        def product1(e, d, first=0, wide=C, to=0):
-            dx = dh_psum.tile([P, C], F32, name="dh")
+        def product1(e, d, bank, first=0, wide=C, to=0):
+            dx = dh_psum.tile([P, C], F32, name="dx", tag=f"bank{bank}")
             nc.tensor.matmul_mx(
                 out=dx[:],
                 lhsT=w1_sb[:, 2 * e * K : 2 * (e + 1) * K].bitcast(E2M1X4),
@@ -216,13 +224,12 @@ def tile_moe_bdx_mlp_relu_kernel(
 
         g = [operand("g") for e in range(E)]
         d_codes = held.tile([P, 2 * C], U32, name="d_codes_23", align_bytes=64)
-        d_scales = held.tile([P, 2 * C], U8, name="d_scales_23", align_bytes=64)
-        d = [operand("d"), operand("d")] + [(d_codes[:, j * C : (j + 1) * C], d_scales[:, j * C : (j + 1) * C]) for j in range(2)]
-        da = [flat_tile(C, "da"), room[:, 5 * C : 7 * C].bitcast(BF16), flat_tile(C, "da"), flat_tile(C, "da")]
-        sign_1 = flat_tile(C, "sign")
+        d = [operand("d"), operand("d")]
+        da = [gi_1, room[:, C : 3 * C].bitcast(BF16), flat_tile(C, "da"), flat_tile(C, "da")]
+        sign_3 = flat_tile(C, "sign")
         sign_2 = flat_tile(C, "sign")
-        gi_3 = flat_tile(C, "gi")
 
+        nc.vector.tensor_copy(early[:], dy_sb[0][:].indirect(offs_sb[:, 3 * C // 16 : (3 * C + half) // 16]))
         gather(0, (0, 1, 2))
         for h in range(2):
             gather(0, (3,), h * half, half)
@@ -230,45 +237,57 @@ def tile_moe_bdx_mlp_relu_kernel(
         gather(1, (0, 1))
         quantise(g[0], gi_0, 0, C)
         for u in range(2):
-            nc.scalar.activation(in_pairs(sign_1)[:, u], a_1[u][:].rearrange("p d c -> p c d"), SIGN)
+            nc.scalar.activation(in_pairs(sign_3)[:, u], a_3[u][:].rearrange("p d c -> p c d"), SIGN)
         turned_0 = [product2(0, g[0], h) for h in range(2)]
         gather(1, (2, 3))
         interleave(gi_1, 1)
         gather(2, (1, 2, 3))
-        clip(keep[1], sign_1)
+        keep_by_vector(keep[0], 0)
         quantise(g[1], gi_1, 0, C)
         sign_of(sign_2, 2)
-        turned_1 = [product2(1, g[1], h) for h in range(2)]
+        rounded_1 = over.tile([P, 4 * H], BF16, name="rounded_1", offset=0, align_bytes=64)
+        gi_2 = over.tile([P, PACK * C], BF16, name="gi_2", offset=8 * C, align_bytes=64)
+        turned_1 = [product2(1, g[1], h, rounded_1[:, 2 * h * H :]) for h in range(2)]
         gather(2, (0,))
         interleave(gi_2[:], 2)
-        gather(3, (1, 2, 3, 0))
-        interleave(gi_3, 3)
-        clip(keep[2], sign_2)
-        quantise(g[2], gi_2[:], 0, C)
-        turned_2 = [product2(2, g[2], h) for h in range(2)]
-        masked(da[1], turned_1[0], keep[1], 0)
-        keep_by_vector(keep[0], 0)
-        masked(da[1], turned_1[1], keep[1], 1)
-        masked(da[0], turned_0[0], keep[0], 0)
-        quantise(g[3], gi_3, 0, C)
-        turned_3 = [product2(3, g[3], h) for h in range(2)]
-        masked(da[0], turned_0[1], keep[0], 1)
-        d[0] = (held.tile([P, C], U32, name="d_codes_0", tag="gi_2", align_bytes=64)[:], d[0][1])
-        keep_by_vector(keep[3], 3)
-        quantise(d[0], da[0], 0, C)
-        product1(0, d[0])
+        nc.gpsimd.tensor_tensor(g4[3][:, 0:half], early[:], gate_sb[3][:, 0:half], MULT)
         for h in range(2):
-            masked(da[2], turned_2[h], keep[2], h)
+            masked(da[0], turned_0[h], keep[0], h)
+        gather(3, (1, 2))
+        gather(3, (3,), 0, half)
+        interleave(gi_3, 3, 0, half)
+        gather(3, (0, 3), half, half)
+        interleave(gi_3, 3, half, half)
+        quantise(g[2], gi_2[:], 0, C)
+        rounded_2 = held.tile([P, 2 * H], BF16, name="rounded_2", tag="late_2", align_bytes=64)
+        turned_2 = [product2(2, g[2], 0), product2(2, g[2], 1, rounded_2)]
+        clip(keep[2], sign_2)
+        keep_by_vector(keep[1], 1)
+        d[0] = (over.tile([P, C], U32, name="d_codes_0", offset=8 * C, align_bytes=64)[:], d[0][1])
+        quantise(d[0], da[0], 0, C)
+        nc.gpsimd.tensor_scalar(keep[3], sign_3, 1.0, 0.0, op0=MIN, op1=MAX)
+        quantise(g[3], gi_3, 0, C)
+        rounded_3 = [held.tile([P, 2 * H], BF16, name=f"rounded_3{h}", tag=f"late_{h}", align_bytes=64) for h in range(2)]
+        turned_3 = [product2(3, g[3], h, rounded_3[h]) for h in range(2)]
+        for e, turned in ((1, turned_1), (2, turned_2)):
+            for h in range(2):
+                masked(da[e], turned[h], keep[e], h)
+        product1(0, d[0], 1)
+        d[1] = (held.tile([P, C], U32, name="d_codes_1", tag="late_2", align_bytes=64)[:], d[1][1])
         quantise(d[1], da[1], 0, C)
-        product1(1, d[1])
+        product1(1, d[1], 3)
         masked(da[3], turned_3[0], keep[3], 0)
+        d.append((d_codes[:, 0:C], held.tile([P, C], U8, name="d_scales_2", tag="late_0", align_bytes=64)[:]))
         quantise(d[2], da[2], 0, C)
-        product1(2, d[2])
+        product1(2, d[2], 2)
         masked(da[3], turned_3[1], keep[3], 1)
+        d_scales = held.tile([P, half + C], U8, name="d_scales_3", tag="late_1", align_bytes=64)
+        nc.gpsimd.memset(d_scales[:, 0:half].bitcast(I32), 0)
+        d.append((d_codes[:, C:], d_scales[:, half:]))
         quantise(d[3], da[3][:, 0 : half * PACK], 0, half)
-        product1(3, (d_codes[:, half : half + C], d_scales[:, half : half + C]), half, half, 0)
+        product1(3, (d_codes[:, half : half + C], d_scales[:, 0:C]), 0, half, half, 0)
         quantise(d[3], da[3][:, half * PACK :], half, half)
-        product1(3, d[3], half, half, half)
+        product1(3, d[3], 1, half, half, half)
 
         first = held.tile([P, T], F32, name="first")
         for h in range(2):

@@ -196,7 +196,7 @@ def tile_moe_bdx_mlp_relu_kernel(
                 pairs = rounded.bitcast(F32)
                 for u in range(2):
                     nc.tensor.transpose(
-                        turned[:, u * half + b * P : u * half + (b + 1) * P], pairs[:, u * P : (u + 1) * P], ident[:]
+                        turned[:].rearrange("p (c u) -> p c u", u=2)[:, b * P : (b + 1) * P, u], pairs[:, u * P : (u + 1) * P], ident[:]
                     )
             return turned
 
@@ -204,7 +204,7 @@ def tile_moe_bdx_mlp_relu_kernel(
             cols = slice(h * half * PACK, (h + 1) * half * PACK)
             nc.vector.tensor_tensor(
                 da[:, cols].rearrange("p (c u d) -> p c u d", u=2, d=2),
-                turned[:].bitcast(BF16).rearrange("p (u c d) -> p c u d", u=2, d=2),
+                turned[:].bitcast(BF16).rearrange("p (c u d) -> p c u d", u=2, d=2),
                 in_pairs(keep)[:, :, h * half : (h + 1) * half, :].rearrange("p u c d -> p c u d"),
                 MULT,
             )

@@ -55,7 +55,8 @@ def tile_moe_bdx_mlp_relu_kernel(
         a_sb = {e: held.tile([P, PACK, C], F32, name=f"a_sb{e}")[:] for e in (0, 1)}
         a_sb[2] = over.tile([P, PACK, C], F32, name="a_sb2", offset=0, align_bytes=64)[:]
         a_3 = [held.tile([P, 2, C], F32, name=f"a_3{u}") for u in range(2)]
-        early = held.tile([P, half], F32, name="early")
+        ahead = half + 64
+        early = held.tile([P, ahead], F32, name="early")
         room = held.tile([P, 10 * C], F32, name="room", align_bytes=64)
         g4 = [room[:, at * C : (at + PACK) * C] for at in (4, 2, 5, 1)]
         gate_sb = [held.tile([P, C], F32, name=f"gate_sb{e}")[:] for e in (0, 1, 3)]
@@ -171,15 +172,14 @@ def tile_moe_bdx_mlp_relu_kernel(
                 in_pairs(keep), a_sb[e].rearrange("p (u d) c -> p u c d", u=2), 0.0, None, op0=IS_GT
             )
 
-        def product2(e, g, h, space=None):
+        def product2(e, g, blocks, space=None):
             turned = turn_psum.tile([P, 2 * half], F32, name="turned")
-            for b in range(2):
-                at = h * half + b * P
-                dh = dh_psum.tile([P, H], F32, name="dh", tag=f"bank{2 * h + b}")
+            for n, b in enumerate(blocks):
+                dh = dh_psum.tile([P, H], F32, name="dh", tag=f"bank{b}")
                 nc.tensor.matmul_mx(
                     out=dh[:],
-                    lhsT=g[0][:, at : at + P].bitcast(E5M2X4),
-                    lhsT_scale=g[1][:, at : at + P],
+                    lhsT=g[0][:, b * P : (b + 1) * P].bitcast(E5M2X4),
+                    lhsT_scale=g[1][:, b * P : (b + 1) * P],
                     rhs=w2_of[e].bitcast(E2M1X4),
                     rhs_scale=s2_of[e],
                     start=True,
@@ -188,7 +188,7 @@ def tile_moe_bdx_mlp_relu_kernel(
                 if space is None:
                     rounded = work.tile([P, H], BF16, name="rounded")[:]
                 else:
-                    rounded = space[:, b * H : (b + 1) * H]
+                    rounded = space[:, (b % 2) * H : (b % 2 + 1) * H]
                 nc.scalar.copy(
                     rounded.rearrange("s (u p d) -> s u p d", u=2, d=2),
                     dh[:].rearrange("s (p u d) -> s u p d", u=2, d=2),
@@ -196,16 +196,18 @@ def tile_moe_bdx_mlp_relu_kernel(
                 pairs = rounded.bitcast(F32)
                 for u in range(2):
                     nc.tensor.transpose(
-                        turned[:].rearrange("p (c u) -> p c u", u=2)[:, b * P : (b + 1) * P, u], pairs[:, u * P : (u + 1) * P], ident[:]
+                        turned[:].rearrange("p (c u) -> p c u", u=2)[:, n * P : (n + 1) * P, u],
+                        pairs[:, u * P : (u + 1) * P],
+                        ident[:],
                     )
-            return turned
+            return turned[:, 0 : 2 * P * len(blocks)], blocks[0] * P, len(blocks) * P
 
-        def masked(da, turned, keep, h):
-            cols = slice(h * half * PACK, (h + 1) * half * PACK)
+        def masked(da, product, keep):
+            turned, first, wide = product
             nc.vector.tensor_tensor(
-                da[:, cols].rearrange("p (c u d) -> p c u d", u=2, d=2),
-                turned[:].bitcast(BF16).rearrange("p (c u d) -> p c u d", u=2, d=2),
-                in_pairs(keep)[:, :, h * half : (h + 1) * half, :].rearrange("p u c d -> p c u d"),
+                da[:, first * PACK : (first + wide) * PACK].rearrange("p (c u d) -> p c u d", u=2, d=2),
+                turned.bitcast(BF16).rearrange("p (c u d) -> p c u d", u=2, d=2),
+                in_pairs(keep)[:, :, first : first + wide, :].rearrange("p u c d -> p c u d"),
                 MULT,
             )
 
@@ -229,7 +231,7 @@ def tile_moe_bdx_mlp_relu_kernel(
         sign_3 = flat_tile(C, "sign")
         sign_2 = flat_tile(C, "sign")
 
-        nc.vector.tensor_copy(early[:], dy_sb[0][:].indirect(offs_sb[:, 3 * C // 16 : (3 * C + half) // 16]))
+        nc.vector.tensor_copy(early[:], dy_sb[0][:].indirect(offs_sb[:, 3 * C // 16 : (3 * C + ahead) // 16]))
         gather(0, (0, 1, 2))
         for h in range(2):
             gather(0, (3,), h * half, half)
@@ -238,7 +240,7 @@ def tile_moe_bdx_mlp_relu_kernel(
         quantise(g[0], gi_0, 0, C)
         for u in range(2):
             nc.scalar.activation(in_pairs(sign_3)[:, u], a_3[u][:].rearrange("p d c -> p c d"), SIGN)
-        turned_0 = [product2(0, g[0], h) for h in range(2)]
+        turned_0 = [product2(0, g[0], (2 * h, 2 * h + 1)) for h in range(2)]
         gather(1, (2, 3))
         interleave(gi_1, 1)
         gather(2, (1, 2, 3))
@@ -247,20 +249,21 @@ def tile_moe_bdx_mlp_relu_kernel(
         sign_of(sign_2, 2)
         rounded_1 = over.tile([P, 4 * H], BF16, name="rounded_1", offset=0, align_bytes=64)
         gi_2 = over.tile([P, PACK * C], BF16, name="gi_2", offset=8 * C, align_bytes=64)
-        turned_1 = [product2(1, g[1], h, rounded_1[:, 2 * h * H :]) for h in range(2)]
+        turned_1 = [product2(1, g[1], (2 * h, 2 * h + 1), rounded_1[:, 2 * h * H :]) for h in range(2)]
         gather(2, (0,))
         interleave(gi_2[:], 2)
-        nc.gpsimd.tensor_tensor(g4[3][:, 0:half], early[:], gate_sb[3][:, 0:half], MULT)
+        nc.gpsimd.tensor_tensor(g4[3][:, 0:ahead], early[:], gate_sb[3][:, 0:ahead], MULT)
         for h in range(2):
-            masked(da[0], turned_0[h], keep[0], h)
+            masked(da[0], turned_0[h], keep[0])
         gather(3, (1, 2))
         gather(3, (3,), 0, half)
         interleave(gi_3, 3, 0, half)
-        gather(3, (0, 3), half, half)
+        gather(3, (0,), ahead, C - ahead)
+        gather(3, (3,), half, half)
         interleave(gi_3, 3, half, half)
         quantise(g[2], gi_2[:], 0, C)
         rounded_2 = held.tile([P, 2 * H], BF16, name="rounded_2", tag="late_2", align_bytes=64)
-        turned_2 = [product2(2, g[2], 0), product2(2, g[2], 1, rounded_2)]
+        turned_2 = [product2(2, g[2], (0, 1)), product2(2, g[2], (2, 3), rounded_2)]
         clip(keep[2], sign_2)
         keep_by_vector(keep[1], 1)
         d[0] = (over.tile([P, C], U32, name="d_codes_0", offset=8 * C, align_bytes=64)[:], d[0][1])
@@ -268,19 +271,20 @@ def tile_moe_bdx_mlp_relu_kernel(
         nc.gpsimd.tensor_scalar(keep[3], sign_3, 1.0, 0.0, op0=MIN, op1=MAX)
         quantise(g[3], gi_3, 0, C)
         rounded_3 = [held.tile([P, 2 * H], BF16, name=f"rounded_3{h}", tag=f"late_{h}", align_bytes=64) for h in range(2)]
-        turned_3 = [product2(3, g[3], h, rounded_3[h]) for h in range(2)]
+        turned_3 = [product2(3, g[3], blocks, rounded_3[blocks[0] // 2]) for blocks in ((0, 1), (2,), (3,))]
         for e, turned in ((1, turned_1), (2, turned_2)):
             for h in range(2):
-                masked(da[e], turned[h], keep[e], h)
+                masked(da[e], turned[h], keep[e])
         product1(0, d[0], 1)
         d[1] = (held.tile([P, C], U32, name="d_codes_1", tag="late_2", align_bytes=64)[:], d[1][1])
         quantise(d[1], da[1], 0, C)
         product1(1, d[1], 3)
-        masked(da[3], turned_3[0], keep[3], 0)
+        masked(da[3], turned_3[0], keep[3])
         d.append((d_codes[:, 0:C], held.tile([P, C], U8, name="d_scales_2", tag="late_0", align_bytes=64)[:]))
         quantise(d[2], da[2], 0, C)
         product1(2, d[2], 2)
-        masked(da[3], turned_3[1], keep[3], 1)
+        masked(da[3], turned_3[1], keep[3])
+        masked(da[3], turned_3[2], keep[3])
         d_scales = held.tile([P, half + C], U8, name="d_scales_3", tag="late_1", align_bytes=64)
         nc.gpsimd.memset(d_scales[:, 0:half].bitcast(I32), 0)
         d.append((d_codes[:, C:], d_scales[:, half:]))

@@ -69,10 +69,10 @@ def tile_moe_bdx_mlp_relu_kernel(
         dx_sb = held.tile([P, S], F32, name="dx_sb")
         ident = held.tile([P, P], F32, name="ident")
 
+        make_identity(nc, ident[:])
         for plane in s2_sb:
             nc.gpsimd.memset(plane[:].bitcast(I32), 0)
         nc.gpsimd.memset(s1_sb[:].bitcast(I32), 0)
-        make_identity(nc, ident[:])
 
         w2_i32 = w2_words.bitcast(I32)
         w1_i32 = w1_words.bitcast(I32)

@@ -8,6 +8,8 @@ T, E, C = 1024, 4, 512
 S = E * C
 P = 128
 PACK = 4
+HALF = C // 2
+AHEAD = HALF + 64
 
 FLOPS = 2 * S * (N * H + H * K)
 BYTES = 4 * N * T + 4 * H * S + E * (N * H + H * K) // 2 + E * (N * H + H * K) // 32 + 4 * S + 2 * P * (S + 2 * T) // 16 + 4 * K * T
@@ -36,15 +38,14 @@ def tile_moe_bdx_mlp_relu_kernel(
         lists = ctx.enter_context(tc.tile_pool(name="lists", bufs=1))
         held = ctx.enter_context(tc.tile_pool(name="held", bufs=1))
         over = ctx.enter_context(tc.tile_pool(name="over", bufs=1))
-        work = ctx.enter_context(tc.tile_pool(name="work", bufs=4))
-        dh_psum = ctx.enter_context(tc.psum_pool(name="dh_psum", bufs=1))
+        work = ctx.enter_context(tc.tile_pool(name="work", bufs=E))
+        sum_psum = ctx.enter_context(tc.psum_pool(name="dh_psum", bufs=1))
         turn_psum = ctx.enter_context(tc.psum_pool(name="turn_psum", bufs=4))
 
         offs_sb = lists.tile([P, S // 16], U16, name="offs_sb")
         pos1_sb = lists.tile([P, T // 16], U16, name="pos1_sb")
         pos2_sb = lists.tile([P, T // 16], U16, name="pos2_sb")
 
-        half = C // 2
         w2_sb = [held.tile([P, n * 2 * H], U8, name=f"w2_sb{j}", align_bytes=64) for j, n in enumerate((1, 1, 2))]
         s2_sb = [held.tile([P, n * H], U8, name=f"s2_sb{j}", align_bytes=64) for j, n in enumerate((1, 3))]
         w2_of = [w2_sb[0][:], w2_sb[1][:], w2_sb[2][:, 0 : 2 * H], w2_sb[2][:, 2 * H :]]
@@ -55,23 +56,23 @@ def tile_moe_bdx_mlp_relu_kernel(
         a_sb = {e: held.tile([P, PACK, C], F32, name=f"a_sb{e}")[:] for e in (0, 1)}
         a_sb[2] = over.tile([P, PACK, C], F32, name="a_sb2", offset=0, align_bytes=64)[:]
         a_3 = [held.tile([P, 2, C], F32, name=f"a_3{u}") for u in range(2)]
-        ahead = half + 64
-        early = held.tile([P, ahead], F32, name="early")
+        early = held.tile([P, AHEAD], F32, name="early")
+
         room = held.tile([P, 10 * C], F32, name="room", align_bytes=64)
-        g4 = [room[:, at * C : (at + PACK) * C] for at in (4, 2, 5, 1)]
+        planes_of = [room[:, at * C : (at + PACK) * C] for at in (4, 2, 5, 1)]
         gate_sb = [held.tile([P, C], F32, name=f"gate_sb{e}")[:] for e in (0, 1, 3)]
         gate_sb.insert(2, room[:, C : 2 * C])
-        gi_0 = room[:, 8 * C : 10 * C].bitcast(BF16)
-        gi_1 = held.tile([P, PACK * C], BF16, name="gi_1", align_bytes=64)[:]
-        gi_3 = held.tile([P, PACK * C], BF16, name="gi_3", align_bytes=64)[:]
-        keep_0 = held.tile([P, PACK * C], BF16, name="keep_0")
-        keep = [keep_0[:], room[:, 7 * C : 9 * C].bitcast(BF16), room[:, 5 * C : 7 * C].bitcast(BF16), gi_1]
+        woven_0 = room[:, 8 * C : 10 * C].bitcast(BF16)
+        woven_1 = held.tile([P, PACK * C], BF16, name="gi_1", align_bytes=64)[:]
+        woven_3 = held.tile([P, PACK * C], BF16, name="gi_3", align_bytes=64)[:]
+        mask_0 = held.tile([P, PACK * C], BF16, name="keep_0")
+        mask = [mask_0[:], room[:, 7 * C : 9 * C].bitcast(BF16), room[:, 5 * C : 7 * C].bitcast(BF16), woven_1]
         dx_sb = held.tile([P, S], F32, name="dx_sb")
         ident = held.tile([P, P], F32, name="ident")
 
         make_identity(nc, ident[:])
-        for plane in s2_sb:
-            nc.gpsimd.memset(plane[:].bitcast(I32), 0)
+        for scales in s2_sb:
+            nc.gpsimd.memset(scales[:].bitcast(I32), 0)
         nc.gpsimd.memset(s1_sb[:].bitcast(I32), 0)
 
         w2_i32 = w2_words.bitcast(I32)
@@ -129,57 +130,43 @@ def tile_moe_bdx_mlp_relu_kernel(
             at = (e * C + first) // 16
             for t in planes:
                 nc.vector.tensor_tensor(
-                    g4[e][:, t * C + first : t * C + first + wide],
+                    planes_of[e][:, t * C + first : t * C + first + wide],
                     dy_sb[t][:].indirect(offs_sb[:, at : at + wide // 16]),
                     gate_sb[e][:, first : first + wide],
                     MULT,
                 )
 
-        def side_by_side(flat):
-            return flat.rearrange("p (c i t) -> p c t i", i=4, t=PACK)
+        def interleave(woven, e, first=0, wide=C):
+            planes = planes_of[e].rearrange("p (t c) -> p t c", t=PACK)[:, :, first : first + wide]
+            nc.scalar.copy(
+                woven[:, PACK * first : PACK * (first + wide)].rearrange("p (c i t) -> p c t i", i=4, t=PACK),
+                planes.rearrange("p t (c i) -> p c t i", i=4),
+            )
 
         def in_pairs(flat):
             return flat.rearrange("p (u c d) -> p u c d", u=2, d=2)
 
-        def by_planes(planes):
-            return planes.rearrange("p t (c i) -> p c t i", i=4)
+        def expert_tile(name):
+            return work.tile([P, C * PACK], BF16, name=name, align_bytes=64)[:]
 
-        def interleave(flat, e, first=0, wide=C):
-            planes = g4[e].rearrange("p (t c) -> p t c", t=PACK)[:, :, first : first + wide]
-            nc.scalar.copy(side_by_side(flat[:, PACK * first : PACK * (first + wide)]), by_planes(planes))
-
-        def flat_tile(wide, name):
-            return work.tile([P, wide * PACK], BF16, name=name, align_bytes=64)[:]
-
-        def operand(name):
-            codes = work.tile([P, C], U32, name=name + "_codes", align_bytes=64)
-            scales = work.tile([P, C], U8, name=name + "_scales", align_bytes=64)
-            return codes[:], scales[:]
-
-        def quantise(dst, flat, first, wide):
+        def quantise(dst, woven, first, wide):
             nc.vector.quantize_mx(
-                out=dst[0][:, first : first + wide].bitcast(E5M2X4), scales=dst[1][:, first : first + wide], in_=flat
+                out=dst[0][:, first : first + wide].bitcast(E5M2X4), scales=dst[1][:, first : first + wide], in_=woven
             )
 
-        def sign_of(sign, e):
-            nc.scalar.activation(in_pairs(sign), a_sb[e].rearrange("p (u d) c -> p u c d", u=2), SIGN)
-
-        def clip(keep, sign):
-            nc.vector.tensor_scalar(keep, sign, 0.0, None, op0=MAX)
-
-        def keep_by_vector(keep, e):
+        def mask_from_a(e):
             nc.vector.tensor_scalar(
-                in_pairs(keep), a_sb[e].rearrange("p (u d) c -> p u c d", u=2), 0.0, None, op0=IS_GT
+                in_pairs(mask[e]), a_sb[e].rearrange("p (u d) c -> p u c d", u=2), 0.0, None, op0=IS_GT
             )
 
-        def product2(e, g, blocks, space=None):
-            turned = turn_psum.tile([P, 2 * half], F32, name="turned")
+        def product2(e, g_e, blocks, space=None):
+            turned = turn_psum.tile([P, 2 * HALF], F32, name="turned")
             for n, b in enumerate(blocks):
-                dh = dh_psum.tile([P, H], F32, name="dh", tag=f"bank{b}")
+                dh = sum_psum.tile([P, H], F32, name="dh", tag=f"bank{b}")
                 nc.tensor.matmul_mx(
                     out=dh[:],
-                    lhsT=g[0][:, b * P : (b + 1) * P].bitcast(E5M2X4),
-                    lhsT_scale=g[1][:, b * P : (b + 1) * P],
+                    lhsT=g_e[0][:, b * P : (b + 1) * P].bitcast(E5M2X4),
+                    lhsT_scale=g_e[1][:, b * P : (b + 1) * P],
                     rhs=w2_of[e].bitcast(E2M1X4),
                     rhs_scale=s2_of[e],
                     start=True,
@@ -202,107 +189,117 @@ def tile_moe_bdx_mlp_relu_kernel(
                     )
             return turned[:, 0 : 2 * P * len(blocks)], blocks[0] * P, len(blocks) * P
 
-        def masked(da, product, keep):
+        def masked(e, product):
             turned, first, wide = product
             nc.vector.tensor_tensor(
-                da[:, first * PACK : (first + wide) * PACK].rearrange("p (c u d) -> p c u d", u=2, d=2),
+                da[e][:, first * PACK : (first + wide) * PACK].rearrange("p (c u d) -> p c u d", u=2, d=2),
                 turned.bitcast(BF16).rearrange("p (c u d) -> p c u d", u=2, d=2),
-                in_pairs(keep)[:, :, first : first + wide, :].rearrange("p u c d -> p c u d"),
+                in_pairs(mask[e])[:, :, first : first + wide, :].rearrange("p u c d -> p c u d"),
                 MULT,
             )
 
-        def product1(e, d, bank, first=0, wide=C, to=0):
-            dx = dh_psum.tile([P, C], F32, name="dx", tag=f"bank{bank}")
+        def product1(e, d_e, bank, first=0, wide=C, to=0):
+            dx = sum_psum.tile([P, C], F32, name="dx", tag=f"bank{bank}")
             nc.tensor.matmul_mx(
                 out=dx[:],
                 lhsT=w1_sb[:, 2 * e * K : 2 * (e + 1) * K].bitcast(E2M1X4),
                 lhsT_scale=s1_sb[:, e * K : (e + 1) * K],
-                rhs=d[0].bitcast(E5M2X4),
-                rhs_scale=d[1],
+                rhs=d_e[0].bitcast(E5M2X4),
+                rhs_scale=d_e[1],
                 start=True,
                 stop=True,
             )
             nc.scalar.copy(dx_sb[:, e * C + to : e * C + to + wide], dx[:, first : first + wide])
 
-        g = [operand("g") for e in range(E)]
-        d_codes = held.tile([P, 2 * C], U32, name="d_codes_23", align_bytes=64)
-        d = [operand("d"), operand("d")]
-        da = [gi_1, room[:, C : 3 * C].bitcast(BF16), flat_tile(C, "da"), flat_tile(C, "da")]
-        sign_3 = flat_tile(C, "sign")
-        sign_2 = flat_tile(C, "sign")
+        g = [
+            (
+                work.tile([P, C], U32, name="g_codes", align_bytes=64)[:],
+                work.tile([P, C], U8, name="g_scales", align_bytes=64)[:],
+            )
+            for e in range(E)
+        ]
+        d_codes_23 = held.tile([P, 2 * C], U32, name="d_codes_23", align_bytes=64)
+        d_scales = [work.tile([P, C], U8, name="d_scales", align_bytes=64)[:] for e in range(2)]
+        da = [woven_1, room[:, C : 3 * C].bitcast(BF16), expert_tile("da"), expert_tile("da")]
+        sign_3 = expert_tile("sign")
+        sign_2 = expert_tile("sign")
+        both_halves = ((0, 1), (2, 3))
 
-        nc.vector.tensor_copy(early[:], dy_sb[0][:].indirect(offs_sb[:, 3 * C // 16 : (3 * C + ahead) // 16]))
+        nc.vector.tensor_copy(early[:], dy_sb[0][:].indirect(offs_sb[:, 3 * C // 16 : (3 * C + AHEAD) // 16]))
         gather(0, (0, 1, 2))
         for h in range(2):
-            gather(0, (3,), h * half, half)
-            interleave(gi_0, 0, h * half, half)
+            gather(0, (3,), h * HALF, HALF)
+            interleave(woven_0, 0, h * HALF, HALF)
         gather(1, (0, 1))
-        quantise(g[0], gi_0, 0, C)
+        quantise(g[0], woven_0, 0, C)
         for u in range(2):
             nc.scalar.activation(in_pairs(sign_3)[:, u], a_3[u][:].rearrange("p d c -> p c d"), SIGN)
-        turned_0 = [product2(0, g[0], (2 * h, 2 * h + 1)) for h in range(2)]
+        turned_0 = [product2(0, g[0], blocks) for blocks in both_halves]
         gather(1, (2, 3))
-        interleave(gi_1, 1)
+        interleave(woven_1, 1)
         gather(2, (1, 2, 3))
-        keep_by_vector(keep[0], 0)
-        quantise(g[1], gi_1, 0, C)
-        sign_of(sign_2, 2)
+        mask_from_a(0)
+        quantise(g[1], woven_1, 0, C)
+        nc.scalar.activation(in_pairs(sign_2), a_sb[2].rearrange("p (u d) c -> p u c d", u=2), SIGN)
         rounded_1 = over.tile([P, 4 * H], BF16, name="rounded_1", offset=0, align_bytes=64)
-        gi_2 = over.tile([P, PACK * C], BF16, name="gi_2", offset=8 * C, align_bytes=64)
-        turned_1 = [product2(1, g[1], (2 * h, 2 * h + 1), rounded_1[:, 2 * h * H :]) for h in range(2)]
+        woven_2 = over.tile([P, PACK * C], BF16, name="gi_2", offset=8 * C, align_bytes=64)
+        turned_1 = [product2(1, g[1], blocks, rounded_1[:, blocks[0] * H :]) for blocks in both_halves]
         gather(2, (0,))
-        interleave(gi_2[:], 2)
-        nc.gpsimd.tensor_tensor(g4[3][:, 0:ahead], early[:], gate_sb[3][:, 0:ahead], MULT)
-        for h in range(2):
-            masked(da[0], turned_0[h], keep[0])
+        interleave(woven_2[:], 2)
+        nc.gpsimd.tensor_tensor(planes_of[3][:, 0:AHEAD], early[:], gate_sb[3][:, 0:AHEAD], MULT)
+        for product in turned_0:
+            masked(0, product)
         gather(3, (1, 2))
-        gather(3, (3,), 0, half)
-        interleave(gi_3, 3, 0, half)
-        gather(3, (0,), ahead, C - ahead)
-        gather(3, (3,), half, half)
-        interleave(gi_3, 3, half, half)
-        quantise(g[2], gi_2[:], 0, C)
+        gather(3, (3,), 0, HALF)
+        interleave(woven_3, 3, 0, HALF)
+        gather(3, (0,), AHEAD, C - AHEAD)
+        gather(3, (3,), HALF, HALF)
+        interleave(woven_3, 3, HALF, HALF)
+        quantise(g[2], woven_2[:], 0, C)
         rounded_2 = held.tile([P, 2 * H], BF16, name="rounded_2", tag="late_2", align_bytes=64)
         turned_2 = [product2(2, g[2], (0, 1)), product2(2, g[2], (2, 3), rounded_2)]
-        clip(keep[2], sign_2)
-        keep_by_vector(keep[1], 1)
-        d[0] = (over.tile([P, C], U32, name="d_codes_0", offset=8 * C, align_bytes=64)[:], d[0][1])
-        quantise(d[0], da[0], 0, C)
-        nc.gpsimd.tensor_scalar(keep[3], sign_3, 1.0, 0.0, op0=MIN, op1=MAX)
-        quantise(g[3], gi_3, 0, C)
+        nc.vector.tensor_scalar(mask[2], sign_2, 0.0, None, op0=MAX)
+        mask_from_a(1)
+        d_0 = (over.tile([P, C], U32, name="d_codes_0", offset=8 * C, align_bytes=64)[:], d_scales[0])
+        quantise(d_0, da[0], 0, C)
+        nc.gpsimd.tensor_scalar(mask[3], sign_3, 1.0, 0.0, op0=MIN, op1=MAX)
+        quantise(g[3], woven_3, 0, C)
         rounded_3 = [held.tile([P, 2 * H], BF16, name=f"rounded_3{h}", tag=f"late_{h}", align_bytes=64) for h in range(2)]
         turned_3 = [product2(3, g[3], blocks, rounded_3[blocks[0] // 2]) for blocks in ((0, 1), (2,), (3,))]
         for e, turned in ((1, turned_1), (2, turned_2)):
-            for h in range(2):
-                masked(da[e], turned[h], keep[e])
-        product1(0, d[0], 1)
-        d[1] = (held.tile([P, C], U32, name="d_codes_1", tag="late_2", align_bytes=64)[:], d[1][1])
-        quantise(d[1], da[1], 0, C)
-        product1(1, d[1], 3)
-        masked(da[3], turned_3[0], keep[3])
-        d.append((d_codes[:, 0:C], held.tile([P, C], U8, name="d_scales_2", tag="late_0", align_bytes=64)[:]))
-        quantise(d[2], da[2], 0, C)
-        product1(2, d[2], 2)
-        masked(da[3], turned_3[1], keep[3])
-        masked(da[3], turned_3[2], keep[3])
-        d_scales = held.tile([P, half + C], U8, name="d_scales_3", tag="late_1", align_bytes=64)
-        nc.gpsimd.memset(d_scales[:, 0:half].bitcast(I32), 0)
-        d.append((d_codes[:, C:], d_scales[:, half:]))
-        quantise(d[3], da[3][:, 0 : half * PACK], 0, half)
-        product1(3, (d_codes[:, half : half + C], d_scales[:, 0:C]), 0, half, half, 0)
-        quantise(d[3], da[3][:, half * PACK :], half, half)
-        product1(3, d[3], 1, half, half, half)
+            for product in turned:
+                masked(e, product)
+        product1(0, d_0, 1)
+        d_1 = (held.tile([P, C], U32, name="d_codes_1", tag="late_2", align_bytes=64)[:], d_scales[1])
+        quantise(d_1, da[1], 0, C)
+        product1(1, d_1, 3)
+        masked(3, turned_3[0])
+        d_2 = (d_codes_23[:, 0:C], held.tile([P, C], U8, name="d_scales_2", tag="late_0", align_bytes=64)[:])
+        quantise(d_2, da[2], 0, C)
+        product1(2, d_2, 2)
+        masked(3, turned_3[1])
+        masked(3, turned_3[2])
+        d_scales_3 = held.tile([P, HALF + C], U8, name="d_scales_3", tag="late_1", align_bytes=64)
+        nc.gpsimd.memset(d_scales_3[:, 0:HALF].bitcast(I32), 0)
+        d_3 = (d_codes_23[:, C:], d_scales_3[:, HALF:])
+        quantise(d_3, da[3][:, 0 : HALF * PACK], 0, HALF)
+        product1(3, (d_codes_23[:, HALF : HALF + C], d_scales_3[:, 0:C]), 0, HALF, HALF, 0)
+        quantise(d_3, da[3][:, HALF * PACK :], HALF, HALF)
+        product1(3, d_3, 1, HALF, HALF, HALF)
 
-        first = held.tile([P, T], F32, name="first")
+        by_pos1 = held.tile([P, T], F32, name="first")
         for h in range(2):
             nc.vector.tensor_copy(
-                first[:, h * T // 2 : (h + 1) * T // 2], dx_sb[:].indirect(pos1_sb[:, h * T // 32 : (h + 1) * T // 32])
+                by_pos1[:, h * T // 2 : (h + 1) * T // 2], dx_sb[:].indirect(pos1_sb[:, h * T // 32 : (h + 1) * T // 32])
             )
-        at = 0
+        token = 0
         for wide in (T // 2, 3 * T // 8, T // 8):
             total = work.tile([P, wide], F32, name="total")
             nc.vector.tensor_tensor(
-                total[:], dx_sb[:].indirect(pos2_sb[:, at // 16 : (at + wide) // 16]), first[:, at : at + wide], ADD
+                total[:],
+                dx_sb[:].indirect(pos2_sb[:, token // 16 : (token + wide) // 16]),
+                by_pos1[:, token : token + wide],
+                ADD,
             )
-            nc.sync.dma_start(out=out[:, at : at + wide], in_=total[:])
-            at = at + wide
+            nc.sync.dma_start(out=out[:, token : token + wide], in_=total[:])
+            token = token + wide

@@ -8,8 +8,8 @@ T, E, C = 1024, 4, 512
 S = E * C
 P = 128
 PACK = 4
+RUN = 4
 HALF = C // 2
-AHEAD = HALF + 64
 
 FLOPS = 2 * S * (N * H + H * K)
 BYTES = 4 * N * T + 4 * H * S + E * (N * H + H * K) // 2 + E * (N * H + H * K) // 32 + 4 * S + 2 * P * (S + 2 * T) // 16 + 4 * K * T
@@ -24,10 +24,8 @@ E5M2X4 = mybir.dt.float8_e5m2_x4
 E2M1X4 = mybir.dt.float4_e2m1fn_x4
 MULT = mybir.AluOpType.mult
 ADD = mybir.AluOpType.add
-MAX = mybir.AluOpType.max
-MIN = mybir.AluOpType.min
 IS_GT = mybir.AluOpType.is_gt
-SIGN = mybir.ActivationFunctionType.Sign
+COPY = mybir.ActivationFunctionType.Copy
 
 
 def tile_moe_bdx_mlp_relu_kernel(
@@ -37,8 +35,8 @@ def tile_moe_bdx_mlp_relu_kernel(
     with ExitStack() as ctx:
         lists = ctx.enter_context(tc.tile_pool(name="lists", bufs=1))
         held = ctx.enter_context(tc.tile_pool(name="held", bufs=1))
-        over = ctx.enter_context(tc.tile_pool(name="over", bufs=1))
         work = ctx.enter_context(tc.tile_pool(name="work", bufs=E))
+        blocks_pool = ctx.enter_context(tc.tile_pool(name="blocks", bufs=2 * PACK))
         sum_psum = ctx.enter_context(tc.psum_pool(name="dh_psum", bufs=1))
         turn_psum = ctx.enter_context(tc.psum_pool(name="turn_psum", bufs=4))
 
@@ -46,51 +44,35 @@ def tile_moe_bdx_mlp_relu_kernel(
         pos1_sb = lists.tile([P, T // 16], U16, name="pos1_sb")
         pos2_sb = lists.tile([P, T // 16], U16, name="pos2_sb")
 
-        w2_sb = [held.tile([P, n * 2 * H], U8, name=f"w2_sb{j}", align_bytes=64) for j, n in enumerate((1, 1, 2))]
-        s2_sb = [held.tile([P, n * H], U8, name=f"s2_sb{j}", align_bytes=64) for j, n in enumerate((1, 3))]
-        w2_of = [w2_sb[0][:], w2_sb[1][:], w2_sb[2][:, 0 : 2 * H], w2_sb[2][:, 2 * H :]]
-        s2_of = [s2_sb[0][:]] + [s2_sb[1][:, j * H : (j + 1) * H] for j in range(3)]
+        w2_sb = held.tile([P, E * 2 * H], U8, name="w2_sb", align_bytes=64)
+        s2_sb = held.tile([P, E * H], U8, name="s2_sb", align_bytes=64)
         w1_sb = held.tile([P, E * 2 * K], U8, name="w1_sb", align_bytes=64)
         s1_sb = held.tile([P, E * K], U8, name="s1_sb", align_bytes=64)
         dy_sb = [held.tile([P, T], F32, name=f"dy_sb{t}") for t in range(PACK)]
-        a_sb = {e: held.tile([P, PACK, C], F32, name=f"a_sb{e}")[:] for e in (0, 1)}
-        a_sb[2] = over.tile([P, PACK, C], F32, name="a_sb2", offset=0, align_bytes=64)[:]
-        a_3 = [held.tile([P, 2, C], F32, name=f"a_3{u}") for u in range(2)]
-        early = held.tile([P, AHEAD], F32, name="early")
+        a_sb = [held.tile([P, PACK, C], F32, name=f"a_sb{e}")[:] for e in range(E)]
 
-        room = held.tile([P, 10 * C], F32, name="room", align_bytes=64)
-        planes_of = [room[:, at * C : (at + PACK) * C] for at in (4, 2, 5, 1)]
-        gate_sb = [held.tile([P, C], F32, name=f"gate_sb{e}")[:] for e in (0, 1, 3)]
-        gate_sb.insert(2, room[:, C : 2 * C])
-        woven_0 = room[:, 8 * C : 10 * C].bitcast(BF16)
-        woven_1 = held.tile([P, PACK * C], BF16, name="gi_1", align_bytes=64)[:]
-        woven_3 = held.tile([P, PACK * C], BF16, name="gi_3", align_bytes=64)[:]
-        mask_0 = held.tile([P, PACK * C], BF16, name="keep_0")
-        mask = [mask_0[:], room[:, 7 * C : 9 * C].bitcast(BF16), room[:, 5 * C : 7 * C].bitcast(BF16), woven_1]
+        room = held.tile([P, 11 * C], F32, name="room", align_bytes=64)
+        planes_of = [room[:, at * C : (at + PACK) * C] for at in (7, 2, 6, 0)]
+        gate_sb = [room[:, HALF : HALF + C]] + [held.tile([P, C], F32, name=f"gate_sb{e}")[:] for e in (1, 2, 3)]
         dx_sb = held.tile([P, S], F32, name="dx_sb")
         ident = held.tile([P, P], F32, name="ident")
 
         make_identity(nc, ident[:])
-        for scales in s2_sb:
-            nc.gpsimd.memset(scales[:].bitcast(I32), 0)
+        nc.gpsimd.memset(s2_sb[:].bitcast(I32), 0)
         nc.gpsimd.memset(s1_sb[:].bitcast(I32), 0)
 
-        w2_i32 = w2_words.bitcast(I32)
-        w1_i32 = w1_words.bitcast(I32)
-        s2_i32 = w2_scales.bitcast(I32)
-        s1_i32 = w1_scales.bitcast(I32)
         dy_planes = dyT.rearrange("(p t) c -> p t c", t=PACK)
         a_planes = a.rearrange("(p t) c -> p t c", t=PACK)
 
-        def load_words(dst, src, first, last):
-            rows = dst[:].bitcast(I32).rearrange("p (e w) -> p e w", e=last - first)
-            nc.sync.dma_start(out=rows, in_=src[first:last, 0].rearrange("e p w -> p e w"))
+        def load_words(dst, src):
+            rows = dst[:].bitcast(I32).rearrange("p (e w) -> p e w", e=E)
+            nc.sync.dma_start(out=rows, in_=src.bitcast(I32)[:, 0].rearrange("e p w -> p e w"))
 
-        def load_scales(dst, src, first, last, queue=nc.sync):
+        def load_scales(dst, src):
             for q in range(4):
-                rows = dst[32 * q : 32 * q + 4, :].bitcast(I32).rearrange("p (e w) -> p e w", e=last - first)
-                queue.dma_start(
-                    out=rows, in_=src[first:last, 0, 4 * q : 4 * q + 4, :].rearrange("e f w -> f e w")
+                rows = dst[32 * q : 32 * q + 4, :].bitcast(I32).rearrange("p (e w) -> p e w", e=E)
+                nc.sync.dma_start(
+                    out=rows, in_=src.bitcast(I32)[:, 0, 4 * q : 4 * q + 4, :].rearrange("e f w -> f e w")
                 )
 
         def load_dy(t):
@@ -105,42 +87,55 @@ def tile_moe_bdx_mlp_relu_kernel(
         load_dy(0)
         nc.sync.dma_start(offs_sb[:], offs)
         load_gate(0)
-        load_scales(s2_sb[0], s2_i32, 0, 1, nc.scalar)
         load_dy(1)
         load_dy(2)
         load_dy(3)
         load_gate(1)
-        for u in range(2):
-            nc.sync.dma_start(out=a_3[u][:], in_=a_planes[:, 2 * u : 2 * u + 2, 3 * C :])
-        load_words(w2_sb[0], w2_i32, 0, 1)
-        load_gate(2)
         load_a(0)
-        load_a(2)
-        load_words(w2_sb[1], w2_i32, 1, 2)
-        load_scales(s2_sb[1], s2_i32, 1, E)
-        load_gate(3)
+        load_gate(2)
         load_a(1)
-        load_words(w2_sb[2], w2_i32, 2, E)
-        load_words(w1_sb, w1_i32, 0, E)
-        load_scales(s1_sb, s1_i32, 0, E)
+        load_words(w2_sb, w2_words)
+        load_scales(s2_sb, w2_scales)
+        load_gate(3)
+        load_a(2)
+        load_a(3)
+        load_words(w1_sb, w1_words)
+        load_scales(s1_sb, w1_scales)
         nc.sync.dma_start(pos1_sb[:], pos1)
         nc.sync.dma_start(pos2_sb[:], pos2)
 
-        def gather(e, planes, first=0, wide=C):
+        def window(e, t, first, wide):
             at = (e * C + first) // 16
-            for t in planes:
-                nc.vector.tensor_tensor(
-                    planes_of[e][:, t * C + first : t * C + first + wide],
-                    dy_sb[t][:].indirect(offs_sb[:, at : at + wide // 16]),
-                    gate_sb[e][:, first : first + wide],
-                    MULT,
-                )
+            return dy_sb[t][:].indirect(offs_sb[:, at : at + wide // 16])
 
-        def interleave(woven, e, first=0, wide=C):
+        def plane(e, t, first, wide):
+            return planes_of[e][:, t * C + first : t * C + first + wide]
+
+        def gather_weighed(e, t, first=0, wide=C):
+            nc.vector.tensor_tensor(
+                plane(e, t, first, wide), window(e, t, first, wide), gate_sb[e][:, first : first + wide], MULT
+            )
+
+        def gather_plain(e, t, first=0, wide=C):
+            nc.scalar.activation(plane(e, t, first, wide), window(e, t, first, wide), COPY)
+
+        def woven_view(e, first, wide):
+            return woven[e][:, PACK * first : PACK * (first + wide)].rearrange("p (c i t) -> p c t i", i=RUN, t=PACK)
+
+        def planes_view(e, first, wide):
             planes = planes_of[e].rearrange("p (t c) -> p t c", t=PACK)[:, :, first : first + wide]
-            nc.scalar.copy(
-                woven[:, PACK * first : PACK * (first + wide)].rearrange("p (c i t) -> p c t i", i=4, t=PACK),
-                planes.rearrange("p t (c i) -> p c t i", i=4),
+            return planes.rearrange("p t (c i) -> p c t i", i=RUN)
+
+        def interleave(e, first, wide):
+            nc.vector.tensor_copy(woven_view(e, first, wide), planes_view(e, first, wide))
+
+        def weigh(e, first=0, wide=C):
+            gates = gate_sb[e][:, first : first + wide].rearrange("p (c i) -> p c i", i=RUN)
+            nc.vector.tensor_tensor(
+                woven_view(e, first, wide),
+                planes_view(e, first, wide),
+                gates.unsqueeze(2).to_broadcast([P, wide // RUN, PACK, RUN]),
+                MULT,
             )
 
         def in_pairs(flat):
@@ -149,33 +144,38 @@ def tile_moe_bdx_mlp_relu_kernel(
         def expert_tile(name):
             return work.tile([P, C * PACK], BF16, name=name, align_bytes=64)[:]
 
-        def quantise(dst, woven, first, wide):
-            nc.vector.quantize_mx(
-                out=dst[0][:, first : first + wide].bitcast(E5M2X4), scales=dst[1][:, first : first + wide], in_=woven
+        def codes(name):
+            return (
+                work.tile([P, C], U32, name=name + "_codes", align_bytes=64)[:],
+                work.tile([P, C], U8, name=name + "_scales", align_bytes=64)[:],
             )
 
-        def mask_from_a(e):
+        def quantise(dst, values, first=0, wide=C):
+            nc.vector.quantize_mx(
+                out=dst[0][:, first : first + wide].bitcast(E5M2X4),
+                scales=dst[1][:, first : first + wide],
+                in_=values[:, PACK * first : PACK * (first + wide)],
+            )
+
+        def make_mask(e):
             nc.vector.tensor_scalar(
                 in_pairs(mask[e]), a_sb[e].rearrange("p (u d) c -> p u c d", u=2), 0.0, None, op0=IS_GT
             )
 
-        def product2(e, g_e, blocks, space=None):
+        def product2(e, blocks):
             turned = turn_psum.tile([P, 2 * HALF], F32, name="turned")
             for n, b in enumerate(blocks):
                 dh = sum_psum.tile([P, H], F32, name="dh", tag=f"bank{b}")
                 nc.tensor.matmul_mx(
                     out=dh[:],
-                    lhsT=g_e[0][:, b * P : (b + 1) * P].bitcast(E5M2X4),
-                    lhsT_scale=g_e[1][:, b * P : (b + 1) * P],
-                    rhs=w2_of[e].bitcast(E2M1X4),
-                    rhs_scale=s2_of[e],
+                    lhsT=g[e][0][:, b * P : (b + 1) * P].bitcast(E5M2X4),
+                    lhsT_scale=g[e][1][:, b * P : (b + 1) * P],
+                    rhs=w2_sb[:, 2 * e * H : 2 * (e + 1) * H].bitcast(E2M1X4),
+                    rhs_scale=s2_sb[:, e * H : (e + 1) * H],
                     start=True,
                     stop=True,
                 )
-                if space is None:
-                    rounded = work.tile([P, H], BF16, name="rounded")[:]
-                else:
-                    rounded = space[:, (b % 2) * H : (b % 2 + 1) * H]
+                rounded = blocks_pool.tile([P, H], BF16, name="rounded")[:]
                 nc.scalar.copy(
                     rounded.rearrange("s (u p d) -> s u p d", u=2, d=2),
                     dh[:].rearrange("s (p u d) -> s u p d", u=2, d=2),
@@ -198,108 +198,88 @@ def tile_moe_bdx_mlp_relu_kernel(
                 MULT,
             )
 
-        def product1(e, d_e, bank, first=0, wide=C, to=0):
-            dx = sum_psum.tile([P, C], F32, name="dx", tag=f"bank{bank}")
+        def product1(e, bank, first=0, wide=C):
+            dx = sum_psum.tile([P, wide], F32, name="dx", tag=f"bank{bank}")
             nc.tensor.matmul_mx(
                 out=dx[:],
                 lhsT=w1_sb[:, 2 * e * K : 2 * (e + 1) * K].bitcast(E2M1X4),
                 lhsT_scale=s1_sb[:, e * K : (e + 1) * K],
-                rhs=d_e[0].bitcast(E5M2X4),
-                rhs_scale=d_e[1],
+                rhs=d[e][0][:, first : first + wide].bitcast(E5M2X4),
+                rhs_scale=d[e][1][:, first : first + wide],
                 start=True,
                 stop=True,
             )
-            nc.scalar.copy(dx_sb[:, e * C + to : e * C + to + wide], dx[:, first : first + wide])
+            nc.scalar.copy(dx_sb[:, e * C + first : e * C + first + wide], dx[:])
 
-        g = [
-            (
-                work.tile([P, C], U32, name="g_codes", align_bytes=64)[:],
-                work.tile([P, C], U8, name="g_scales", align_bytes=64)[:],
-            )
-            for e in range(E)
-        ]
-        d_codes_23 = held.tile([P, 2 * C], U32, name="d_codes_23", align_bytes=64)
-        d_scales = [work.tile([P, C], U8, name="d_scales", align_bytes=64)[:] for e in range(2)]
-        da = [woven_1, room[:, C : 3 * C].bitcast(BF16), expert_tile("da"), expert_tile("da")]
-        sign_3 = expert_tile("sign")
-        sign_2 = expert_tile("sign")
+        woven = [expert_tile("woven") for e in range(E)]
+        mask = [expert_tile("mask") for e in range(E)]
+        da = [expert_tile("da") for e in range(E)]
+        g = [codes("g") for e in range(E)]
+        d = [codes("d") for e in range(E)]
         both_halves = ((0, 1), (2, 3))
 
-        nc.vector.tensor_copy(early[:], dy_sb[0][:].indirect(offs_sb[:, 3 * C // 16 : (3 * C + AHEAD) // 16]))
-        gather(0, (0, 1, 2))
+        nc.vector.tensor_copy(plane(3, 0, 0, HALF), window(3, 0, 0, HALF))
+        gather_plain(1, 0)
+        gather_plain(2, 0)
+        for t in range(1, PACK):
+            gather_plain(1, t)
+        for t in range(PACK - 1):
+            gather_weighed(0, t)
         for h in range(2):
-            gather(0, (3,), h * HALF, HALF)
-            interleave(woven_0, 0, h * HALF, HALF)
-        gather(1, (0, 1))
-        quantise(g[0], woven_0, 0, C)
-        for u in range(2):
-            nc.scalar.activation(in_pairs(sign_3)[:, u], a_3[u][:].rearrange("p d c -> p c d"), SIGN)
-        turned_0 = [product2(0, g[0], blocks) for blocks in both_halves]
-        gather(1, (2, 3))
-        interleave(woven_1, 1)
-        gather(2, (1, 2, 3))
-        mask_from_a(0)
-        quantise(g[1], woven_1, 0, C)
-        nc.scalar.activation(in_pairs(sign_2), a_sb[2].rearrange("p (u d) c -> p u c d", u=2), SIGN)
-        rounded_1 = over.tile([P, 4 * H], BF16, name="rounded_1", offset=0, align_bytes=64)
-        woven_2 = over.tile([P, PACK * C], BF16, name="gi_2", offset=8 * C, align_bytes=64)
-        turned_1 = [product2(1, g[1], blocks, rounded_1[:, blocks[0] * H :]) for blocks in both_halves]
-        gather(2, (0,))
-        interleave(woven_2[:], 2)
-        nc.gpsimd.tensor_tensor(planes_of[3][:, 0:AHEAD], early[:], gate_sb[3][:, 0:AHEAD], MULT)
-        for product in turned_0:
-            masked(0, product)
-        gather(3, (1, 2))
-        gather(3, (3,), 0, HALF)
-        interleave(woven_3, 3, 0, HALF)
-        gather(3, (0,), AHEAD, C - AHEAD)
-        gather(3, (3,), HALF, HALF)
-        interleave(woven_3, 3, HALF, HALF)
-        quantise(g[2], woven_2[:], 0, C)
-        rounded_2 = held.tile([P, 2 * H], BF16, name="rounded_2", tag="late_2", align_bytes=64)
-        turned_2 = [product2(2, g[2], (0, 1)), product2(2, g[2], (2, 3), rounded_2)]
-        nc.vector.tensor_scalar(mask[2], sign_2, 0.0, None, op0=MAX)
-        mask_from_a(1)
-        d_0 = (over.tile([P, C], U32, name="d_codes_0", offset=8 * C, align_bytes=64)[:], d_scales[0])
-        quantise(d_0, da[0], 0, C)
-        nc.gpsimd.tensor_scalar(mask[3], sign_3, 1.0, 0.0, op0=MIN, op1=MAX)
-        quantise(g[3], woven_3, 0, C)
-        rounded_3 = [held.tile([P, 2 * H], BF16, name=f"rounded_3{h}", tag=f"late_{h}", align_bytes=64) for h in range(2)]
-        turned_3 = [product2(3, g[3], blocks, rounded_3[blocks[0] // 2]) for blocks in ((0, 1), (2,), (3,))]
-        for e, turned in ((1, turned_1), (2, turned_2)):
-            for product in turned:
-                masked(e, product)
-        product1(0, d_0, 1)
-        d_1 = (held.tile([P, C], U32, name="d_codes_1", tag="late_2", align_bytes=64)[:], d_scales[1])
-        quantise(d_1, da[1], 0, C)
-        product1(1, d_1, 3)
-        masked(3, turned_3[0])
-        d_2 = (d_codes_23[:, 0:C], held.tile([P, C], U8, name="d_scales_2", tag="late_0", align_bytes=64)[:])
-        quantise(d_2, da[2], 0, C)
-        product1(2, d_2, 2)
-        masked(3, turned_3[1])
-        masked(3, turned_3[2])
-        d_scales_3 = held.tile([P, HALF + C], U8, name="d_scales_3", tag="late_1", align_bytes=64)
-        nc.gpsimd.memset(d_scales_3[:, 0:HALF].bitcast(I32), 0)
-        d_3 = (d_codes_23[:, C:], d_scales_3[:, HALF:])
-        quantise(d_3, da[3][:, 0 : HALF * PACK], 0, HALF)
-        product1(3, (d_codes_23[:, HALF : HALF + C], d_scales_3[:, 0:C]), 0, HALF, HALF, 0)
-        quantise(d_3, da[3][:, HALF * PACK :], HALF, HALF)
-        product1(3, d_3, 1, HALF, HALF, HALF)
+            gather_weighed(0, PACK - 1, h * HALF, HALF)
+        for h in range(2):
+            interleave(0, h * HALF, HALF)
+        gather_plain(3, 0, HALF, HALF)
+        gather_plain(3, 1)
+        for t in range(1, PACK):
+            gather_plain(2, t)
+        weigh(1, 0, HALF)
+        quantise(g[0], woven[0])
+        weigh(1, HALF, HALF)
+        for t in range(2, PACK):
+            gather_plain(3, t)
+        make_mask(0)
+        quantise(g[1], woven[1])
+        make_mask(1)
+        weigh(2)
+        make_mask(2)
+        quantise(g[2], woven[2])
+        weigh(3)
+        make_mask(3)
+        quantise(g[3], woven[3])
 
-        by_pos1 = held.tile([P, T], F32, name="first")
+        turned = [[product2(e, blocks) for blocks in both_halves] for e in range(2)]
+        masked(0, turned[0][0])
+        masked(0, turned[0][1])
+        turned.append([product2(2, blocks) for blocks in both_halves])
+        masked(1, turned[1][0])
+        quantise(d[0], da[0])
+        masked(1, turned[1][1])
+        turned.append([product2(3, blocks) for blocks in both_halves])
+        product1(0, 0)
+        masked(2, turned[2][0])
+        quantise(d[1], da[1])
+        product1(1, 1)
+        masked(2, turned[2][1])
+        masked(3, turned[3][0])
+        quantise(d[2], da[2])
+        product1(2, 2)
+        masked(3, turned[3][1])
         for h in range(2):
-            nc.vector.tensor_copy(
-                by_pos1[:, h * T // 2 : (h + 1) * T // 2], dx_sb[:].indirect(pos1_sb[:, h * T // 32 : (h + 1) * T // 32])
-            )
-        token = 0
-        for wide in (T // 2, 3 * T // 8, T // 8):
-            total = work.tile([P, wide], F32, name="total")
-            nc.vector.tensor_tensor(
-                total[:],
-                dx_sb[:].indirect(pos2_sb[:, token // 16 : (token + wide) // 16]),
-                by_pos1[:, token : token + wide],
-                ADD,
-            )
-            nc.sync.dma_start(out=out[:, token : token + wide], in_=total[:])
-            token = token + wide
+            quantise(d[3], da[3], h * HALF, HALF)
+            product1(3, 3 * (1 - h), h * HALF, HALF)
+
+        by_pos1 = held.tile([P, T], F32, name="by_pos1")
+
+        def slots_by(pos, first, wide):
+            return dx_sb[:].indirect(pos[:, first // 16 : (first + wide) // 16])
+
+        nc.vector.tensor_copy(by_pos1[:, 0:P], slots_by(pos1_sb, 0, P))
+        pieces = [(P, P), (0, P), (2 * P, 2 * P), (4 * P, 2 * P), (6 * P, 2 * P)]
+        for first, wide in pieces:
+            if first > 0:
+                nc.scalar.activation(by_pos1[:, first : first + wide], slots_by(pos1_sb, first, wide), COPY)
+        for first, wide in pieces:
+            total = blocks_pool.tile([P, wide], F32, name="total")
+            nc.vector.tensor_tensor(total[:], slots_by(pos2_sb, first, wide), by_pos1[:, first : first + wide], ADD)
+            nc.sync.dma_start(out=out[:, first : first + wide], in_=total[:])

@@ -57,6 +57,9 @@ def tile_moe_bdx_mlp_relu_kernel(
         dx_sb = held.tile([P, S], F32, name="dx_sb")
         ident = held.tile([P, P], F32, name="ident")
 
+        warm = held.tile([P, 2], F32, name="warm")
+        nc.gpsimd.memset(warm[:, 0:1], 0.0)
+        nc.scalar.activation(warm[:, 1:2], warm[:, 0:1], COPY)
         make_identity(nc, ident[:])
         nc.gpsimd.memset(s2_sb[:].bitcast(I32), 0)
         nc.gpsimd.memset(s1_sb[:].bitcast(I32), 0)

@@ -1,7 +1,6 @@
 from contextlib import ExitStack
 
 import concourse.mybir as mybir
-from concourse.masks import make_identity
 
 N, H, K = 512, 512, 128
 T, E, C = 1024, 4, 512
@@ -10,6 +9,8 @@ P = 128
 PACK = 4
 RUN = 4
 HALF = C // 2
+
+SHARE = 3 * P
 
 FLOPS = 2 * S * (N * H + H * K)
 BYTES = 4 * N * T + 4 * H * S + E * (N * H + H * K) // 2 + E * (N * H + H * K) // 32 + 4 * S + 2 * P * (S + 2 * T) // 16 + 4 * K * T
@@ -35,41 +36,50 @@ def tile_moe_bdx_mlp_relu_kernel(
     with ExitStack() as ctx:
         lists = ctx.enter_context(tc.tile_pool(name="lists", bufs=1))
         held = ctx.enter_context(tc.tile_pool(name="held", bufs=1))
+        over = ctx.enter_context(tc.tile_pool(name="over", bufs=1))
         work = ctx.enter_context(tc.tile_pool(name="work", bufs=E))
-        blocks_pool = ctx.enter_context(tc.tile_pool(name="blocks", bufs=2 * PACK))
-        sum_psum = ctx.enter_context(tc.psum_pool(name="dh_psum", bufs=1))
-        turn_psum = ctx.enter_context(tc.psum_pool(name="turn_psum", bufs=4))
+        ends = ctx.enter_context(tc.tile_pool(name="ends", bufs=5))
+        dh_psum = ctx.enter_context(tc.psum_pool(name="dh_psum", bufs=4))
+        dx_psum = ctx.enter_context(tc.psum_pool(name="dx_psum", bufs=4))
 
         offs_sb = lists.tile([P, S // 16], U16, name="offs_sb")
         pos1_sb = lists.tile([P, T // 16], U16, name="pos1_sb")
         pos2_sb = lists.tile([P, T // 16], U16, name="pos2_sb")
 
-        w2_sb = held.tile([P, E * 2 * H], U8, name="w2_sb", align_bytes=64)
+        w2_sb = [held.tile([P, n * 2 * H], U8, name=f"w2_sb{j}", align_bytes=64) for j, n in enumerate((2, 2))]
+        w2_of = [w2_sb[e // 2][:, (e % 2) * 2 * H : (e % 2 + 1) * 2 * H] for e in range(E)]
         s2_sb = held.tile([P, E * H], U8, name="s2_sb", align_bytes=64)
+        w2_turned = [held.tile([P, 2 * H], U8, name=f"w2_turned{e}", align_bytes=64)[:] for e in range(1)]
+        s2_turned = [held.tile([P, 2 * H], U8, name=f"s2_turned{j}", align_bytes=64) for j in range(2)]
         w1_sb = held.tile([P, E * 2 * K], U8, name="w1_sb", align_bytes=64)
         s1_sb = held.tile([P, E * K], U8, name="s1_sb", align_bytes=64)
         dy_sb = [held.tile([P, T], F32, name=f"dy_sb{t}") for t in range(PACK)]
-        a_sb = [held.tile([P, PACK, C], F32, name=f"a_sb{e}")[:] for e in range(E)]
+        a_sb = [held.tile([P, PACK, C], F32, name=f"a_sb{e}", tag=f"a{e}", align_bytes=64)[:] for e in range(E - 1)]
+        a_3 = [held.tile([P, PACK, HALF], F32, name=f"a_3{h}")[:] for h in range(2)]
 
-        room = held.tile([P, 11 * C], F32, name="room", align_bytes=64)
-        planes_of = [room[:, at * C : (at + PACK) * C] for at in (7, 2, 6, 0)]
-        gate_sb = [room[:, HALF : HALF + C]] + [held.tile([P, C], F32, name=f"gate_sb{e}")[:] for e in (1, 2, 3)]
+        room = held.tile([P, 19 * HALF], F32, name="room", align_bytes=64)
+        planes_of = [room[:, at * HALF : at * HALF + PACK * C] for at in (11, 1, 9, 0)]
+        gate_sb = [held.tile([P, C], F32, name=f"gate_sb{e}")[:] for e in range(E)]
+
+        def saved_for(e, first, wide):
+            if e < E - 1:
+                return a_sb[e], slice(first, first + wide)
+            return a_3[first // HALF], slice(first % HALF, first % HALF + wide)
+
         dx_sb = held.tile([P, S], F32, name="dx_sb")
-        ident = held.tile([P, P], F32, name="ident")
 
         warm = held.tile([P, 2], F32, name="warm")
         nc.gpsimd.memset(warm[:, 0:1], 0.0)
         nc.scalar.activation(warm[:, 1:2], warm[:, 0:1], COPY)
-        make_identity(nc, ident[:])
         nc.gpsimd.memset(s2_sb[:].bitcast(I32), 0)
         nc.gpsimd.memset(s1_sb[:].bitcast(I32), 0)
 
         dy_planes = dyT.rearrange("(p t) c -> p t c", t=PACK)
         a_planes = a.rearrange("(p t) c -> p t c", t=PACK)
 
-        def load_words(dst, src):
-            rows = dst[:].bitcast(I32).rearrange("p (e w) -> p e w", e=E)
-            nc.sync.dma_start(out=rows, in_=src.bitcast(I32)[:, 0].rearrange("e p w -> p e w"))
+        def load_words(dst, src, first, last):
+            rows = dst[:].bitcast(I32).rearrange("p (e w) -> p e w", e=last - first)
+            nc.sync.dma_start(out=rows, in_=src.bitcast(I32)[first:last, 0].rearrange("e p w -> p e w"))
 
         def load_scales(dst, src):
             for q in range(4):
@@ -87,22 +97,27 @@ def tile_moe_bdx_mlp_relu_kernel(
         def load_a(e):
             nc.sync.dma_start(out=a_sb[e], in_=a_planes[:, :, e * C : (e + 1) * C])
 
+        def load_a_3(h):
+            nc.sync.dma_start(out=a_3[h], in_=a_planes[:, :, 3 * C + h * HALF : 3 * C + (h + 1) * HALF])
+
         load_dy(0)
         nc.sync.dma_start(offs_sb[:], offs)
         load_gate(0)
         load_dy(1)
         load_dy(2)
         load_dy(3)
+        load_words(w2_sb[0], w2_words, 0, 2)
         load_gate(1)
-        load_a(0)
-        load_gate(2)
-        load_a(1)
-        load_words(w2_sb, w2_words)
         load_scales(s2_sb, w2_scales)
+        load_a(0)
+        load_a(1)
+        load_gate(2)
+        load_words(w2_sb[1], w2_words, 2, E)
         load_gate(3)
         load_a(2)
-        load_a(3)
-        load_words(w1_sb, w1_words)
+        load_a_3(1)
+        load_a_3(0)
+        load_words(w1_sb, w1_words, 0, E)
         load_scales(s1_sb, w1_scales)
         nc.sync.dma_start(pos1_sb[:], pos1)
         nc.sync.dma_start(pos2_sb[:], pos2)
@@ -122,27 +137,33 @@ def tile_moe_bdx_mlp_relu_kernel(
         def gather_plain(e, t, first=0, wide=C):
             nc.scalar.activation(plane(e, t, first, wide), window(e, t, first, wide), COPY)
 
-        def woven_view(e, first, wide):
-            return woven[e][:, PACK * first : PACK * (first + wide)].rearrange("p (c i t) -> p c t i", i=RUN, t=PACK)
+        def woven_view(values):
+            return values.rearrange("p (c i t) -> p c t i", i=RUN, t=PACK)
 
         def planes_view(e, first, wide):
             planes = planes_of[e].rearrange("p (t c) -> p t c", t=PACK)[:, :, first : first + wide]
             return planes.rearrange("p t (c i) -> p c t i", i=RUN)
 
-        def interleave(e, first, wide):
-            nc.vector.tensor_copy(woven_view(e, first, wide), planes_view(e, first, wide))
-
-        def weigh(e, first=0, wide=C):
+        def weigh(engine, values, e, first=0, wide=C):
             gates = gate_sb[e][:, first : first + wide].rearrange("p (c i) -> p c i", i=RUN)
-            nc.vector.tensor_tensor(
-                woven_view(e, first, wide),
+            engine.tensor_tensor(
+                woven_view(values),
                 planes_view(e, first, wide),
                 gates.unsqueeze(2).to_broadcast([P, wide // RUN, PACK, RUN]),
                 MULT,
             )
 
-        def in_pairs(flat):
-            return flat.rearrange("p (u c d) -> p u c d", u=2, d=2)
+        def turn_words(e):
+            nc.scalar.copy(
+                w2_turned[e].bitcast(U16).rearrange("p (t m) -> p t m", t=PACK),
+                w2_of[e].bitcast(U16).rearrange("p (m t) -> p t m", t=PACK),
+            )
+
+        def turn_scales(j):
+            nc.vector.tensor_copy(
+                s2_turned[j][:].rearrange("p (e t m) -> p e t m", e=2, t=PACK),
+                s2_sb[:, 2 * j * H : 2 * (j + 1) * H].rearrange("p (e m t) -> p e t m", e=2, t=PACK),
+            )
 
         def expert_tile(name):
             return work.tile([P, C * PACK], BF16, name=name, align_bytes=64)[:]
@@ -155,122 +176,152 @@ def tile_moe_bdx_mlp_relu_kernel(
 
         def quantise(dst, values, first=0, wide=C):
             nc.vector.quantize_mx(
-                out=dst[0][:, first : first + wide].bitcast(E5M2X4),
-                scales=dst[1][:, first : first + wide],
-                in_=values[:, PACK * first : PACK * (first + wide)],
+                out=dst[0][:, first : first + wide].bitcast(E5M2X4), scales=dst[1][:, first : first + wide], in_=values
             )
 
-        def make_mask(e):
-            nc.vector.tensor_scalar(
-                in_pairs(mask[e]), a_sb[e].rearrange("p (u d) c -> p u c d", u=2), 0.0, None, op0=IS_GT
-            )
+        def masked_product(e, h):
+            cols = slice(h * HALF, (h + 1) * HALF)
+            saved, saved_cols = saved_for(e, h * HALF, HALF)
+            for u in range(2):
+                dh = dh_psum.tile([P, 2 * HALF], F32, name="dh")
+                for d in range(2):
+                    t = 2 * u + d
+                    nc.tensor.matmul_mx(
+                        out=dh[:, d * HALF : (d + 1) * HALF],
+                        lhsT=w2_turned[e][:, 2 * t * P : 2 * (t + 1) * P].bitcast(E2M1X4),
+                        lhsT_scale=s2_turned[e // 2][:, (e % 2) * H + t * P : (e % 2) * H + (t + 1) * P],
+                        rhs=g[e][0][:, cols].bitcast(E5M2X4),
+                        rhs_scale=g[e][1][:, cols],
+                        start=True,
+                        stop=True,
+                    )
+                nc.vector.scalar_tensor_tensor(
+                    pairs[e].rearrange("p (u c d) -> p u c d", u=2, d=2)[:, u, cols, :],
+                    saved[:, 2 * u : 2 * u + 2, saved_cols].rearrange("p d c -> p c d"),
+                    0.0,
+                    dh[:].rearrange("p (d c) -> p c d", d=2),
+                    op0=IS_GT,
+                    op1=MULT,
+                )
 
-        def product2(e, blocks):
-            turned = turn_psum.tile([P, 2 * HALF], F32, name="turned")
-            for n, b in enumerate(blocks):
-                dh = sum_psum.tile([P, H], F32, name="dh", tag=f"bank{b}")
+        def masked_block(e, b):
+            cols = slice(b * P, (b + 1) * P)
+            saved, saved_cols = saved_for(e, b * P, P)
+            dh = dh_psum.tile([P, PACK * P], F32, name="dh")
+            for t in range(PACK):
                 nc.tensor.matmul_mx(
-                    out=dh[:],
-                    lhsT=g[e][0][:, b * P : (b + 1) * P].bitcast(E5M2X4),
-                    lhsT_scale=g[e][1][:, b * P : (b + 1) * P],
-                    rhs=w2_sb[:, 2 * e * H : 2 * (e + 1) * H].bitcast(E2M1X4),
-                    rhs_scale=s2_sb[:, e * H : (e + 1) * H],
+                    out=dh[:, t * P : (t + 1) * P],
+                    lhsT=w2_turned[e][:, 2 * t * P : 2 * (t + 1) * P].bitcast(E2M1X4),
+                    lhsT_scale=s2_turned[e // 2][:, (e % 2) * H + t * P : (e % 2) * H + (t + 1) * P],
+                    rhs=g[e][0][:, cols].bitcast(E5M2X4),
+                    rhs_scale=g[e][1][:, cols],
                     start=True,
                     stop=True,
                 )
-                rounded = blocks_pool.tile([P, H], BF16, name="rounded")[:]
-                nc.scalar.copy(
-                    rounded.rearrange("s (u p d) -> s u p d", u=2, d=2),
-                    dh[:].rearrange("s (p u d) -> s u p d", u=2, d=2),
-                )
-                pairs = rounded.bitcast(F32)
-                for u in range(2):
-                    nc.tensor.transpose(
-                        turned[:].rearrange("p (c u) -> p c u", u=2)[:, n * P : (n + 1) * P, u],
-                        pairs[:, u * P : (u + 1) * P],
-                        ident[:],
-                    )
-            return turned[:, 0 : 2 * P * len(blocks)], blocks[0] * P, len(blocks) * P
-
-        def masked(e, product):
-            turned, first, wide = product
-            nc.vector.tensor_tensor(
-                da[e][:, first * PACK : (first + wide) * PACK].rearrange("p (c u d) -> p c u d", u=2, d=2),
-                turned.bitcast(BF16).rearrange("p (c u d) -> p c u d", u=2, d=2),
-                in_pairs(mask[e])[:, :, first : first + wide, :].rearrange("p u c d -> p c u d"),
-                MULT,
+            nc.vector.scalar_tensor_tensor(
+                da[e].rearrange("p (c t) -> p c t", t=PACK)[:, cols, :],
+                saved[:, :, saved_cols].rearrange("p t c -> p c t"),
+                0.0,
+                dh[:].rearrange("p (t c) -> p c t", t=PACK),
+                op0=IS_GT,
+                op1=MULT,
             )
 
-        def product1(e, bank, first=0, wide=C):
-            dx = sum_psum.tile([P, wide], F32, name="dx", tag=f"bank{bank}")
+        def weave_pairs(e, h):
+            cols = slice(h * HALF, (h + 1) * HALF)
+            nc.scalar.copy(
+                da[e].bitcast(U32).rearrange("p (c u) -> p c u", u=2)[:, cols, :],
+                pairs[e].bitcast(U32).rearrange("p (u c) -> p c u", u=2)[:, cols, :],
+            )
+
+        def product1(e, first=0, wide=C):
+            dx = dx_psum.tile([P, wide], F32, name="dx")
             nc.tensor.matmul_mx(
                 out=dx[:],
                 lhsT=w1_sb[:, 2 * e * K : 2 * (e + 1) * K].bitcast(E2M1X4),
                 lhsT_scale=s1_sb[:, e * K : (e + 1) * K],
-                rhs=d[e][0][:, first : first + wide].bitcast(E5M2X4),
-                rhs_scale=d[e][1][:, first : first + wide],
+                rhs=d_of[e][0][:, first : first + wide].bitcast(E5M2X4),
+                rhs_scale=d_of[e][1][:, first : first + wide],
                 start=True,
                 stop=True,
             )
             nc.scalar.copy(dx_sb[:, e * C + first : e * C + first + wide], dx[:])
 
-        woven = [expert_tile("woven") for e in range(E)]
-        mask = [expert_tile("mask") for e in range(E)]
+        woven_0 = held.tile([P, PACK * C], BF16, name="woven_0", tag="woven_0", align_bytes=64)[:]
+        woven_1 = over.tile([P, PACK * C], BF16, name="woven_1", offset=0, align_bytes=64)[:]
+        pairs = [expert_tile("pairs") for e in range(E)]
+        pairs[2] = held.tile([P, PACK * C], BF16, name="pairs_2", tag="pairs_2", align_bytes=64)[:]
         da = [expert_tile("da") for e in range(E)]
         g = [codes("g") for e in range(E)]
-        d = [codes("d") for e in range(E)]
-        both_halves = ((0, 1), (2, 3))
+        d_of = [codes("d") for e in range(E)]
 
         nc.vector.tensor_copy(plane(3, 0, 0, HALF), window(3, 0, 0, HALF))
         gather_plain(1, 0)
         gather_plain(2, 0)
         for t in range(1, PACK):
             gather_plain(1, t)
+        turn_words(0)
         for t in range(PACK - 1):
             gather_weighed(0, t)
         for h in range(2):
             gather_weighed(0, PACK - 1, h * HALF, HALF)
         for h in range(2):
-            interleave(0, h * HALF, HALF)
-        gather_plain(3, 0, HALF, HALF)
-        gather_plain(3, 1)
+            nc.vector.tensor_copy(
+                woven_view(woven_0[:, h * PACK * HALF : (h + 1) * PACK * HALF]), planes_view(0, h * HALF, HALF)
+            )
         for t in range(1, PACK):
             gather_plain(2, t)
-        weigh(1, 0, HALF)
-        quantise(g[0], woven[0])
-        weigh(1, HALF, HALF)
-        for t in range(2, PACK):
+        turn_scales(0)
+        weigh(nc.vector, woven_1[:, 0 : PACK * HALF], 1, 0, HALF)
+        quantise(g[0], woven_0)
+        w2_turned.append(held.tile([P, 2 * H], U8, name="w2_turned1", tag="woven_0", align_bytes=64)[:])
+        turn_words(1)
+        gather_plain(3, 0, HALF, HALF)
+        weigh(nc.vector, woven_1[:, PACK * HALF :], 1, HALF, HALF)
+        for t in range(1, PACK):
             gather_plain(3, t)
-        make_mask(0)
-        quantise(g[1], woven[1])
-        make_mask(1)
-        weigh(2)
-        make_mask(2)
-        quantise(g[2], woven[2])
-        weigh(3)
-        make_mask(3)
-        quantise(g[3], woven[3])
-
-        turned = [[product2(e, blocks) for blocks in both_halves] for e in range(2)]
-        masked(0, turned[0][0])
-        masked(0, turned[0][1])
-        turned.append([product2(2, blocks) for blocks in both_halves])
-        masked(1, turned[1][0])
-        quantise(d[0], da[0])
-        masked(1, turned[1][1])
-        turned.append([product2(3, blocks) for blocks in both_halves])
-        product1(0, 0)
-        masked(2, turned[2][0])
-        quantise(d[1], da[1])
-        product1(1, 1)
-        masked(2, turned[2][1])
-        masked(3, turned[3][0])
-        quantise(d[2], da[2])
-        product1(2, 2)
-        masked(3, turned[3][1])
+        turn_scales(1)
+        quantise(g[1], woven_1)
+        woven_2 = over.tile([P, PACK * C], BF16, name="woven_2", offset=0, align_bytes=64)[:]
+        weigh(nc.gpsimd, woven_2[:, 0 : PACK * SHARE], 2, 0, SHARE)
+        for e in range(2):
+            for h in range(2):
+                masked_product(e, h)
         for h in range(2):
-            quantise(d[3], da[3], h * HALF, HALF)
-            product1(3, 3 * (1 - h), h * HALF, HALF)
+            weave_pairs(0, h)
+        late_words = held.tile([P, 4 * H], U8, name="late_words", tag="a0", align_bytes=64)
+        w2_turned.extend([late_words[:, 0 : 2 * H], late_words[:, 2 * H :]])
+        for h in range(2):
+            weave_pairs(1, h)
+        turn_words(2)
+        turn_words(3)
+        weigh(nc.vector, woven_2[:, PACK * SHARE :], 2, SHARE, C - SHARE)
+        quantise(d_of[0], da[0])
+        quantise(g[2], woven_2)
+        product1(0)
+        woven_3 = over.tile([P, PACK * HALF], BF16, name="woven_3", offset=0, align_bytes=64)[:]
+        weigh(nc.vector, woven_3, 3, HALF, HALF)
+        d_of[1] = (over.tile([P, C], U32, name="d_codes_1", offset=2 * PACK * HALF, align_bytes=64)[:], d_of[1][1])
+        quantise(d_of[1], da[1])
+        quantise(g[3], woven_3, HALF, HALF)
+        product1(1)
+        weigh(nc.gpsimd, woven_3, 3, 0, HALF)
+        for h in range(2):
+            masked_product(2, h)
+            weave_pairs(2, h)
+        masked_product(3, 1)
+        weave_pairs(3, 1)
+        g[3] = (held.tile([P, HALF], U32, name="g_codes_3", tag="pairs_2", align_bytes=64)[:], g[3][1])
+        quantise(g[3], woven_3, 0, HALF)
+        quantise(d_of[2], da[2])
+        masked_block(3, 0)
+        quantise(d_of[3], da[3][:, PACK * HALF :], HALF, HALF)
+        masked_block(3, 1)
+        product1(2)
+        product1(3, HALF, HALF)
+        for b in range(2):
+            quantise(d_of[3], da[3][:, b * PACK * P : (b + 1) * PACK * P], b * P, P)
+            product1(3, b * P, P)
 
         by_pos1 = held.tile([P, T], F32, name="by_pos1")
 
@@ -283,6 +334,6 @@ def tile_moe_bdx_mlp_relu_kernel(
             if first > 0:
                 nc.scalar.activation(by_pos1[:, first : first + wide], slots_by(pos1_sb, first, wide), COPY)
         for first, wide in pieces:
-            total = blocks_pool.tile([P, wide], F32, name="total")
+            total = ends.tile([P, wide], F32, name="total")
             nc.vector.tensor_tensor(total[:], slots_by(pos2_sb, first, wide), by_pos1[:, first : first + wide], ADD)
             nc.sync.dma_start(out=out[:, first : first + wide], in_=total[:])

@@ -1,6 +1,7 @@
 from contextlib import ExitStack
 
 import concourse.mybir as mybir
+from concourse.masks import make_identity
 
 N, H, K = 512, 512, 128
 T, E, C = 1024, 4, 512
@@ -10,7 +11,16 @@ PACK = 4
 RUN = 4
 HALF = C // 2
 
-SHARE = 3 * P
+SHARE = 416
+
+AT_WOVEN = 0
+AT_A0 = AT_WOVEN + 2 * PACK * C
+AT_A1 = AT_A0 + 4 * PACK * C
+AT_A31 = AT_A1 + 4 * PACK * C
+AT_G1_SCALES = AT_A31 + 4 * PACK * HALF
+AT_A30 = AT_G1_SCALES + C
+AT_S2 = AT_G1_SCALES - C // 2
+AT_PAIRS_2 = AT_A30 + 4 * PACK * HALF
 
 FLOPS = 2 * S * (N * H + H * K)
 BYTES = 4 * N * T + 4 * H * S + E * (N * H + H * K) // 2 + E * (N * H + H * K) // 32 + 4 * S + 2 * P * (S + 2 * T) // 16 + 4 * K * T
@@ -48,23 +58,32 @@ def tile_moe_bdx_mlp_relu_kernel(
 
         w2_sb = [held.tile([P, n * 2 * H], U8, name=f"w2_sb{j}", align_bytes=64) for j, n in enumerate((2, 2))]
         w2_of = [w2_sb[e // 2][:, (e % 2) * 2 * H : (e % 2 + 1) * 2 * H] for e in range(E)]
-        s2_sb = held.tile([P, E * H], U8, name="s2_sb", align_bytes=64)
+        s2_sb = over.tile([P, 2 * H], U8, name="s2_sb", offset=AT_S2, align_bytes=64)
         w2_turned = [held.tile([P, 2 * H], U8, name=f"w2_turned{e}", align_bytes=64)[:] for e in range(1)]
         s2_turned = [held.tile([P, 2 * H], U8, name=f"s2_turned{j}", align_bytes=64) for j in range(2)]
         w1_sb = held.tile([P, E * 2 * K], U8, name="w1_sb", align_bytes=64)
         s1_sb = held.tile([P, E * K], U8, name="s1_sb", align_bytes=64)
         dy_sb = [held.tile([P, T], F32, name=f"dy_sb{t}") for t in range(PACK)]
-        a_sb = [held.tile([P, PACK, C], F32, name=f"a_sb{e}", tag=f"a{e}", align_bytes=64)[:] for e in range(E - 1)]
-        a_3 = [held.tile([P, PACK, HALF], F32, name=f"a_3{h}")[:] for h in range(2)]
+        a_sb = [over.tile([P, PACK, C], F32, name=f"a_sb{e}", offset=at, align_bytes=64)[:] for e, at in enumerate((AT_A0, AT_A1))]
+        a_sb.append(held.tile([P, PACK, C], F32, name="a_sb2")[:])
 
-        room = held.tile([P, 19 * HALF], F32, name="room", align_bytes=64)
-        planes_of = [room[:, at * HALF : at * HALF + PACK * C] for at in (11, 1, 9, 0)]
-        gate_sb = [held.tile([P, C], F32, name=f"gate_sb{e}")[:] for e in range(E)]
+        room = held.tile([P, 2 * PACK * C], F32, name="room", align_bytes=64)
+        room_0 = held.tile([P, PACK * C], F32, name="room_0", align_bytes=64)
+        planes_of = [
+            flat.rearrange("p (t c) -> p t c", t=PACK) for flat in (room_0[:], room[:, 0 : PACK * C], room[:, PACK * C :])
+        ]
+        planes_3 = {1: room[:, 0 : PACK * HALF].rearrange("p (t c) -> p t c", t=PACK)}
+        a_3 = {}
+        gate_sb = {e: held.tile([P, C], F32, name=f"gate_sb{e}", tag=f"gate{e}", align_bytes=64)[:] for e in (2, 3)}
+        gate_sb[0] = room[:, (PACK + 1) * C + HALF : (PACK + 2) * C + HALF]
+        gate_1 = held.tile([P, P], F32, name="gate_1")
+        gate_columns = held.tile([P, RUN], F32, name="gate_columns")
+        ident = held.tile([P, P], F32, name="ident")
 
-        def saved_for(e, first, wide):
+        def part(whole, halves, e, first, wide):
             if e < E - 1:
-                return a_sb[e], slice(first, first + wide)
-            return a_3[first // HALF], slice(first % HALF, first % HALF + wide)
+                return whole[e][:, :, first : first + wide]
+            return halves[first // HALF][:, :, first % HALF : first % HALF + wide]
 
         dx_sb = held.tile([P, S], F32, name="dx_sb")
 
@@ -72,6 +91,9 @@ def tile_moe_bdx_mlp_relu_kernel(
         nc.gpsimd.memset(warm[:, 0:1], 0.0)
         nc.scalar.activation(warm[:, 1:2], warm[:, 0:1], COPY)
         nc.gpsimd.memset(s2_sb[:].bitcast(I32), 0)
+        nc.gpsimd.dma_start(out=gate_columns[:], in_=gate[0, C : 2 * C].rearrange("(c i) -> c i", i=RUN))
+        make_identity(nc, ident[:])
+        nc.gpsimd.memset(s2_turned[1][:].bitcast(I32), 0)
         nc.gpsimd.memset(s1_sb[:].bitcast(I32), 0)
 
         dy_planes = dyT.rearrange("(p t) c -> p t c", t=PACK)
@@ -81,11 +103,11 @@ def tile_moe_bdx_mlp_relu_kernel(
             rows = dst[:].bitcast(I32).rearrange("p (e w) -> p e w", e=last - first)
             nc.sync.dma_start(out=rows, in_=src.bitcast(I32)[first:last, 0].rearrange("e p w -> p e w"))
 
-        def load_scales(dst, src):
+        def load_scales(dst, src, first, last, row=0):
             for q in range(4):
-                rows = dst[32 * q : 32 * q + 4, :].bitcast(I32).rearrange("p (e w) -> p e w", e=E)
+                rows = dst[32 * q + row : 32 * q + row + 4, :].bitcast(I32).rearrange("p (e w) -> p e w", e=last - first)
                 nc.sync.dma_start(
-                    out=rows, in_=src.bitcast(I32)[:, 0, 4 * q : 4 * q + 4, :].rearrange("e f w -> f e w")
+                    out=rows, in_=src.bitcast(I32)[first:last, 0, 4 * q : 4 * q + 4, :].rearrange("e f w -> f e w")
                 )
 
         def load_dy(t):
@@ -97,7 +119,8 @@ def tile_moe_bdx_mlp_relu_kernel(
         def load_a(e):
             nc.sync.dma_start(out=a_sb[e], in_=a_planes[:, :, e * C : (e + 1) * C])
 
-        def load_a_3(h):
+        def load_a_3(h, at):
+            a_3[h] = over.tile([P, PACK, HALF], F32, name=f"a_3{h}", offset=at, align_bytes=64)[:]
             nc.sync.dma_start(out=a_3[h], in_=a_planes[:, :, 3 * C + h * HALF : 3 * C + (h + 1) * HALF])
 
         load_dy(0)
@@ -107,27 +130,22 @@ def tile_moe_bdx_mlp_relu_kernel(
         load_dy(2)
         load_dy(3)
         load_words(w2_sb[0], w2_words, 0, 2)
-        load_gate(1)
-        load_scales(s2_sb, w2_scales)
+        nc.sync.dma_start(out=gate_1[:], in_=gate[0:P, 2 * C - P : 2 * C])
+        load_scales(s2_sb, w2_scales, 0, 2)
         load_a(0)
+        load_scales(s2_sb, w2_scales, 2, E, 4)
         load_a(1)
         load_gate(2)
         load_words(w2_sb[1], w2_words, 2, E)
         load_gate(3)
         load_a(2)
-        load_a_3(1)
-        load_a_3(0)
-        load_words(w1_sb, w1_words, 0, E)
-        load_scales(s1_sb, w1_scales)
-        nc.sync.dma_start(pos1_sb[:], pos1)
-        nc.sync.dma_start(pos2_sb[:], pos2)
 
         def window(e, t, first, wide):
             at = (e * C + first) // 16
             return dy_sb[t][:].indirect(offs_sb[:, at : at + wide // 16])
 
         def plane(e, t, first, wide):
-            return planes_of[e][:, t * C + first : t * C + first + wide]
+            return part(planes_of, planes_3, e, first, wide)[:, t, :]
 
         def gather_weighed(e, t, first=0, wide=C):
             nc.vector.tensor_tensor(
@@ -141,11 +159,14 @@ def tile_moe_bdx_mlp_relu_kernel(
             return values.rearrange("p (c i t) -> p c t i", i=RUN, t=PACK)
 
         def planes_view(e, first, wide):
-            planes = planes_of[e].rearrange("p (t c) -> p t c", t=PACK)[:, :, first : first + wide]
-            return planes.rearrange("p t (c i) -> p c t i", i=RUN)
+            return part(planes_of, planes_3, e, first, wide).rearrange("p t (c i) -> p c t i", i=RUN)
 
-        def weigh(engine, values, e, first=0, wide=C):
-            gates = gate_sb[e][:, first : first + wide].rearrange("p (c i) -> p c i", i=RUN)
+        def in_runs(gates):
+            return gates.rearrange("p (c i) -> p c i", i=RUN)
+
+        def weigh(engine, values, e, first, wide, gates=None):
+            if gates is None:
+                gates = in_runs(gate_sb[e][:, first : first + wide])
             engine.tensor_tensor(
                 woven_view(values),
                 planes_view(e, first, wide),
@@ -159,11 +180,16 @@ def tile_moe_bdx_mlp_relu_kernel(
                 w2_of[e].bitcast(U16).rearrange("p (m t) -> p t m", t=PACK),
             )
 
-        def turn_scales(j):
+        def turn_scales():
             nc.vector.tensor_copy(
-                s2_turned[j][:].rearrange("p (e t m) -> p e t m", e=2, t=PACK),
-                s2_sb[:, 2 * j * H : 2 * (j + 1) * H].rearrange("p (e m t) -> p e t m", e=2, t=PACK),
+                s2_turned[0][:].rearrange("p (e t m) -> p e t m", e=2, t=PACK),
+                s2_sb[:].rearrange("p (e m t) -> p e t m", e=2, t=PACK),
             )
+            for q in range(4):
+                nc.sync.dma_start(
+                    out=s2_turned[1][32 * q : 32 * q + 4, :].bitcast(I32),
+                    in_=s2_turned[0][32 * q + 4 : 32 * q + 8, :].bitcast(I32),
+                )
 
         def expert_tile(name):
             return work.tile([P, C * PACK], BF16, name=name, align_bytes=64)[:]
@@ -181,7 +207,6 @@ def tile_moe_bdx_mlp_relu_kernel(
 
         def masked_product(e, h):
             cols = slice(h * HALF, (h + 1) * HALF)
-            saved, saved_cols = saved_for(e, h * HALF, HALF)
             for u in range(2):
                 dh = dh_psum.tile([P, 2 * HALF], F32, name="dh")
                 for d in range(2):
@@ -197,7 +222,7 @@ def tile_moe_bdx_mlp_relu_kernel(
                     )
                 nc.vector.scalar_tensor_tensor(
                     pairs[e].rearrange("p (u c d) -> p u c d", u=2, d=2)[:, u, cols, :],
-                    saved[:, 2 * u : 2 * u + 2, saved_cols].rearrange("p d c -> p c d"),
+                    part(a_sb, a_3, e, h * HALF, HALF)[:, 2 * u : 2 * u + 2, :].rearrange("p d c -> p c d"),
                     0.0,
                     dh[:].rearrange("p (d c) -> p c d", d=2),
                     op0=IS_GT,
@@ -206,7 +231,6 @@ def tile_moe_bdx_mlp_relu_kernel(
 
         def masked_block(e, b):
             cols = slice(b * P, (b + 1) * P)
-            saved, saved_cols = saved_for(e, b * P, P)
             dh = dh_psum.tile([P, PACK * P], F32, name="dh")
             for t in range(PACK):
                 nc.tensor.matmul_mx(
@@ -220,7 +244,7 @@ def tile_moe_bdx_mlp_relu_kernel(
                 )
             nc.vector.scalar_tensor_tensor(
                 da[e].rearrange("p (c t) -> p c t", t=PACK)[:, cols, :],
-                saved[:, :, saved_cols].rearrange("p t c -> p c t"),
+                part(a_sb, a_3, e, b * P, P).rearrange("p t c -> p c t"),
                 0.0,
                 dh[:].rearrange("p (t c) -> p c t", t=PACK),
                 op0=IS_GT,
@@ -234,8 +258,8 @@ def tile_moe_bdx_mlp_relu_kernel(
                 pairs[e].bitcast(U32).rearrange("p (u c) -> p c u", u=2)[:, cols, :],
             )
 
-        def product1(e, first=0, wide=C):
-            dx = dx_psum.tile([P, wide], F32, name="dx")
+        def product1(e, first=0, wide=C, copy=nc.scalar.copy, banks=dx_psum, tag="dx"):
+            dx = banks.tile([P, wide], F32, name="dx", tag=tag)
             nc.tensor.matmul_mx(
                 out=dx[:],
                 lhsT=w1_sb[:, 2 * e * K : 2 * (e + 1) * K].bitcast(E2M1X4),
@@ -245,19 +269,25 @@ def tile_moe_bdx_mlp_relu_kernel(
                 start=True,
                 stop=True,
             )
-            nc.scalar.copy(dx_sb[:, e * C + first : e * C + first + wide], dx[:])
+            copy(dx_sb[:, e * C + first : e * C + first + wide], dx[:])
 
         woven_0 = held.tile([P, PACK * C], BF16, name="woven_0", tag="woven_0", align_bytes=64)[:]
-        woven_1 = over.tile([P, PACK * C], BF16, name="woven_1", offset=0, align_bytes=64)[:]
+        woven_1 = over.tile([P, PACK * (C - P)], BF16, name="woven_1", offset=AT_WOVEN, align_bytes=64)[:]
         pairs = [expert_tile("pairs") for e in range(E)]
-        pairs[2] = held.tile([P, PACK * C], BF16, name="pairs_2", tag="pairs_2", align_bytes=64)[:]
+        pairs[2] = over.tile([P, PACK * C], BF16, name="pairs_2", offset=AT_PAIRS_2, align_bytes=64)[:]
         da = [expert_tile("da") for e in range(E)]
         g = [codes("g") for e in range(E)]
         d_of = [codes("d") for e in range(E)]
 
-        nc.vector.tensor_copy(plane(3, 0, 0, HALF), window(3, 0, 0, HALF))
+        gate_bank = dx_psum.tile([P, C], F32, name="dx")
+        for i in range(RUN):
+            nc.tensor.transpose(
+                gate_bank[:, i * P : (i + 1) * P], gate_columns[:, i : i + 1].to_broadcast([P, P]), ident[:]
+            )
+
+        nc.vector.tensor_copy(plane(2, 0, 0, HALF), window(2, 0, 0, HALF))
         gather_plain(1, 0)
-        gather_plain(2, 0)
+        gather_plain(2, 0, HALF, HALF)
         for t in range(1, PACK):
             gather_plain(1, t)
         turn_words(0)
@@ -271,57 +301,72 @@ def tile_moe_bdx_mlp_relu_kernel(
             )
         for t in range(1, PACK):
             gather_plain(2, t)
-        turn_scales(0)
-        weigh(nc.vector, woven_1[:, 0 : PACK * HALF], 1, 0, HALF)
+        banked = gate_bank[:].rearrange("p (i c) -> p c i", i=RUN)[:, 0 : (C - P) // RUN, :]
+        weigh(nc.vector, woven_1, 1, 0, C - P, banked)
+        woven_1_last = room_0[:, PACK * C - HALF :].bitcast(BF16)
+        weigh(nc.gpsimd, woven_1_last, 1, C - P, P, in_runs(gate_1[:]))
         quantise(g[0], woven_0)
+        turn_scales()
+        load_a_3(1, AT_A31)
+        load_a_3(0, AT_A30)
+        load_words(w1_sb, w1_words, 0, E)
+        load_scales(s1_sb, w1_scales, 0, E)
+        nc.sync.dma_start(pos1_sb[:], pos1)
+        nc.sync.dma_start(pos2_sb[:], pos2)
+        g[1] = (g[1][0], over.tile([P, C], U8, name="g_scales_1", offset=AT_G1_SCALES, align_bytes=64)[:])
+        quantise(g[1], woven_1_last, C - P, P)
+        quantise(g[1], woven_1[:, 0 : PACK * HALF], 0, HALF)
+        quantise(g[1], woven_1[:, PACK * HALF :], HALF, P)
         w2_turned.append(held.tile([P, 2 * H], U8, name="w2_turned1", tag="woven_0", align_bytes=64)[:])
         turn_words(1)
-        gather_plain(3, 0, HALF, HALF)
-        weigh(nc.vector, woven_1[:, PACK * HALF :], 1, HALF, HALF)
-        for t in range(1, PACK):
-            gather_plain(3, t)
-        turn_scales(1)
-        quantise(g[1], woven_1)
-        woven_2 = over.tile([P, PACK * C], BF16, name="woven_2", offset=0, align_bytes=64)[:]
+        for t in range(PACK):
+            gather_plain(3, t, HALF, HALF)
+        woven_2 = over.tile([P, PACK * C], BF16, name="woven_2", offset=AT_WOVEN, align_bytes=64)[:]
         weigh(nc.gpsimd, woven_2[:, 0 : PACK * SHARE], 2, 0, SHARE)
         for e in range(2):
             for h in range(2):
                 masked_product(e, h)
+        late_words = over.tile([P, 4 * H], U8, name="late_words", offset=AT_A0, align_bytes=64)
+        w2_turned.extend([late_words[:, 0 : 2 * H], late_words[:, 2 * H :]])
+        planes_3[0] = over.tile([P, PACK, HALF], F32, name="planes_30", offset=AT_A0 + 4 * H, align_bytes=64)[:]
+        turn_words(2)
         for h in range(2):
             weave_pairs(0, h)
-        late_words = held.tile([P, 4 * H], U8, name="late_words", tag="a0", align_bytes=64)
-        w2_turned.extend([late_words[:, 0 : 2 * H], late_words[:, 2 * H :]])
+        for t in range(PACK):
+            gather_plain(3, t, 0, HALF)
+        turn_words(3)
         for h in range(2):
             weave_pairs(1, h)
-        turn_words(2)
-        turn_words(3)
         weigh(nc.vector, woven_2[:, PACK * SHARE :], 2, SHARE, C - SHARE)
-        quantise(d_of[0], da[0])
-        quantise(g[2], woven_2)
-        product1(0)
-        woven_3 = over.tile([P, PACK * HALF], BF16, name="woven_3", offset=0, align_bytes=64)[:]
+        quantise(g[2], woven_2[:, 0 : PACK * HALF], 0, HALF)
+        woven_3 = held.tile([P, PACK * HALF], BF16, name="woven_3", tag="gate2", align_bytes=64)[:]
         weigh(nc.vector, woven_3, 3, HALF, HALF)
-        d_of[1] = (over.tile([P, C], U32, name="d_codes_1", offset=2 * PACK * HALF, align_bytes=64)[:], d_of[1][1])
-        quantise(d_of[1], da[1])
+        quantise(g[2], woven_2[:, PACK * HALF :], HALF, HALF)
+        d_of[0] = (over.tile([P, C], U32, name="d_codes_0", offset=AT_A1, align_bytes=64)[:], d_of[0][1])
+        quantise(d_of[0], da[0])
         quantise(g[3], woven_3, HALF, HALF)
-        product1(1)
+        product1(0)
         weigh(nc.gpsimd, woven_3, 3, 0, HALF)
         for h in range(2):
             masked_product(2, h)
             weave_pairs(2, h)
         masked_product(3, 1)
         weave_pairs(3, 1)
-        g[3] = (held.tile([P, HALF], U32, name="g_codes_3", tag="pairs_2", align_bytes=64)[:], g[3][1])
+        g[3] = (over.tile([P, HALF], U32, name="g_codes_3", offset=AT_PAIRS_2, align_bytes=64)[:], g[3][1])
         quantise(g[3], woven_3, 0, HALF)
+        d_of[1] = (over.tile([P, C], U32, name="d_codes_1", offset=AT_PAIRS_2 + 4 * HALF, align_bytes=64)[:], d_of[1][1])
+        quantise(d_of[1], da[1])
         quantise(d_of[2], da[2])
         masked_block(3, 0)
         quantise(d_of[3], da[3][:, PACK * HALF :], HALF, HALF)
         masked_block(3, 1)
+        product1(1)
         product1(2)
-        product1(3, HALF, HALF)
         for b in range(2):
             quantise(d_of[3], da[3][:, b * PACK * P : (b + 1) * PACK * P], b * P, P)
-            product1(3, b * P, P)
+        product1(3, HALF, HALF, nc.vector.tensor_copy)
+        product1(3, 0, P, nc.vector.tensor_copy, dh_psum, "dh")
+        product1(3, P, P, nc.scalar.copy, dh_psum, "dh")
 
         by_pos1 = held.tile([P, T], F32, name="by_pos1")
 

from contextlib import ExitStack

import concourse.mybir as mybir
from concourse.masks import make_identity

N, H, K = 512, 512, 128
T, E, C = 1024, 4, 512
S = E * C
P = 128
PACK = 4
RUN = 4
HALF = C // 2

SHARE = 416

AT_WOVEN = 0
AT_A0 = AT_WOVEN + 2 * PACK * C
AT_A1 = AT_A0 + 4 * PACK * C
AT_A31 = AT_A1 + 4 * PACK * C
AT_G1_SCALES = AT_A31 + 4 * PACK * HALF
AT_A30 = AT_G1_SCALES + C
AT_S2 = AT_G1_SCALES - C // 2
AT_PAIRS_2 = AT_A30 + 4 * PACK * HALF

FLOPS = 2 * S * (N * H + H * K)
BYTES = 4 * N * T + 4 * H * S + E * (N * H + H * K) // 2 + E * (N * H + H * K) // 32 + 4 * S + 2 * P * (S + 2 * T) // 16 + 4 * K * T

F32 = mybir.dt.float32
BF16 = mybir.dt.bfloat16
I32 = mybir.dt.int32
U32 = mybir.dt.uint32
U16 = mybir.dt.uint16
U8 = mybir.dt.uint8
E5M2X4 = mybir.dt.float8_e5m2_x4
E2M1X4 = mybir.dt.float4_e2m1fn_x4
MULT = mybir.AluOpType.mult
ADD = mybir.AluOpType.add
IS_GT = mybir.AluOpType.is_gt
COPY = mybir.ActivationFunctionType.Copy


def tile_moe_bdx_mlp_relu_kernel(
    tc, dyT, a, w2_words, w2_scales, w1_words, w1_scales, gate, offs, pos1, pos2, out
):
    nc = tc.nc
    with ExitStack() as ctx:
        lists = ctx.enter_context(tc.tile_pool(name="lists", bufs=1))
        held = ctx.enter_context(tc.tile_pool(name="held", bufs=1))
        over = ctx.enter_context(tc.tile_pool(name="over", bufs=1))
        work = ctx.enter_context(tc.tile_pool(name="work", bufs=E))
        ends = ctx.enter_context(tc.tile_pool(name="ends", bufs=5))
        dh_psum = ctx.enter_context(tc.psum_pool(name="dh_psum", bufs=4))
        dx_psum = ctx.enter_context(tc.psum_pool(name="dx_psum", bufs=4))

        offs_sb = lists.tile([P, S // 16], U16, name="offs_sb")
        pos1_sb = lists.tile([P, T // 16], U16, name="pos1_sb")
        pos2_sb = lists.tile([P, T // 16], U16, name="pos2_sb")

        w2_sb = [held.tile([P, n * 2 * H], U8, name=f"w2_sb{j}", align_bytes=64) for j, n in enumerate((2, 2))]
        w2_of = [w2_sb[e // 2][:, (e % 2) * 2 * H : (e % 2 + 1) * 2 * H] for e in range(E)]
        s2_sb = over.tile([P, 2 * H], U8, name="s2_sb", offset=AT_S2, align_bytes=64)
        w2_turned = [held.tile([P, 2 * H], U8, name=f"w2_turned{e}", align_bytes=64)[:] for e in range(1)]
        s2_turned = [held.tile([P, 2 * H], U8, name=f"s2_turned{j}", align_bytes=64) for j in range(2)]
        w1_sb = held.tile([P, E * 2 * K], U8, name="w1_sb", align_bytes=64)
        s1_sb = held.tile([P, E * K], U8, name="s1_sb", align_bytes=64)
        dy_sb = [held.tile([P, T], F32, name=f"dy_sb{t}") for t in range(PACK)]
        a_sb = [over.tile([P, PACK, C], F32, name=f"a_sb{e}", offset=at, align_bytes=64)[:] for e, at in enumerate((AT_A0, AT_A1))]
        a_sb.append(held.tile([P, PACK, C], F32, name="a_sb2")[:])

        room = held.tile([P, 2 * PACK * C], F32, name="room", align_bytes=64)
        room_0 = held.tile([P, PACK * C], F32, name="room_0", align_bytes=64)
        planes_of = [
            flat.rearrange("p (t c) -> p t c", t=PACK) for flat in (room_0[:], room[:, 0 : PACK * C], room[:, PACK * C :])
        ]
        planes_3 = {1: room[:, 0 : PACK * HALF].rearrange("p (t c) -> p t c", t=PACK)}
        a_3 = {}
        gate_sb = {e: held.tile([P, C], F32, name=f"gate_sb{e}", tag=f"gate{e}", align_bytes=64)[:] for e in (2, 3)}
        gate_sb[0] = room[:, (PACK + 1) * C + HALF : (PACK + 2) * C + HALF]
        gate_1 = held.tile([P, P], F32, name="gate_1")
        gate_columns = held.tile([P, RUN], F32, name="gate_columns")
        ident = held.tile([P, P], F32, name="ident")

        def part(whole, halves, e, first, wide):
            if e < E - 1:
                return whole[e][:, :, first : first + wide]
            return halves[first // HALF][:, :, first % HALF : first % HALF + wide]

        dx_sb = held.tile([P, S], F32, name="dx_sb")

        warm = held.tile([P, 2], F32, name="warm")
        nc.gpsimd.memset(warm[:, 0:1], 0.0)
        nc.scalar.activation(warm[:, 1:2], warm[:, 0:1], COPY)
        nc.gpsimd.memset(s2_sb[:].bitcast(I32), 0)
        nc.gpsimd.dma_start(out=gate_columns[:], in_=gate[0, C : 2 * C].rearrange("(c i) -> c i", i=RUN))
        make_identity(nc, ident[:])
        nc.gpsimd.memset(s2_turned[1][:].bitcast(I32), 0)
        nc.gpsimd.memset(s1_sb[:].bitcast(I32), 0)

        dy_planes = dyT.rearrange("(p t) c -> p t c", t=PACK)
        a_planes = a.rearrange("(p t) c -> p t c", t=PACK)

        def load_words(dst, src, first, last):
            rows = dst[:].bitcast(I32).rearrange("p (e w) -> p e w", e=last - first)
            nc.sync.dma_start(out=rows, in_=src.bitcast(I32)[first:last, 0].rearrange("e p w -> p e w"))

        def load_scales(dst, src, first, last, row=0):
            for q in range(4):
                rows = dst[32 * q + row : 32 * q + row + 4, :].bitcast(I32).rearrange("p (e w) -> p e w", e=last - first)
                nc.sync.dma_start(
                    out=rows, in_=src.bitcast(I32)[first:last, 0, 4 * q : 4 * q + 4, :].rearrange("e f w -> f e w")
                )

        def load_dy(t):
            nc.sync.dma_start(out=dy_sb[t][:], in_=dy_planes[:, t, :])

        def load_gate(e):
            nc.sync.dma_start(out=gate_sb[e], in_=gate[0:P, e * C : (e + 1) * C])

        def load_a(e):
            nc.sync.dma_start(out=a_sb[e], in_=a_planes[:, :, e * C : (e + 1) * C])

        def load_a_3(h, at):
            a_3[h] = over.tile([P, PACK, HALF], F32, name=f"a_3{h}", offset=at, align_bytes=64)[:]
            nc.sync.dma_start(out=a_3[h], in_=a_planes[:, :, 3 * C + h * HALF : 3 * C + (h + 1) * HALF])

        load_dy(0)
        nc.sync.dma_start(offs_sb[:], offs)
        load_gate(0)
        load_dy(1)
        load_dy(2)
        load_dy(3)
        load_words(w2_sb[0], w2_words, 0, 2)
        nc.sync.dma_start(out=gate_1[:], in_=gate[0:P, 2 * C - P : 2 * C])
        load_scales(s2_sb, w2_scales, 0, 2)
        load_a(0)
        load_scales(s2_sb, w2_scales, 2, E, 4)
        load_a(1)
        load_gate(2)
        load_words(w2_sb[1], w2_words, 2, E)
        load_gate(3)
        load_a(2)

        def window(e, t, first, wide):
            at = (e * C + first) // 16
            return dy_sb[t][:].indirect(offs_sb[:, at : at + wide // 16])

        def plane(e, t, first, wide):
            return part(planes_of, planes_3, e, first, wide)[:, t, :]

        def gather_weighed(e, t, first=0, wide=C):
            nc.vector.tensor_tensor(
                plane(e, t, first, wide), window(e, t, first, wide), gate_sb[e][:, first : first + wide], MULT
            )

        def gather_plain(e, t, first=0, wide=C):
            nc.scalar.activation(plane(e, t, first, wide), window(e, t, first, wide), COPY)

        def woven_view(values):
            return values.rearrange("p (c i t) -> p c t i", i=RUN, t=PACK)

        def planes_view(e, first, wide):
            return part(planes_of, planes_3, e, first, wide).rearrange("p t (c i) -> p c t i", i=RUN)

        def in_runs(gates):
            return gates.rearrange("p (c i) -> p c i", i=RUN)

        def weigh(engine, values, e, first, wide, gates=None):
            if gates is None:
                gates = in_runs(gate_sb[e][:, first : first + wide])
            engine.tensor_tensor(
                woven_view(values),
                planes_view(e, first, wide),
                gates.unsqueeze(2).to_broadcast([P, wide // RUN, PACK, RUN]),
                MULT,
            )

        def turn_words(e):
            nc.scalar.copy(
                w2_turned[e].bitcast(U16).rearrange("p (t m) -> p t m", t=PACK),
                w2_of[e].bitcast(U16).rearrange("p (m t) -> p t m", t=PACK),
            )

        def turn_scales():
            nc.vector.tensor_copy(
                s2_turned[0][:].rearrange("p (e t m) -> p e t m", e=2, t=PACK),
                s2_sb[:].rearrange("p (e m t) -> p e t m", e=2, t=PACK),
            )
            for q in range(4):
                nc.sync.dma_start(
                    out=s2_turned[1][32 * q : 32 * q + 4, :].bitcast(I32),
                    in_=s2_turned[0][32 * q + 4 : 32 * q + 8, :].bitcast(I32),
                )

        def expert_tile(name):
            return work.tile([P, C * PACK], BF16, name=name, align_bytes=64)[:]

        def codes(name):
            return (
                work.tile([P, C], U32, name=name + "_codes", align_bytes=64)[:],
                work.tile([P, C], U8, name=name + "_scales", align_bytes=64)[:],
            )

        def quantise(dst, values, first=0, wide=C):
            nc.vector.quantize_mx(
                out=dst[0][:, first : first + wide].bitcast(E5M2X4), scales=dst[1][:, first : first + wide], in_=values
            )

        def masked_product(e, h):
            cols = slice(h * HALF, (h + 1) * HALF)
            for u in range(2):
                dh = dh_psum.tile([P, 2 * HALF], F32, name="dh")
                for d in range(2):
                    t = 2 * u + d
                    nc.tensor.matmul_mx(
                        out=dh[:, d * HALF : (d + 1) * HALF],
                        lhsT=w2_turned[e][:, 2 * t * P : 2 * (t + 1) * P].bitcast(E2M1X4),
                        lhsT_scale=s2_turned[e // 2][:, (e % 2) * H + t * P : (e % 2) * H + (t + 1) * P],
                        rhs=g[e][0][:, cols].bitcast(E5M2X4),
                        rhs_scale=g[e][1][:, cols],
                        start=True,
                        stop=True,
                    )
                nc.vector.scalar_tensor_tensor(
                    pairs[e].rearrange("p (u c d) -> p u c d", u=2, d=2)[:, u, cols, :],
                    part(a_sb, a_3, e, h * HALF, HALF)[:, 2 * u : 2 * u + 2, :].rearrange("p d c -> p c d"),
                    0.0,
                    dh[:].rearrange("p (d c) -> p c d", d=2),
                    op0=IS_GT,
                    op1=MULT,
                )

        def masked_block(e, b):
            cols = slice(b * P, (b + 1) * P)
            dh = dh_psum.tile([P, PACK * P], F32, name="dh")
            for t in range(PACK):
                nc.tensor.matmul_mx(
                    out=dh[:, t * P : (t + 1) * P],
                    lhsT=w2_turned[e][:, 2 * t * P : 2 * (t + 1) * P].bitcast(E2M1X4),
                    lhsT_scale=s2_turned[e // 2][:, (e % 2) * H + t * P : (e % 2) * H + (t + 1) * P],
                    rhs=g[e][0][:, cols].bitcast(E5M2X4),
                    rhs_scale=g[e][1][:, cols],
                    start=True,
                    stop=True,
                )
            nc.vector.scalar_tensor_tensor(
                da[e].rearrange("p (c t) -> p c t", t=PACK)[:, cols, :],
                part(a_sb, a_3, e, b * P, P).rearrange("p t c -> p c t"),
                0.0,
                dh[:].rearrange("p (t c) -> p c t", t=PACK),
                op0=IS_GT,
                op1=MULT,
            )

        def weave_pairs(e, h):
            cols = slice(h * HALF, (h + 1) * HALF)
            nc.scalar.copy(
                da[e].bitcast(U32).rearrange("p (c u) -> p c u", u=2)[:, cols, :],
                pairs[e].bitcast(U32).rearrange("p (u c) -> p c u", u=2)[:, cols, :],
            )

        def product1(e, first=0, wide=C, copy=nc.scalar.copy, banks=dx_psum, tag="dx"):
            dx = banks.tile([P, wide], F32, name="dx", tag=tag)
            nc.tensor.matmul_mx(
                out=dx[:],
                lhsT=w1_sb[:, 2 * e * K : 2 * (e + 1) * K].bitcast(E2M1X4),
                lhsT_scale=s1_sb[:, e * K : (e + 1) * K],
                rhs=d_of[e][0][:, first : first + wide].bitcast(E5M2X4),
                rhs_scale=d_of[e][1][:, first : first + wide],
                start=True,
                stop=True,
            )
            copy(dx_sb[:, e * C + first : e * C + first + wide], dx[:])

        woven_0 = held.tile([P, PACK * C], BF16, name="woven_0", tag="woven_0", align_bytes=64)[:]
        woven_1 = over.tile([P, PACK * (C - P)], BF16, name="woven_1", offset=AT_WOVEN, align_bytes=64)[:]
        pairs = [expert_tile("pairs") for e in range(E)]
        pairs[2] = over.tile([P, PACK * C], BF16, name="pairs_2", offset=AT_PAIRS_2, align_bytes=64)[:]
        da = [expert_tile("da") for e in range(E)]
        g = [codes("g") for e in range(E)]
        d_of = [codes("d") for e in range(E)]

        gate_bank = dx_psum.tile([P, C], F32, name="dx")
        for i in range(RUN):
            nc.tensor.transpose(
                gate_bank[:, i * P : (i + 1) * P], gate_columns[:, i : i + 1].to_broadcast([P, P]), ident[:]
            )

        nc.vector.tensor_copy(plane(2, 0, 0, HALF), window(2, 0, 0, HALF))
        gather_plain(1, 0)
        gather_plain(2, 0, HALF, HALF)
        for t in range(1, PACK):
            gather_plain(1, t)
        turn_words(0)
        for t in range(PACK - 1):
            gather_weighed(0, t)
        for h in range(2):
            gather_weighed(0, PACK - 1, h * HALF, HALF)
        for h in range(2):
            nc.vector.tensor_copy(
                woven_view(woven_0[:, h * PACK * HALF : (h + 1) * PACK * HALF]), planes_view(0, h * HALF, HALF)
            )
        for t in range(1, PACK):
            gather_plain(2, t)
        banked = gate_bank[:].rearrange("p (i c) -> p c i", i=RUN)[:, 0 : (C - P) // RUN, :]
        weigh(nc.vector, woven_1, 1, 0, C - P, banked)
        woven_1_last = room_0[:, PACK * C - HALF :].bitcast(BF16)
        weigh(nc.gpsimd, woven_1_last, 1, C - P, P, in_runs(gate_1[:]))
        quantise(g[0], woven_0)
        turn_scales()
        load_a_3(1, AT_A31)
        load_a_3(0, AT_A30)
        load_words(w1_sb, w1_words, 0, E)
        load_scales(s1_sb, w1_scales, 0, E)
        nc.sync.dma_start(pos1_sb[:], pos1)
        nc.sync.dma_start(pos2_sb[:], pos2)
        g[1] = (g[1][0], over.tile([P, C], U8, name="g_scales_1", offset=AT_G1_SCALES, align_bytes=64)[:])
        quantise(g[1], woven_1_last, C - P, P)
        quantise(g[1], woven_1[:, 0 : PACK * HALF], 0, HALF)
        quantise(g[1], woven_1[:, PACK * HALF :], HALF, P)
        w2_turned.append(held.tile([P, 2 * H], U8, name="w2_turned1", tag="woven_0", align_bytes=64)[:])
        turn_words(1)
        for t in range(PACK):
            gather_plain(3, t, HALF, HALF)
        woven_2 = over.tile([P, PACK * C], BF16, name="woven_2", offset=AT_WOVEN, align_bytes=64)[:]
        weigh(nc.gpsimd, woven_2[:, 0 : PACK * SHARE], 2, 0, SHARE)
        for e in range(2):
            for h in range(2):
                masked_product(e, h)
        late_words = over.tile([P, 4 * H], U8, name="late_words", offset=AT_A0, align_bytes=64)
        w2_turned.extend([late_words[:, 0 : 2 * H], late_words[:, 2 * H :]])
        planes_3[0] = over.tile([P, PACK, HALF], F32, name="planes_30", offset=AT_A0 + 4 * H, align_bytes=64)[:]
        turn_words(2)
        for h in range(2):
            weave_pairs(0, h)
        for t in range(PACK):
            gather_plain(3, t, 0, HALF)
        turn_words(3)
        for h in range(2):
            weave_pairs(1, h)
        weigh(nc.vector, woven_2[:, PACK * SHARE :], 2, SHARE, C - SHARE)
        quantise(g[2], woven_2[:, 0 : PACK * HALF], 0, HALF)
        woven_3 = held.tile([P, PACK * HALF], BF16, name="woven_3", tag="gate2", align_bytes=64)[:]
        weigh(nc.vector, woven_3, 3, HALF, HALF)
        quantise(g[2], woven_2[:, PACK * HALF :], HALF, HALF)
        d_of[0] = (over.tile([P, C], U32, name="d_codes_0", offset=AT_A1, align_bytes=64)[:], d_of[0][1])
        quantise(d_of[0], da[0])
        quantise(g[3], woven_3, HALF, HALF)
        product1(0)
        weigh(nc.gpsimd, woven_3, 3, 0, HALF)
        for h in range(2):
            masked_product(2, h)
            weave_pairs(2, h)
        masked_product(3, 1)
        weave_pairs(3, 1)
        g[3] = (over.tile([P, HALF], U32, name="g_codes_3", offset=AT_PAIRS_2, align_bytes=64)[:], g[3][1])
        quantise(g[3], woven_3, 0, HALF)
        d_of[1] = (over.tile([P, C], U32, name="d_codes_1", offset=AT_PAIRS_2 + 4 * HALF, align_bytes=64)[:], d_of[1][1])
        quantise(d_of[1], da[1])
        quantise(d_of[2], da[2])
        masked_block(3, 0)
        quantise(d_of[3], da[3][:, PACK * HALF :], HALF, HALF)
        masked_block(3, 1)
        product1(1)
        product1(2)
        for b in range(2):
            quantise(d_of[3], da[3][:, b * PACK * P : (b + 1) * PACK * P], b * P, P)
        product1(3, HALF, HALF, nc.vector.tensor_copy)
        product1(3, 0, P, nc.vector.tensor_copy, dh_psum, "dh")
        product1(3, P, P, nc.scalar.copy, dh_psum, "dh")

        by_pos1 = held.tile([P, T], F32, name="by_pos1")

        def slots_by(pos, first, wide):
            return dx_sb[:].indirect(pos[:, first // 16 : (first + wide) // 16])

        nc.vector.tensor_copy(by_pos1[:, 0:P], slots_by(pos1_sb, 0, P))
        pieces = [(P, P), (0, P), (2 * P, 2 * P), (4 * P, 2 * P), (6 * P, 2 * P)]
        for first, wide in pieces:
            if first > 0:
                nc.scalar.activation(by_pos1[:, first : first + wide], slots_by(pos1_sb, first, wide), COPY)
        for first, wide in pieces:
            total = ends.tile([P, wide], F32, name="total")
            nc.vector.tensor_tensor(total[:], slots_by(pos2_sb, first, wide), by_pos1[:, first : first + wide], ADD)
            nc.sync.dma_start(out=out[:, first : first + wide], in_=total[:])
